import numpy as np
import ml_dtypes


def mxq(x, axis, fmt="e4m3"):
    dtype, down = {"e4m3": (ml_dtypes.float8_e4m3fn, 7), "e5m2": (ml_dtypes.float8_e5m2, 14)}[fmt]
    v = np.moveaxis(np.asarray(x, np.float32).astype(ml_dtypes.bfloat16).astype(np.float64), axis, -1)
    blocks = v.reshape(v.shape[:-1] + (-1, 32))
    amax = np.abs(blocks).max(-1, keepdims=True)
    byte = np.maximum(np.where(amax > 0, np.frexp(amax)[1] - 1 + 127, 0) - down, 1)
    scale = np.exp2(byte - 127.0)
    codes = (blocks / scale).astype(np.float32).astype(dtype).astype(np.float64)
    return np.moveaxis((codes * scale).reshape(v.shape), -1, axis)


WIDE = False


def mx_kscale(k):
    if not WIDE:
        return np.ones(k)
    levels = np.array([10, -10, 5, -5, 0])
    if k % 512:
        return np.exp2(np.random.permutation(np.resize(levels, k // 32))).repeat(32)
    a = np.empty((k // 512, 16))
    for p in range(k // 512):
        a[p, :8] = np.random.permutation(np.resize(levels, 8))
        for g in range(8):
            far = levels[np.abs(levels - a[p, g]) >= 10]
            a[p, g + 8] = far[np.random.randint(len(far))]
    return np.exp2(a.ravel()).repeat(32)


def f64(x):
    return np.asarray(x).astype(np.float64)


def striped(idx):
    return np.tile(idx.reshape(-1, 16).T, (8, 1)).astype(np.uint16)


def unstriped(offs):
    return offs[:16].T.reshape(-1).astype(np.int64)


E2M1 = np.array([0.0, 0.5, 1.0, 1.5, 2.0, 3.0, 4.0, 6.0, -0.0, -0.5, -1.0, -1.5, -2.0, -3.0, -4.0, -6.0])


def pack_weight(w, fmt):
    k, n = w.shape
    w = f64(np.asarray(w, np.float32).astype(ml_dtypes.bfloat16)).reshape(k // 32, 32, n)
    amax = np.abs(w).max(1)
    if fmt == "e4m3":
        byte = np.frexp(amax)[1] - 1 + 127 - 7
    else:
        mant, ex = np.frexp(amax / 6.0)
        byte = np.where(mant > 0.5, ex, ex - 1) + 127
    byte = np.clip(np.where(amax > 0, byte, 1), 1, 254)
    scaled = (w * np.exp2(127.0 - byte)[:, None, :]).reshape(k, n).astype(np.float32)
    by_word = np.ascontiguousarray(scaled.reshape(k // 512, 128, 4, n).transpose(0, 1, 3, 2))
    if fmt == "e4m3":
        words = by_word.astype(ml_dtypes.float8_e4m3fn).view(np.uint8)
    else:
        c = by_word.astype(ml_dtypes.float4_e2m1fn).view(np.uint8) & 0xF
        words = (c[..., 0::2] | (c[..., 1::2] << 4)).reshape(k // 512, 128, 2 * n)
    return np.ascontiguousarray(words), np.ascontiguousarray(byte.astype(np.uint8).reshape(k // 512, 16, n))


def unpack_weight(words, scales, fmt):
    g, _, n = scales.shape
    words = np.ascontiguousarray(words).reshape(g, 128, n, -1)
    if fmt == "e4m3":
        vals = words.view(ml_dtypes.float8_e4m3fn).astype(np.float64)
    else:
        nib = np.empty((g, 128, n, 4), np.uint8)
        nib[..., 0::2] = words & 0xF
        nib[..., 1::2] = words >> 4
        vals = E2M1[nib]
    vals = vals * np.repeat(np.exp2(scales.astype(np.float64) - 127.0), 8, axis=1)[..., None]
    return vals.transpose(0, 1, 3, 2).reshape(g * 512, n)


def gelu(v):
    return 0.5 * v * (1.0 + np.tanh(np.sqrt(2.0 / np.pi) * (v + 0.044715 * v**3)))


K, R, H, N, T, S, T2 = 1024, 512, 1024, 512, 2048, 512, 1024

def setup_inputs():
    n = np.random.standard_normal
    s = mx_kscale(K)[:, None]
    e = mx_kscale(R)[:, None]
    u = mx_kscale(H)[:, None]
    tab_words, tab_scales = pack_weight(n((K, T)) * s, "e4m3")
    w1_words, w1_scales = pack_weight(n((K, H)) / np.sqrt(K) / s * u.T, "e2m1")
    w3_words, w3_scales = pack_weight(1.4 * n((R, H)) / np.sqrt(R) / e * u.T, "e4m3")
    return {
        "tab_words": tab_words, "tab_scales": tab_scales,
        "offs": striped(np.random.permutation(T)[:S]),
        "offs2": striped(np.random.permutation(T2)[:S]),
        "offs3": striped(np.random.permutation(T2)[:S]),
        "w1_words": w1_words, "w1_scales": w1_scales,
        "w2": (n((K, R)) / np.sqrt(K) / s * e.T).astype(np.float32),
        "b2": (0.3 * n(R) * e[:, 0]).astype(np.float32),
        "w3_words": w3_words, "w3_scales": w3_scales,
        "wg1": np.exp(0.3 * n((128, S))).astype(np.float32),
        "wg2": np.exp(0.3 * n((128, S))).astype(np.float32),
        "least": (0.5 * np.abs(n((H, T2))) * u).astype(np.float32),
        "w4": (n((H, N)) / np.sqrt(H) / u).astype(np.float32),
    }

def reference(tab_words, tab_scales, offs, offs2, offs3, w1_words, w1_scales, w2, b2,
              w3_words, w3_scales, wg1, wg2, least, w4):
    v = unpack_weight(tab_words, tab_scales, "e4m3")[:, unstriped(offs)]
    w1 = unpack_weight(w1_words, w1_scales, "e2m1")
    w3 = unpack_weight(w3_words, w3_scales, "e4m3")
    h1 = w1.T @ v
    d = np.maximum((mxq(f64(w2), 0, "e4m3").T @ v) + f64(b2)[:, None], 0.0)
    h2 = w3.T @ mxq(d, 0, "e4m3")
    pageA = np.zeros((H, T2))
    pageA[:, unstriped(offs2)] = np.tile(f64(wg1), (H // 128, 1)) * h1
    pageB = np.zeros((H, T2))
    pageB[:, unstriped(offs3)] = np.tile(f64(wg2), (H // 128, 1)) * h2
    z = np.maximum(np.maximum(pageA, pageB), f64(least))
    return mxq(f64(w4), 0, "e4m3").T @ mxq(z, 0, "e4m3")

@@ -1,0 +1,270 @@
+from contextlib import ExitStack
+
+import concourse.mybir as mybir
+
+K, R, H, N, T, S, T2 = 1024, 512, 1024, 512, 2048, 512, 1024
+FLOPS = 2 * (K * H * S + K * R * S + R * H * S + H * N * T2)
+
+F32 = mybir.dt.float32
+BF16 = mybir.dt.bfloat16
+I32 = mybir.dt.int32
+U32 = mybir.dt.uint32
+U16 = mybir.dt.uint16
+U8 = mybir.dt.uint8
+FP8X4 = mybir.dt.float8_e4m3fn_x4
+FP4X4 = mybir.dt.float4_e2m1fn_x4
+MULT = mybir.AluOpType.mult
+MAX = mybir.AluOpType.max
+RELU = mybir.ActivationFunctionType.Relu
+
+P = 128
+CH = 256
+A_PAGES, B_PAGES = 3, 2
+
+
+def tile_list_antenna_hour_urgency_kernel(tc, tab_words, tab_scales, offs, offs2, offs3, w1_words,
+                                                    w1_scales, w2, b2, w3_words, w3_scales, wg1, wg2, least, w4, out):
+    nc = tc.nc
+    with ExitStack() as ctx:
+        sb = ctx.enter_context(tc.tile_pool(name="sb", bufs=1))
+        ring = ctx.enter_context(tc.tile_pool(name="ring", bufs=2))
+        ps = ctx.enter_context(tc.psum_pool(name="ps", bufs=1))
+
+        def tile(name, shape, dtype, tag=None):
+            return sb.tile(shape, dtype, name=name, tag=tag or name, align_bytes=64)
+
+        def bank(b, name):
+            return ps.tile([P, 512], F32, name=name, tag="bank%d" % b)
+
+        idx = tile("idx", [P, S // 16], U16)
+        idx2 = tile("idx2", [P, S // 16], U16)
+        idx3 = tile("idx3", [P, S // 16], U16)
+        tab = [tile("tab%d" % a, [P, T], I32) for a in range(2)]
+        tab_s = tile("tab_s", [P, 2, T], U8)
+        w1_raw = tile("w1_raw", [P, 2, 2 * H], U8)
+        w1s_raw = tile("w1s_raw", [P, 2, H], U8)
+        w3_raw = tile("w3_raw", [P, H], I32)
+        w3s_raw = tile("w3s_raw", [P, H], U8)
+        wgA = tile("wgA", [P, 4, S], F32)
+        wgB = tile("wgB", [P, 4, S], F32)
+        w2_raw = [tile("w2_raw%d" % a, [P, 4, R], F32, tag="plane%d" % a) for a in range(2)]
+        w4_raw = [tile("w4_raw%d" % a, [P, 4, N], F32) for a in range(2)]
+        bias = tile("bias", [P, 4], F32)
+        l_raw = [tile("l_raw%d" % s, [P, T2], F32, tag="lz%d" % s) for s in range(8)]
+        pageA = [tile("pageA%d" % i, [P, T2], F32) for i in range(A_PAGES)]
+        pageB = [tile("pageB%d" % i, [P, T2], F32) for i in range(B_PAGES)]
+
+        nc.vector.memset(tab_s[:].bitcast(I32), 0)
+        nc.vector.memset(w1s_raw[:].bitcast(I32), 0)
+
+        nc.sync.dma_start(idx[:], offs)
+        nc.sync.dma_start(tab[0][:], tab_words[0].rearrange("p t i -> p (t i)").bitcast(I32))
+        nc.sync.dma_start(w1_raw[:].bitcast(I32), w1_words.rearrange("a p b -> p a b").bitcast(I32))
+        nc.sync.dma_start(tab[1][:], tab_words[1].rearrange("p t i -> p (t i)").bitcast(I32))
+        for q in range(4):
+            nc.scalar.dma_start(tab_s[32 * q:32 * q + 4].bitcast(I32),
+                                tab_scales[:, 4 * q:4 * q + 4, :].rearrange("a q c -> q a c").bitcast(I32))
+        for q in range(4):
+            nc.scalar.dma_start(w1s_raw[32 * q:32 * q + 4].bitcast(I32),
+                                w1_scales[:, 4 * q:4 * q + 4, :].rearrange("a q c -> q a c").bitcast(I32))
+        nc.sync.dma_start(idx2[:], offs2)
+        for q in (0, 2, 1, 3):
+            nc.sync.dma_start(wgA[32 * q:32 * q + 32], wg1.rearrange("(p t) j -> p t j", t=4))
+        for a in range(2):
+            nc.sync.dma_start(w2_raw[a][:], w2[512 * a:512 * a + 512].rearrange("(p j) m -> p j m", j=4))
+        nc.sync.dma_start(bias[:], b2.rearrange("(p t) -> p t", t=4))
+        for page in pageA:
+            nc.vector.memset(page[:], 0.0)
+        nc.vector.memset(w3s_raw[:].bitcast(I32), 0)
+        for page in pageB:
+            nc.vector.memset(page[:], 0.0)
+        nc.sync.dma_start(w3_raw[:], w3_words[0].rearrange("p c i -> p (c i)").bitcast(I32))
+        for q in range(4):
+            nc.sync.dma_start(w3s_raw[32 * q:32 * q + 4].bitcast(I32), w3_scales[0, 4 * q:4 * q + 4, :].bitcast(I32))
+        least_v = least.rearrange("(a p t) c -> a t p c", a=2, t=4)
+        for s in range(4):
+            nc.sync.dma_start(l_raw[s][:], least_v[0, s])
+        nc.sync.dma_start(idx3[:], offs3)
+        for q in (0, 2, 1, 3):
+            nc.sync.dma_start(wgB[32 * q:32 * q + 32], wg2.rearrange("(p t) j -> p t j", t=4))
+        for a in range(2):
+            nc.sync.dma_start(w4_raw[a][:], w4[512 * a:512 * a + 512].rearrange("(p j) n -> p j n", j=4))
+        for s in range(4, 8):
+            nc.sync.dma_start(l_raw[s][:], least_v[1, s - 4])
+
+        v_w = [tile("v_w%d" % a, [P, S], U32) for a in range(2)]
+        v_s = [tile("v_s%d" % a, [P, S], U8) for a in range(2)]
+        w1_p = [tile("w1_p%d" % h, [P, 2, 1024], U8) for h in range(2)]
+        w1s_p = [tile("w1s_p%d" % h, [P, 2, 512], U8) for h in range(2)]
+
+        def permute_w1(h):
+            nc.vector.tensor_copy(
+                w1_p[h][:].bitcast(U16).rearrange("p a (t m) -> p a t m", t=4),
+                w1_raw[:].bitcast(U16)[:, :, 512 * h:512 * h + 512].rearrange("p a (m t) -> p a t m", t=4))
+            nc.vector.tensor_copy(
+                w1s_p[h][:].rearrange("p a (t m) -> p a t m", t=4),
+                w1s_raw[:, :, 512 * h:512 * h + 512].rearrange("p a (m t) -> p a t m", t=4))
+
+        for a in range(2):
+            nc.vector.tensor_copy(v_s[a][:], tab_s[:, a, :].indirect(idx[:]))
+        nc.vector.tensor_copy(v_w[0][:], tab[0][:].bitcast(U32).indirect(idx[:]))
+        permute_w1(0)
+        nc.vector.tensor_copy(v_w[1][:], tab[1][:].bitcast(U32).indirect(idx[:]))
+        permute_w1(1)
+
+        h1 = [tile("h1_%d" % s, [P, S], F32) for s in range(8)]
+        h2 = [tile("h2_%d" % s, [P, S], F32) for s in range(8)]
+        for s in range(8):
+            h, t = divmod(s, 4)
+            acc = bank(s, "acc_h1_%d" % s)
+            for a in range(2):
+                nc.tensor.matmul_mx(out=acc[:], lhsT=w1_p[h][:, a, 256 * t:256 * t + 256].bitcast(FP4X4),
+                                    lhsT_scale=w1s_p[h][:, a, 128 * t:128 * t + 128],
+                                    rhs=v_w[a][:].bitcast(FP8X4), rhs_scale=v_s[a][:], start=(a == 0), stop=(a == 1))
+            nc.scalar.copy(h1[s][:], acc[:])
+
+        def scatter_a(s):
+            nc.vector.tensor_tensor(pageA[s % A_PAGES][:].indirect(idx2[:]), h1[s][:], wgA[:, s % 4, :], MULT)
+
+        def scatter_b(s):
+            nc.vector.tensor_tensor(pageB[s % B_PAGES][:].indirect(idx3[:]), h2[s][:], wgB[:, s % 4, :], MULT)
+
+        for s in range(A_PAGES):
+            scatter_a(s)
+
+        w2_q = tile("w2_q", [P, 2, R], U32)
+        w2_s = tile("w2_s", [P, 2, R], U8)
+        for a in range(2):
+            w2_b = tile("w2_b%d" % a, [P, 4 * R], BF16, tag="wb%d" % a)
+            nc.scalar.copy(w2_b[:].rearrange("p (t m j) -> p m t j", t=4, j=4),
+                           w2_raw[a][:].rearrange("p j (m t) -> p m t j", t=4))
+            nc.vector.quantize_mx(out=w2_q[:, a, :].bitcast(FP8X4), scales=w2_s[:, a, :], in_=w2_b[:])
+        w3_p = tile("w3_p", [P, H], I32)
+        w3s_p = tile("w3s_p", [P, H], U8)
+        nc.vector.tensor_copy(w3_p[:].rearrange("p (h t u i) -> p h u t i", h=2, t=4, i=4),
+                              w3_raw[:].rearrange("p (h u i t) -> p h u t i", h=2, t=4, i=4))
+        nc.vector.tensor_copy(w3s_p[:].rearrange("p (h t m) -> p h t m", h=2, t=4),
+                              w3s_raw[:].rearrange("p (h m t) -> p h t m", h=2, t=4))
+
+        d_pl = tile("d_pl", [P, 4, S], BF16)
+        d_b = tile("d_b", [P, S, 4], BF16)
+        d_q = tile("d_q", [P, S], U32)
+        d_s = tile("d_s", [P, S], U8)
+        for t in range(4):
+            acc = bank(t, "acc_d_%d" % t)
+            for a in range(2):
+                nc.tensor.matmul_mx(out=acc[:], lhsT=w2_q[:, a, 128 * t:128 * t + 128].bitcast(FP8X4),
+                                    lhsT_scale=w2_s[:, a, 128 * t:128 * t + 128],
+                                    rhs=v_w[a][:].bitcast(FP8X4), rhs_scale=v_s[a][:], start=(a == 0), stop=(a == 1))
+            nc.scalar.activation(d_pl[:, t, :], acc[:], RELU, bias=bias[:, t:t + 1])
+        nc.scalar.copy(d_b[:].rearrange("p (c i) t -> p c t i", i=4), d_pl[:].rearrange("p t (c i) -> p c t i", i=4))
+        nc.vector.quantize_mx(out=d_q[:].bitcast(FP8X4), scales=d_s[:], in_=d_b[:].rearrange("p j t -> p (j t)"))
+
+        z_pl = [tile("z_pl%d" % a, [P, 4, T2], BF16, tag="plane%d" % a) for a in range(2)]
+
+        def plane(s):
+            return z_pl[s // 4][:, s % 4, :]
+
+        def round_a(s):
+            nc.scalar.copy(plane(s), pageA[s % A_PAGES][:])
+            if s + A_PAGES < 8:
+                scatter_a(s + A_PAGES)
+
+        def max_least(s):
+            l_b = ring.tile([P, T2], BF16, name="l_b", tag="l_b")
+            nc.scalar.copy(l_b[:], l_raw[s][:])
+            nc.vector.tensor_tensor(plane(s), plane(s), l_b[:], MAX)
+
+        for s in range(3):
+            round_a(s)
+        for s in range(8):
+            acc = bank((s + 4) % 8, "acc_h2_%d" % s)
+            nc.tensor.matmul_mx(out=acc[:], lhsT=w3_p[:, 128 * s:128 * s + 128].bitcast(FP8X4),
+                                lhsT_scale=w3s_p[:, 128 * s:128 * s + 128],
+                                rhs=d_q[:].bitcast(FP8X4), rhs_scale=d_s[:], start=True, stop=True)
+            nc.scalar.copy(h2[s][:], acc[:])
+        for s in range(3, 6):
+            round_a(s)
+        for s in range(B_PAGES):
+            scatter_b(s)
+        for s in range(4):
+            max_least(s)
+        for s in range(6, 8):
+            round_a(s)
+
+        w4_q = tile("w4_q", [P, 2, N], U32)
+        w4_s = tile("w4_s", [P, 2, N], U8)
+        z_q = tile("z_q", [P, 2, T2], U32)
+        z_s = [tile("z_s%d" % i, [P, CH], U8) for i in range(8)]
+        o_acc = [bank(b, "acc_o_%d" % b) for b in range(8)]
+        o_sb = [tile("o_sb%d" % i, [P, 4, 512], F32, tag="tab%d" % i) for i in range(2)]
+        out_v = out.rearrange("(n p) c -> p n c", p=P)
+
+        def quantise_w4(a):
+            w4_b = tile("w4_b%d" % a, [P, N, 4], BF16, tag="wb%d" % a)
+            nc.scalar.copy(w4_b[:].rearrange("p (c i) j -> p c j i", i=4),
+                           w4_raw[a][:].rearrange("p j (c i) -> p c j i", i=4))
+            nc.vector.quantize_mx(out=w4_q[:, a, :].bitcast(FP8X4), scales=w4_s[:, a, :],
+                                  in_=w4_b[:].rearrange("p n j -> p (n j)"))
+
+        def max_b(s):
+            b_b = ring.tile([P, T2], BF16, name="b_b", tag="b_b")
+            nc.scalar.copy(b_b[:], pageB[s % B_PAGES][:])
+            nc.vector.tensor_tensor(plane(s), plane(s), b_b[:], MAX)
+            if s + B_PAGES < 8:
+                scatter_b(s + B_PAGES)
+
+        def finish(a, c, on_vector):
+            cols = slice(CH * c, CH * c + CH)
+            z_b = tile("z_b%d" % (4 * a + c), [P, CH, 4], BF16, tag="lz%d" % (4 * a + c))
+            dst = z_b[:].rearrange("p (c i) t -> p c t i", i=4)
+            src = z_pl[a][:, :, cols].rearrange("p t (c i) -> p c t i", i=4)
+            if on_vector:
+                nc.vector.tensor_copy(dst, src)
+            else:
+                nc.scalar.copy(dst, src)
+            nc.vector.quantize_mx(out=z_q[:, a, cols].bitcast(FP8X4), scales=z_s[4 * a + c][:],
+                                  in_=z_b[:].rearrange("p c t -> p (c t)"))
+            for n in range(4):
+                acc = o_acc[2 * c + n // 2]
+                nc.tensor.matmul_mx(out=acc[:, CH * (n % 2):CH * (n % 2) + CH],
+                                    lhsT=w4_q[:, a, 128 * n:128 * n + 128].bitcast(FP8X4),
+                                    lhsT_scale=w4_s[:, a, 128 * n:128 * n + 128],
+                                    rhs=z_q[:, a, cols].bitcast(FP8X4), rhs_scale=z_s[4 * a + c][:],
+                                    start=(a == 0 and n % 2 == 0), stop=(a == 1 and n % 2 == 1))
+
+        max_b(0)
+        quantise_w4(0)
+        max_b(1)
+        quantise_w4(1)
+        max_b(2)
+        max_least(4)
+        max_least(5)
+        max_b(3)
+        max_least(6)
+        finish(0, 0, False)
+        max_b(4)
+        max_least(7)
+        finish(0, 1, False)
+        max_b(5)
+        finish(0, 2, False)
+        finish(0, 3, False)
+        max_b(6)
+        def max_last(c):
+            cols = slice(CH * c, CH * c + CH)
+            nc.vector.tensor_tensor(z_pl[1][:, 3, cols], pageB[7 % B_PAGES][:, cols], z_pl[1][:, 3, cols], MAX)
+
+        max_last(0)
+        for c in range(4):
+            cols = slice(CH * c, CH * c + CH)
+            if c < 3:
+                max_last(c + 1)
+            finish(1, c, c != 1)
+            for k in range(2):
+                b = 2 * c + k
+                dst = o_sb[b // 4][:, b % 4, :]
+                if b == 7:
+                    nc.vector.tensor_copy(dst, o_acc[b][:])
+                else:
+                    nc.scalar.copy(dst, o_acc[b][:])
+                nc.sync.dma_start(out_v[:, 2 * k:2 * k + 2, cols], dst.rearrange("p (n c) -> p n c", n=2))

@@ -19,7 +19,7 @@ RELU = mybir.ActivationFunctionType.Relu
 
 P = 128
 CH = 256
-A_PAGES, B_PAGES = 3, 2
+A_PAGES, B_PAGES = 4, 2
 
 
 def tile_list_antenna_hour_urgency_kernel(tc, tab_words, tab_scales, offs, offs2, offs3, w1_words,
@@ -39,112 +39,155 @@ def tile_list_antenna_hour_urgency_kernel(tc, tab_words, tab_scales, offs, offs2
         idx = tile("idx", [P, S // 16], U16)
         idx2 = tile("idx2", [P, S // 16], U16)
         idx3 = tile("idx3", [P, S // 16], U16)
-        tab = [tile("tab%d" % a, [P, T], I32) for a in range(2)]
+        tab = [tile("tab%d" % a, [P, T], I32, tag=("wgA", "big1")[a]) for a in range(2)]
         tab_s = tile("tab_s", [P, 2, T], U8)
-        w1_raw = tile("w1_raw", [P, 2, 2 * H], U8)
-        w1s_raw = tile("w1s_raw", [P, 2, H], U8)
-        w3_raw = tile("w3_raw", [P, H], I32)
-        w3s_raw = tile("w3s_raw", [P, H], U8)
-        wgA = tile("wgA", [P, 4, S], F32)
-        wgB = tile("wgB", [P, 4, S], F32)
-        w2_raw = [tile("w2_raw%d" % a, [P, 4, R], F32, tag="plane%d" % a) for a in range(2)]
-        w4_raw = [tile("w4_raw%d" % a, [P, 4, N], F32) for a in range(2)]
-        bias = tile("bias", [P, 4], F32)
-        l_raw = [tile("l_raw%d" % s, [P, T2], F32, tag="lz%d" % s) for s in range(8)]
-        pageA = [tile("pageA%d" % i, [P, T2], F32) for i in range(A_PAGES)]
-        pageB = [tile("pageB%d" % i, [P, T2], F32) for i in range(B_PAGES)]
-
-        nc.vector.memset(tab_s[:].bitcast(I32), 0)
-        nc.vector.memset(w1s_raw[:].bitcast(I32), 0)
+        w1_raw = tile("w1_raw", [P, 2, 2 * H], U8, tag="big0")
+        w1s_raw = tile("w1s_raw", [P, 2, H], U8, tag="pageA2")
+        v_w = [tile("v_w%d" % a, [P, S], U32) for a in range(2)]
+        v_g = tile("v_g", [P, 2, S], U8, tag="w3_raw")
+        v_s = tile("v_s", [P, 2, S], U8)
+        w1_p, w1s_p = [], []
 
         nc.sync.dma_start(idx[:], offs)
+        nc.sync.dma_start(idx2[:], offs2)
+        nc.sync.dma_start(idx3[:], offs3)
+        nc.sync.dma_start(tab_s[16:32].bitcast(I32), tab_scales.rearrange("a q c -> q a c").bitcast(I32))
         nc.sync.dma_start(tab[0][:], tab_words[0].rearrange("p t i -> p (t i)").bitcast(I32))
         nc.sync.dma_start(w1_raw[:].bitcast(I32), w1_words.rearrange("a p b -> p a b").bitcast(I32))
         nc.sync.dma_start(tab[1][:], tab_words[1].rearrange("p t i -> p (t i)").bitcast(I32))
-        for q in range(4):
-            nc.scalar.dma_start(tab_s[32 * q:32 * q + 4].bitcast(I32),
-                                tab_scales[:, 4 * q:4 * q + 4, :].rearrange("a q c -> q a c").bitcast(I32))
-        for q in range(4):
-            nc.scalar.dma_start(w1s_raw[32 * q:32 * q + 4].bitcast(I32),
-                                w1_scales[:, 4 * q:4 * q + 4, :].rearrange("a q c -> q a c").bitcast(I32))
-        nc.sync.dma_start(idx2[:], offs2)
-        for q in (0, 2, 1, 3):
-            nc.sync.dma_start(wgA[32 * q:32 * q + 32], wg1.rearrange("(p t) j -> p t j", t=4))
-        for a in range(2):
-            nc.sync.dma_start(w2_raw[a][:], w2[512 * a:512 * a + 512].rearrange("(p j) m -> p j m", j=4))
-        nc.sync.dma_start(bias[:], b2.rearrange("(p t) -> p t", t=4))
-        for page in pageA:
-            nc.vector.memset(page[:], 0.0)
-        nc.vector.memset(w3s_raw[:].bitcast(I32), 0)
-        for page in pageB:
-            nc.vector.memset(page[:], 0.0)
-        nc.sync.dma_start(w3_raw[:], w3_words[0].rearrange("p c i -> p (c i)").bitcast(I32))
-        for q in range(4):
-            nc.sync.dma_start(w3s_raw[32 * q:32 * q + 4].bitcast(I32), w3_scales[0, 4 * q:4 * q + 4, :].bitcast(I32))
-        least_v = least.rearrange("(a p t) c -> a t p c", a=2, t=4)
-        for s in range(4):
-            nc.sync.dma_start(l_raw[s][:], least_v[0, s])
-        nc.sync.dma_start(idx3[:], offs3)
-        for q in (0, 2, 1, 3):
-            nc.sync.dma_start(wgB[32 * q:32 * q + 32], wg2.rearrange("(p t) j -> p t j", t=4))
-        for a in range(2):
-            nc.sync.dma_start(w4_raw[a][:], w4[512 * a:512 * a + 512].rearrange("(p j) n -> p j n", j=4))
-        for s in range(4, 8):
-            nc.sync.dma_start(l_raw[s][:], least_v[1, s - 4])
 
-        v_w = [tile("v_w%d" % a, [P, S], U32) for a in range(2)]
-        v_s = [tile("v_s%d" % a, [P, S], U8) for a in range(2)]
-        w1_p = [tile("w1_p%d" % h, [P, 2, 1024], U8) for h in range(2)]
-        w1s_p = [tile("w1s_p%d" % h, [P, 2, 512], U8) for h in range(2)]
+        pageA = [tile("pageA%d" % i, [P, T2], F32) for i in range(2)]
+        nc.gpsimd.memset(pageA[0][:], 0.0)
+        nc.vector.memset(w1s_raw[:].bitcast(I32), 0)
+        for q in range(4):
+            (nc.gpsimd if q >= 2 else nc.scalar).dma_start(
+                w1s_raw[32 * q:32 * q + 4].bitcast(I32),
+                w1_scales[:, 4 * q:4 * q + 4, :].rearrange("a q c -> q a c").bitcast(I32))
+        for rows in (slice(0, 16), slice(32, 64), slice(64, 128)):
+            nc.vector.memset(tab_s[rows].bitcast(I32), 0)
+        nc.vector.memset(v_s[:].bitcast(I32), 0)
+        nc.gpsimd.memset(pageA[1][:], 0.0)
+        for a in range(2):
+            nc.vector.tensor_copy(v_g[:, a, :], tab_s[:, a, :].indirect(idx[:]))
+        for q in range(4):
+            nc.scalar.dma_start(v_s[32 * q:32 * q + 4].bitcast(I32), v_g[16 + 4 * q:20 + 4 * q].bitcast(I32))
 
         def permute_w1(h):
+            both = tile("w1_p%d" % h, [P, 3072], U8, tag=("w1_p0", "big1")[h])
+            w1_p.append(both[:, 0:2048].rearrange("p (a b) -> p a b", a=2))
+            w1s_p.append(both[:, 2048:3072].rearrange("p (a b) -> p a b", a=2))
             nc.vector.tensor_copy(
-                w1_p[h][:].bitcast(U16).rearrange("p a (t m) -> p a t m", t=4),
+                w1_p[h].bitcast(U16).rearrange("p a (t m) -> p a t m", t=4),
                 w1_raw[:].bitcast(U16)[:, :, 512 * h:512 * h + 512].rearrange("p a (m t) -> p a t m", t=4))
             nc.vector.tensor_copy(
-                w1s_p[h][:].rearrange("p a (t m) -> p a t m", t=4),
+                w1s_p[h].rearrange("p a (t m) -> p a t m", t=4),
                 w1s_raw[:, :, 512 * h:512 * h + 512].rearrange("p a (m t) -> p a t m", t=4))
 
-        for a in range(2):
-            nc.vector.tensor_copy(v_s[a][:], tab_s[:, a, :].indirect(idx[:]))
         nc.vector.tensor_copy(v_w[0][:], tab[0][:].bitcast(U32).indirect(idx[:]))
         permute_w1(0)
         nc.vector.tensor_copy(v_w[1][:], tab[1][:].bitcast(U32).indirect(idx[:]))
         permute_w1(1)
+        pageA.append(tile("pageA2", [P, T2], F32))
+        nc.gpsimd.memset(pageA[2][:], 0.0)
 
-        h1 = [tile("h1_%d" % s, [P, S], F32) for s in range(8)]
+        wgA_t = tile("wgA", [P, 4 * S + 16], F32, tag="wgA")
+        wgA = wgA_t[:, 0:4 * S].rearrange("p (t j) -> p t j", t=4)
+        bias = wgA_t[:, 4 * S:4 * S + 4]
+        w2_raw = tile("w2_raw", [P, 2, 4, R], F32, tag="big0")
+        w3_in = tile("w3_in", [P, H + H // 4], I32, tag="w3_raw")
+        w3_raw = w3_in[:, 0:H]
+        w3s_raw = w3_in[:, H:H + H // 4]
+        nc.gpsimd.memset(w3s_raw, 0)
+        wg1_v = wg1.rearrange("(p t) j -> p t j", t=4)
+        for q in (0, 2, 1, 3):
+            nc.sync.dma_start(wgA[32 * q:32 * q + 32, 0, :], wg1_v[:, 0, :])
+        for q in (0, 2, 1, 3):
+            nc.sync.dma_start(wgA[32 * q:32 * q + 32, 1:4, :], wg1_v[:, 1:4, :])
+        for a in range(2):
+            nc.sync.dma_start(w2_raw[:, a], w2[512 * a:512 * a + 512].rearrange("(p j) m -> p j m", j=4))
+        nc.sync.dma_start(bias, b2.rearrange("(p t) -> p t", t=4))
+        nc.sync.dma_start(w3_raw, w3_words[0].rearrange("p c i -> p (c i)").bitcast(I32))
+        for q in range(4):
+            nc.sync.dma_start(w3s_raw[32 * q:32 * q + 4], w3_scales[0, 4 * q:4 * q + 4, :].bitcast(I32))
+
+        h1_acc = [bank(s, "acc_h1_%d" % s) for s in range(8)]
+        h1 = [tile("h1_%d" % s, [P, S], F32) for s in range(7)]
         h2 = [tile("h2_%d" % s, [P, S], F32) for s in range(8)]
         for s in range(8):
             h, t = divmod(s, 4)
-            acc = bank(s, "acc_h1_%d" % s)
-            for a in range(2):
-                nc.tensor.matmul_mx(out=acc[:], lhsT=w1_p[h][:, a, 256 * t:256 * t + 256].bitcast(FP4X4),
+            first, last = (0, 1) if s == 0 else (1, 0)
+            for a in (first, last):
+                nc.tensor.matmul_mx(out=h1_acc[s][:], lhsT=w1_p[h][:, a, 256 * t:256 * t + 256].bitcast(FP4X4),
                                     lhsT_scale=w1s_p[h][:, a, 128 * t:128 * t + 128],
-                                    rhs=v_w[a][:].bitcast(FP8X4), rhs_scale=v_s[a][:], start=(a == 0), stop=(a == 1))
-            nc.scalar.copy(h1[s][:], acc[:])
+                                    rhs=v_w[a][:].bitcast(FP8X4), rhs_scale=v_s[:, a, :],
+                                    start=(a == first), stop=(a == last))
+            if s < 7:
+                nc.scalar.copy(h1[s][:], h1_acc[s][:])
+
+        l_raw = tile("l_raw", [P, 8, T2], F32, tag="big1")
+        least_v = least.rearrange("(a p t) c -> a t p c", a=2, t=4)
+        for s in range(4):
+            nc.sync.dma_start(l_raw[:, s, :], least_v[0, s])
 
         def scatter_a(s):
             nc.vector.tensor_tensor(pageA[s % A_PAGES][:].indirect(idx2[:]), h1[s][:], wgA[:, s % 4, :], MULT)
 
-        def scatter_b(s):
-            nc.vector.tensor_tensor(pageB[s % B_PAGES][:].indirect(idx3[:]), h2[s][:], wgB[:, s % 4, :], MULT)
+        def page_b(s):
+            return pageB[min(s, 6) % B_PAGES]
 
-        for s in range(A_PAGES):
+        def scatter_b(s):
+            nc.vector.tensor_tensor(page_b(s)[:].indirect(idx3[:]), h2[s][:], wgB[:, s % 4, :], MULT)
+
+        for s in range(3):
             scatter_a(s)
+        pageA.append(tile("pageA3", [P, T2], F32, tag="h1_0"))
+        nc.gpsimd.memset(pageA[3][:], 0.0)
+        scatter_a(3)
+        late = tile("late", [P, 12, S], F32, tag="h1_1")
+        wgB = late[:, 0:4, :]
+        w4_raw = [late[:, 4 + 4 * a:8 + 4 * a, :] for a in range(2)]
+        for q in (0, 2, 1, 3):
+            nc.sync.dma_start(wgB[32 * q:32 * q + 32], wg2.rearrange("(p t) j -> p t j", t=4))
+        for a in range(2):
+            nc.sync.dma_start(w4_raw[a], w4[512 * a:512 * a + 512].rearrange("(p j) n -> p j n", j=4))
+        for s in range(4, 8):
+            nc.sync.dma_start(l_raw[:, s, :], least_v[1, s - 4])
 
         w2_q = tile("w2_q", [P, 2, R], U32)
         w2_s = tile("w2_s", [P, 2, R], U8)
         for a in range(2):
             w2_b = tile("w2_b%d" % a, [P, 4 * R], BF16, tag="wb%d" % a)
             nc.scalar.copy(w2_b[:].rearrange("p (t m j) -> p m t j", t=4, j=4),
-                           w2_raw[a][:].rearrange("p j (m t) -> p m t j", t=4))
+                           w2_raw[:, a].rearrange("p j (m t) -> p m t j", t=4))
             nc.vector.quantize_mx(out=w2_q[:, a, :].bitcast(FP8X4), scales=w2_s[:, a, :], in_=w2_b[:])
+        pageB = [tile("pageB%d" % i, [P, T2], F32, tag="wb%d" % i) for i in range(B_PAGES)]
+        for page in pageB:
+            nc.gpsimd.memset(page[:], 0.0)
         w3_p = tile("w3_p", [P, H], I32)
-        w3s_p = tile("w3s_p", [P, H], U8)
         nc.vector.tensor_copy(w3_p[:].rearrange("p (h t u i) -> p h u t i", h=2, t=4, i=4),
-                              w3_raw[:].rearrange("p (h u i t) -> p h u t i", h=2, t=4, i=4))
+                              w3_raw.rearrange("p (h u i t) -> p h u t i", h=2, t=4, i=4))
+        w3s_p = tile("w3s_p", [P, H], U8)
         nc.vector.tensor_copy(w3s_p[:].rearrange("p (h t m) -> p h t m", h=2, t=4),
-                              w3s_raw[:].rearrange("p (h m t) -> p h t m", h=2, t=4))
+                              w3s_raw.bitcast(U8).rearrange("p (h m t) -> p h t m", h=2, t=4))
+
+        z_pl = [tile("z_pl0", [P, 4, T2], BF16, tag="big0")]
+        l_b = [tile("l_b0", [P, 4, T2], BF16)]
+
+        def plane(s):
+            return z_pl[s // 4][:, s % 4, :]
+
+        def round_a(s):
+            nc.scalar.copy(plane(s), pageA[s % A_PAGES][:])
+
+        def max_least(s):
+            nc.scalar.copy(l_b[s // 4][:, s % 4, :], l_raw[:, s, :])
+            nc.vector.tensor_tensor(plane(s), plane(s), l_b[s // 4][:, s % 4, :], MAX)
+
+        for s in range(3):
+            round_a(s)
+            scatter_a(s + A_PAGES)
+        for s in range(3):
+            max_least(s)
 
         d_pl = tile("d_pl", [P, 4, S], BF16)
         d_b = tile("d_b", [P, S, 4], BF16)
@@ -155,76 +198,60 @@ def tile_list_antenna_hour_urgency_kernel(tc, tab_words, tab_scales, offs, offs2
             for a in range(2):
                 nc.tensor.matmul_mx(out=acc[:], lhsT=w2_q[:, a, 128 * t:128 * t + 128].bitcast(FP8X4),
                                     lhsT_scale=w2_s[:, a, 128 * t:128 * t + 128],
-                                    rhs=v_w[a][:].bitcast(FP8X4), rhs_scale=v_s[a][:], start=(a == 0), stop=(a == 1))
+                                    rhs=v_w[a][:].bitcast(FP8X4), rhs_scale=v_s[:, a, :], start=(a == 0), stop=(a == 1))
             nc.scalar.activation(d_pl[:, t, :], acc[:], RELU, bias=bias[:, t:t + 1])
         nc.scalar.copy(d_b[:].rearrange("p (c i) t -> p c t i", i=4), d_pl[:].rearrange("p t (c i) -> p c t i", i=4))
         nc.vector.quantize_mx(out=d_q[:].bitcast(FP8X4), scales=d_s[:], in_=d_b[:].rearrange("p j t -> p (j t)"))
 
-        z_pl = [tile("z_pl%d" % a, [P, 4, T2], BF16, tag="plane%d" % a) for a in range(2)]
-
-        def plane(s):
-            return z_pl[s // 4][:, s % 4, :]
-
-        def round_a(s):
-            nc.scalar.copy(plane(s), pageA[s % A_PAGES][:])
-            if s + A_PAGES < 8:
-                scatter_a(s + A_PAGES)
-
-        def max_least(s):
-            l_b = ring.tile([P, T2], BF16, name="l_b", tag="l_b")
-            nc.scalar.copy(l_b[:], l_raw[s][:])
-            nc.vector.tensor_tensor(plane(s), plane(s), l_b[:], MAX)
-
-        for s in range(3):
-            round_a(s)
+        h1.append(tile("h1_7", [P, S], F32, tag="d_pl"))
+        nc.scalar.copy(h1[7][:], h1_acc[7][:])
+        round_a(3)
+        scatter_a(7)
+        max_least(3)
         for s in range(8):
-            acc = bank((s + 4) % 8, "acc_h2_%d" % s)
+            acc = bank((s + 4) % 7 if s < 7 else 7, "acc_h2_%d" % s)
             nc.tensor.matmul_mx(out=acc[:], lhsT=w3_p[:, 128 * s:128 * s + 128].bitcast(FP8X4),
                                 lhsT_scale=w3s_p[:, 128 * s:128 * s + 128],
                                 rhs=d_q[:].bitcast(FP8X4), rhs_scale=d_s[:], start=True, stop=True)
             nc.scalar.copy(h2[s][:], acc[:])
-        for s in range(3, 6):
-            round_a(s)
+        z_pl.append(tile("z_pl1", [P, 4, T2], BF16, tag="w3_p"))
+        l_b.append(tile("l_b1", [P, 4, T2], BF16, tag="d_s"))
         for s in range(B_PAGES):
             scatter_b(s)
-        for s in range(4):
-            max_least(s)
-        for s in range(6, 8):
-            round_a(s)
 
         w4_q = tile("w4_q", [P, 2, N], U32)
         w4_s = tile("w4_s", [P, 2, N], U8)
         z_q = tile("z_q", [P, 2, T2], U32)
         z_s = [tile("z_s%d" % i, [P, CH], U8) for i in range(8)]
         o_acc = [bank(b, "acc_o_%d" % b) for b in range(8)]
-        o_sb = [tile("o_sb%d" % i, [P, 4, 512], F32, tag="tab%d" % i) for i in range(2)]
+        o_sb = [tile("o_sb%d" % i, [P, 4, CH], F32, tag=("pageA0", "pageA1", "pageA2", "h1_0")[i]) for i in range(4)]
         out_v = out.rearrange("(n p) c -> p n c", p=P)
 
         def quantise_w4(a):
-            w4_b = tile("w4_b%d" % a, [P, N, 4], BF16, tag="wb%d" % a)
+            w4_b = tile("w4_b%d" % a, [P, N, 4], BF16, tag=("d_q", "w3s_p")[a])
             nc.scalar.copy(w4_b[:].rearrange("p (c i) j -> p c j i", i=4),
-                           w4_raw[a][:].rearrange("p j (c i) -> p c j i", i=4))
+                           w4_raw[a].rearrange("p j (c i) -> p c j i", i=4))
             nc.vector.quantize_mx(out=w4_q[:, a, :].bitcast(FP8X4), scales=w4_s[:, a, :],
                                   in_=w4_b[:].rearrange("p n j -> p (n j)"))
 
         def max_b(s):
             b_b = ring.tile([P, T2], BF16, name="b_b", tag="b_b")
-            nc.scalar.copy(b_b[:], pageB[s % B_PAGES][:])
+            nc.scalar.copy(b_b[:], page_b(s)[:])
             nc.vector.tensor_tensor(plane(s), plane(s), b_b[:], MAX)
-            if s + B_PAGES < 8:
+            if s + B_PAGES < 7:
                 scatter_b(s + B_PAGES)
 
-        def finish(a, c, on_vector):
+        z_b = [tile("z_b%d" % i, [P, CH, 4], BF16) for i in range(8)]
+
+        def weave(a, c):
             cols = slice(CH * c, CH * c + CH)
-            z_b = tile("z_b%d" % (4 * a + c), [P, CH, 4], BF16, tag="lz%d" % (4 * a + c))
-            dst = z_b[:].rearrange("p (c i) t -> p c t i", i=4)
-            src = z_pl[a][:, :, cols].rearrange("p t (c i) -> p c t i", i=4)
-            if on_vector:
-                nc.vector.tensor_copy(dst, src)
-            else:
-                nc.scalar.copy(dst, src)
+            nc.scalar.copy(z_b[4 * a + c][:].rearrange("p (c i) t -> p c t i", i=4),
+                           z_pl[a][:, :, cols].rearrange("p t (c i) -> p c t i", i=4))
+
+        def finish(a, c):
+            cols = slice(CH * c, CH * c + CH)
             nc.vector.quantize_mx(out=z_q[:, a, cols].bitcast(FP8X4), scales=z_s[4 * a + c][:],
-                                  in_=z_b[:].rearrange("p c t -> p (c t)"))
+                                  in_=z_b[4 * a + c][:].rearrange("p c t -> p (c t)"))
             for n in range(4):
                 acc = o_acc[2 * c + n // 2]
                 nc.tensor.matmul_mx(out=acc[:, CH * (n % 2):CH * (n % 2) + CH],
@@ -233,38 +260,48 @@ def tile_list_antenna_hour_urgency_kernel(tc, tab_words, tab_scales, offs, offs2
                                     rhs=z_q[:, a, cols].bitcast(FP8X4), rhs_scale=z_s[4 * a + c][:],
                                     start=(a == 0 and n % 2 == 0), stop=(a == 1 and n % 2 == 1))
 
-        max_b(0)
-        quantise_w4(0)
-        max_b(1)
-        quantise_w4(1)
-        max_b(2)
-        max_least(4)
-        max_least(5)
-        max_b(3)
-        max_least(6)
-        finish(0, 0, False)
-        max_b(4)
-        max_least(7)
-        finish(0, 1, False)
-        max_b(5)
-        finish(0, 2, False)
-        finish(0, 3, False)
-        max_b(6)
         def max_last(c):
             cols = slice(CH * c, CH * c + CH)
-            nc.vector.tensor_tensor(z_pl[1][:, 3, cols], pageB[7 % B_PAGES][:, cols], z_pl[1][:, 3, cols], MAX)
+            nc.vector.tensor_tensor(z_b[4 + c][:, :, 3], page_b(7)[:, cols], z_b[4 + c][:, :, 3], MAX)
 
+        max_b(0)
+        round_a(4)
+        round_a(5)
+        max_least(4)
+        max_b(1)
+        quantise_w4(0)
+        max_least(5)
+        max_b(2)
+        quantise_w4(1)
+        round_a(6)
+        max_b(3)
+        round_a(7)
+        max_least(6)
+        weave(0, 0)
+        finish(0, 0)
+        max_b(4)
+        max_least(7)
+        weave(0, 1)
+        finish(0, 1)
+        max_b(5)
+        for c in (2, 3):
+            weave(0, c)
+            finish(0, c)
+        max_b(6)
+        scatter_b(7)
+        for c in range(4):
+            weave(1, c)
         max_last(0)
         for c in range(4):
             cols = slice(CH * c, CH * c + CH)
             if c < 3:
                 max_last(c + 1)
-            finish(1, c, c != 1)
+            finish(1, c)
             for k in range(2):
                 b = 2 * c + k
-                dst = o_sb[b // 4][:, b % 4, :]
-                if b == 7:
+                dst = o_sb[c][:, 2 * k:2 * k + 2, :].rearrange("p n c -> p (n c)")
+                if b in (5, 7):
                     nc.vector.tensor_copy(dst, o_acc[b][:])
                 else:
                     nc.scalar.copy(dst, o_acc[b][:])
-                nc.sync.dma_start(out_v[:, 2 * k:2 * k + 2, cols], dst.rearrange("p (n c) -> p n c", n=2))
+            nc.sync.dma_start(out_v[:, :, cols], o_sb[c][:])

@@ -27,7 +27,6 @@ def tile_list_antenna_hour_urgency_kernel(tc, tab_words, tab_scales, offs, offs2
     nc = tc.nc
     with ExitStack() as ctx:
         sb = ctx.enter_context(tc.tile_pool(name="sb", bufs=1))
-        ring = ctx.enter_context(tc.tile_pool(name="ring", bufs=2))
         ps = ctx.enter_context(tc.psum_pool(name="ps", bufs=1))
 
         def tile(name, shape, dtype, tag=None):
@@ -41,12 +40,12 @@ def tile_list_antenna_hour_urgency_kernel(tc, tab_words, tab_scales, offs, offs2
         idx3 = tile("idx3", [P, S // 16], U16)
         tab = [tile("tab%d" % a, [P, T], I32, tag=("wgA", "big1")[a]) for a in range(2)]
         tab_s = tile("tab_s", [P, 2, T], U8)
-        w1_raw = tile("w1_raw", [P, 2, 2 * H], U8, tag="big0")
-        w1s_raw = tile("w1s_raw", [P, 2, H], U8, tag="pageA2")
-        v_w = [tile("v_w%d" % a, [P, S], U32) for a in range(2)]
-        v_g = tile("v_g", [P, 2, S], U8, tag="w3_raw")
+        w1_raw = tile("w1_raw", [P, 2, 2 * H], U8, tag="pageA2")
+        w1s_raw = tile("w1s_raw", [P, 2, H], U8, tag="v_w1")
+        v_w = [tile("v_w0", [P, S], U32)]
+        v_g = tile("v_g", [P, 2, S], U8, tag="big0")
         v_s = tile("v_s", [P, 2, S], U8)
-        w1_p, w1s_p = [], []
+        w1_p = []
 
         nc.sync.dma_start(idx[:], offs)
         nc.sync.dma_start(idx2[:], offs2)
@@ -60,7 +59,7 @@ def tile_list_antenna_hour_urgency_kernel(tc, tab_words, tab_scales, offs, offs2
         nc.gpsimd.memset(pageA[0][:], 0.0)
         nc.vector.memset(w1s_raw[:].bitcast(I32), 0)
         for q in range(4):
-            (nc.gpsimd if q >= 2 else nc.scalar).dma_start(
+            (nc.gpsimd if q >= 1 else nc.scalar).dma_start(
                 w1s_raw[32 * q:32 * q + 4].bitcast(I32),
                 w1_scales[:, 4 * q:4 * q + 4, :].rearrange("a q c -> q a c").bitcast(I32))
         for rows in (slice(0, 16), slice(32, 64), slice(64, 128)):
@@ -73,18 +72,17 @@ def tile_list_antenna_hour_urgency_kernel(tc, tab_words, tab_scales, offs, offs2
             nc.scalar.dma_start(v_s[32 * q:32 * q + 4].bitcast(I32), v_g[16 + 4 * q:20 + 4 * q].bitcast(I32))
 
         def permute_w1(h):
-            both = tile("w1_p%d" % h, [P, 3072], U8, tag=("w1_p0", "big1")[h])
-            w1_p.append(both[:, 0:2048].rearrange("p (a b) -> p a b", a=2))
-            w1s_p.append(both[:, 2048:3072].rearrange("p (a b) -> p a b", a=2))
+            w1_p.append(tile("w1_p%d" % h, [P, 2, 1024], U8, tag=("w1_p0", "big1")[h]))
             nc.vector.tensor_copy(
-                w1_p[h].bitcast(U16).rearrange("p a (t m) -> p a t m", t=4),
+                w1_p[h][:].bitcast(U16).rearrange("p a (t m) -> p a t m", t=4),
                 w1_raw[:].bitcast(U16)[:, :, 512 * h:512 * h + 512].rearrange("p a (m t) -> p a t m", t=4))
-            nc.vector.tensor_copy(
-                w1s_p[h].rearrange("p a (t m) -> p a t m", t=4),
-                w1s_raw[:, :, 512 * h:512 * h + 512].rearrange("p a (m t) -> p a t m", t=4))
 
         nc.vector.tensor_copy(v_w[0][:], tab[0][:].bitcast(U32).indirect(idx[:]))
         permute_w1(0)
+        w1s_p = tile("w1s_p", [P, 2, H], U8)
+        nc.vector.tensor_copy(w1s_p[:].rearrange("p a (h t m) -> p (a h) t m", h=2, t=4),
+                              w1s_raw[:].rearrange("p a (h m t) -> p (a h) t m", h=2, t=4))
+        v_w.append(tile("v_w1", [P, S], U32))
         nc.vector.tensor_copy(v_w[1][:], tab[1][:].bitcast(U32).indirect(idx[:]))
         permute_w1(1)
         pageA.append(tile("pageA2", [P, T2], F32))
@@ -93,22 +91,18 @@ def tile_list_antenna_hour_urgency_kernel(tc, tab_words, tab_scales, offs, offs2
         wgA_t = tile("wgA", [P, 4 * S + 16], F32, tag="wgA")
         wgA = wgA_t[:, 0:4 * S].rearrange("p (t j) -> p t j", t=4)
         bias = wgA_t[:, 4 * S:4 * S + 4]
-        w2_raw = tile("w2_raw", [P, 2, 4, R], F32, tag="big0")
-        w3_in = tile("w3_in", [P, H + H // 4], I32, tag="w3_raw")
-        w3_raw = w3_in[:, 0:H]
-        w3s_raw = w3_in[:, H:H + H // 4]
-        nc.gpsimd.memset(w3s_raw, 0)
+        w2_raw = tile("w2_raw", [P, 3, 4, R], F32, tag="big0")
         wg1_v = wg1.rearrange("(p t) j -> p t j", t=4)
         for q in (0, 2, 1, 3):
             nc.sync.dma_start(wgA[32 * q:32 * q + 32, 0, :], wg1_v[:, 0, :])
         for q in (0, 2, 1, 3):
             nc.sync.dma_start(wgA[32 * q:32 * q + 32, 1:4, :], wg1_v[:, 1:4, :])
-        for a in range(2):
-            nc.sync.dma_start(w2_raw[:, a], w2[512 * a:512 * a + 512].rearrange("(p j) m -> p j m", j=4))
+        w4_v = w4.rearrange("(a p j) n -> a p j n", a=2, j=4)
+        w2_v = w2.rearrange("(a p j) m -> a p j m", a=2, j=4)
+        nc.sync.dma_start(w2_raw[:, 0], w2_v[0])
+        nc.sync.dma_start(w2_raw[:, 2], w4_v[0])
+        nc.sync.dma_start(w2_raw[:, 1], w2_v[1])
         nc.sync.dma_start(bias, b2.rearrange("(p t) -> p t", t=4))
-        nc.sync.dma_start(w3_raw, w3_words[0].rearrange("p c i -> p (c i)").bitcast(I32))
-        for q in range(4):
-            nc.sync.dma_start(w3s_raw[32 * q:32 * q + 4], w3_scales[0, 4 * q:4 * q + 4, :].bitcast(I32))
 
         h1_acc = [bank(s, "acc_h1_%d" % s) for s in range(8)]
         h1 = [tile("h1_%d" % s, [P, S], F32) for s in range(7)]
@@ -118,16 +112,11 @@ def tile_list_antenna_hour_urgency_kernel(tc, tab_words, tab_scales, offs, offs2
             first, last = (0, 1) if s == 0 else (1, 0)
             for a in (first, last):
                 nc.tensor.matmul_mx(out=h1_acc[s][:], lhsT=w1_p[h][:, a, 256 * t:256 * t + 256].bitcast(FP4X4),
-                                    lhsT_scale=w1s_p[h][:, a, 128 * t:128 * t + 128],
+                                    lhsT_scale=w1s_p[:, a, 128 * s:128 * s + 128],
                                     rhs=v_w[a][:].bitcast(FP8X4), rhs_scale=v_s[:, a, :],
                                     start=(a == first), stop=(a == last))
             if s < 7:
                 nc.scalar.copy(h1[s][:], h1_acc[s][:])
-
-        l_raw = tile("l_raw", [P, 8, T2], F32, tag="big1")
-        least_v = least.rearrange("(a p t) c -> a t p c", a=2, t=4)
-        for s in range(4):
-            nc.sync.dma_start(l_raw[:, s, :], least_v[0, s])
 
         def scatter_a(s):
             nc.vector.tensor_tensor(pageA[s % A_PAGES][:].indirect(idx2[:]), h1[s][:], wgA[:, s % 4, :], MULT)
@@ -140,18 +129,32 @@ def tile_list_antenna_hour_urgency_kernel(tc, tab_words, tab_scales, offs, offs2
 
         for s in range(3):
             scatter_a(s)
-        pageA.append(tile("pageA3", [P, T2], F32, tag="h1_0"))
+        w3_in = tile("w3_in", [P, H + H // 4], I32, tag="h1_0")
+        w3_raw = w3_in[:, 0:H]
+        w3s_raw = w3_in[:, H:H + H // 4]
+        nc.gpsimd.memset(w3s_raw, 0)
+        nc.sync.dma_start(w3_raw, w3_words[0].rearrange("p c i -> p (c i)").bitcast(I32))
+        for q in range(4):
+            nc.sync.dma_start(w3s_raw[32 * q:32 * q + 4], w3_scales[0, 4 * q:4 * q + 4, :].bitcast(I32))
+
+        pageA.append(tile("pageA3", [P, T2], F32, tag="h1_1"))
         nc.gpsimd.memset(pageA[3][:], 0.0)
         scatter_a(3)
-        late = tile("late", [P, 12, S], F32, tag="h1_1")
+        l_raw = tile("l_raw", [P, 8, T2], F32, tag="big1")
+        late = tile("late", [P, 8, S], F32, tag="h1_2")
         wgB = late[:, 0:4, :]
-        w4_raw = [late[:, 4 + 4 * a:8 + 4 * a, :] for a in range(2)]
+        w4_raw = [w2_raw[:, 2], late[:, 4:8, :]]
+        least_v = least.rearrange("(a p t) c -> a t p c", a=2, t=4)
+        for s in range(3):
+            nc.sync.dma_start(l_raw[:, s, :], least_v[0, s])
         for q in (0, 2, 1, 3):
             nc.sync.dma_start(wgB[32 * q:32 * q + 32], wg2.rearrange("(p t) j -> p t j", t=4))
-        for a in range(2):
-            nc.sync.dma_start(w4_raw[a], w4[512 * a:512 * a + 512].rearrange("(p j) n -> p j n", j=4))
-        for s in range(4, 8):
-            nc.sync.dma_start(l_raw[:, s, :], least_v[1, s - 4])
+        nc.sync.dma_start(l_raw[:, 3, :], least_v[0, 3])
+        nc.sync.dma_start(w4_raw[1], w4_v[1])
+        nc.sync.dma_start(l_raw[:, 4, :], least_v[1, 0])
+        nc.sync.dma_start(l_raw[:, 5, :], least_v[1, 1])
+        nc.sync.dma_start(l_raw[:, 6, :], least_v[1, 2])
+        nc.sync.dma_start(l_raw[:, 7, :], least_v[1, 3])
 
         w2_q = tile("w2_q", [P, 2, R], U32)
         w2_s = tile("w2_s", [P, 2, R], U8)
@@ -170,8 +173,18 @@ def tile_list_antenna_hour_urgency_kernel(tc, tab_words, tab_scales, offs, offs2
         nc.vector.tensor_copy(w3s_p[:].rearrange("p (h t m) -> p h t m", h=2, t=4),
                               w3s_raw.bitcast(U8).rearrange("p (h m t) -> p h t m", h=2, t=4))
 
+        w4_q = tile("w4_q", [P, 2, N], U32)
+        w4_s = tile("w4_s", [P, 2, N], U8)
+
+        def quantise_w4(a):
+            w4_b = tile("w4_b%d" % a, [P, N, 4], BF16)
+            nc.scalar.copy(w4_b[:].rearrange("p (c i) j -> p c j i", i=4),
+                           w4_raw[a].rearrange("p j (c i) -> p c j i", i=4))
+            nc.vector.quantize_mx(out=w4_q[:, a, :].bitcast(FP8X4), scales=w4_s[:, a, :],
+                                  in_=w4_b[:].rearrange("p n j -> p (n j)"))
+
+        quantise_w4(0)
         z_pl = [tile("z_pl0", [P, 4, T2], BF16, tag="big0")]
-        l_b = [tile("l_b0", [P, 4, T2], BF16)]
 
         def plane(s):
             return z_pl[s // 4][:, s % 4, :]
@@ -180,14 +193,14 @@ def tile_list_antenna_hour_urgency_kernel(tc, tab_words, tab_scales, offs, offs2
             nc.scalar.copy(plane(s), pageA[s % A_PAGES][:])
 
         def max_least(s):
-            nc.scalar.copy(l_b[s // 4][:, s % 4, :], l_raw[:, s, :])
-            nc.vector.tensor_tensor(plane(s), plane(s), l_b[s // 4][:, s % 4, :], MAX)
+            l_b = tile("l_b%d" % s, [P, T2], BF16)
+            nc.scalar.copy(l_b[:], l_raw[:, s, :])
+            nc.vector.tensor_tensor(plane(s), plane(s), l_b[:], MAX)
 
         for s in range(3):
             round_a(s)
             scatter_a(s + A_PAGES)
-        for s in range(3):
-            max_least(s)
+        max_least(0)
 
         d_pl = tile("d_pl", [P, 4, S], BF16)
         d_b = tile("d_b", [P, S, 4], BF16)
@@ -207,7 +220,8 @@ def tile_list_antenna_hour_urgency_kernel(tc, tab_words, tab_scales, offs, offs2
         nc.scalar.copy(h1[7][:], h1_acc[7][:])
         round_a(3)
         scatter_a(7)
-        max_least(3)
+        max_least(1)
+        max_least(2)
         for s in range(8):
             acc = bank((s + 4) % 7 if s < 7 else 7, "acc_h2_%d" % s)
             nc.tensor.matmul_mx(out=acc[:], lhsT=w3_p[:, 128 * s:128 * s + 128].bitcast(FP8X4),
@@ -215,27 +229,17 @@ def tile_list_antenna_hour_urgency_kernel(tc, tab_words, tab_scales, offs, offs2
                                 rhs=d_q[:].bitcast(FP8X4), rhs_scale=d_s[:], start=True, stop=True)
             nc.scalar.copy(h2[s][:], acc[:])
         z_pl.append(tile("z_pl1", [P, 4, T2], BF16, tag="w3_p"))
-        l_b.append(tile("l_b1", [P, 4, T2], BF16, tag="d_s"))
         for s in range(B_PAGES):
             scatter_b(s)
 
-        w4_q = tile("w4_q", [P, 2, N], U32)
-        w4_s = tile("w4_s", [P, 2, N], U8)
         z_q = tile("z_q", [P, 2, T2], U32)
         z_s = [tile("z_s%d" % i, [P, CH], U8) for i in range(8)]
         o_acc = [bank(b, "acc_o_%d" % b) for b in range(8)]
-        o_sb = [tile("o_sb%d" % i, [P, 4, CH], F32, tag=("pageA0", "pageA1", "pageA2", "h1_0")[i]) for i in range(4)]
+        o_sb = [tile("o_sb%d" % i, [P, 4, CH], F32, tag=("pageA0", "pageA1", "pageA2", "h1_1")[i]) for i in range(4)]
         out_v = out.rearrange("(n p) c -> p n c", p=P)
 
-        def quantise_w4(a):
-            w4_b = tile("w4_b%d" % a, [P, N, 4], BF16, tag=("d_q", "w3s_p")[a])
-            nc.scalar.copy(w4_b[:].rearrange("p (c i) j -> p c j i", i=4),
-                           w4_raw[a].rearrange("p j (c i) -> p c j i", i=4))
-            nc.vector.quantize_mx(out=w4_q[:, a, :].bitcast(FP8X4), scales=w4_s[:, a, :],
-                                  in_=w4_b[:].rearrange("p n j -> p (n j)"))
-
         def max_b(s):
-            b_b = ring.tile([P, T2], BF16, name="b_b", tag="b_b")
+            b_b = tile("b_b%d" % s, [P, T2], BF16, tag="b_b%d" % (s % 2))
             nc.scalar.copy(b_b[:], page_b(s)[:])
             nc.vector.tensor_tensor(plane(s), plane(s), b_b[:], MAX)
             if s + B_PAGES < 7:
@@ -264,44 +268,50 @@ def tile_list_antenna_hour_urgency_kernel(tc, tab_words, tab_scales, offs, offs2
             cols = slice(CH * c, CH * c + CH)
             nc.vector.tensor_tensor(z_b[4 + c][:, :, 3], page_b(7)[:, cols], z_b[4 + c][:, :, 3], MAX)
 
+        max_least(3)
         max_b(0)
         round_a(4)
-        round_a(5)
-        max_least(4)
         max_b(1)
-        quantise_w4(0)
-        max_least(5)
-        max_b(2)
+        round_a(5)
         quantise_w4(1)
+        max_b(2)
         round_a(6)
+        max_least(4)
         max_b(3)
         round_a(7)
+        max_least(5)
+        max_b(4)
         max_least(6)
         weave(0, 0)
         finish(0, 0)
-        max_b(4)
-        max_least(7)
         weave(0, 1)
         finish(0, 1)
         max_b(5)
-        for c in (2, 3):
-            weave(0, c)
-            finish(0, c)
+        max_least(7)
+        weave(0, 2)
+        finish(0, 2)
+        weave(0, 3)
+        finish(0, 3)
         max_b(6)
         scatter_b(7)
-        for c in range(4):
+        for c in range(3):
             weave(1, c)
-        max_last(0)
+        late_cols = slice(3 * CH, 4 * CH)
+        nc.vector.tensor_tensor(z_pl[1][:, 3, late_cols], page_b(7)[:, late_cols], z_pl[1][:, 3, late_cols], MAX)
+        weave(1, 3)
         for c in range(4):
             cols = slice(CH * c, CH * c + CH)
             if c < 3:
-                max_last(c + 1)
+                max_last(c)
             finish(1, c)
             for k in range(2):
                 b = 2 * c + k
-                dst = o_sb[c][:, 2 * k:2 * k + 2, :].rearrange("p n c -> p (n c)")
+                dst = o_sb[c][:, 2 * k:2 * k + 2, :]
                 if b in (5, 7):
-                    nc.vector.tensor_copy(dst, o_acc[b][:])
+                    nc.vector.tensor_copy(dst.rearrange("p n c -> p (n c)"), o_acc[b][:])
                 else:
-                    nc.scalar.copy(dst, o_acc[b][:])
-            nc.sync.dma_start(out_v[:, :, cols], o_sb[c][:])
+                    nc.scalar.copy(dst.rearrange("p n c -> p (n c)"), o_acc[b][:])
+                if c < 2:
+                    nc.sync.dma_start(out_v[:, 2 * k:2 * k + 2, cols], dst)
+            if c >= 2:
+                nc.sync.dma_start(out_v[:, :, cols], o_sb[c][:])

@@ -38,53 +38,48 @@ def tile_list_antenna_hour_urgency_kernel(tc, tab_words, tab_scales, offs, offs2
         idx = tile("idx", [P, S // 16], U16)
         idx2 = tile("idx2", [P, S // 16], U16)
         idx3 = tile("idx3", [P, S // 16], U16)
-        tab = [tile("tab%d" % a, [P, T], I32, tag=("wgA", "big1")[a]) for a in range(2)]
-        tab_s = tile("tab_s", [P, 2, T], U8)
-        w1_raw = tile("w1_raw", [P, 2, 2 * H], U8, tag="pageA2")
-        w1s_raw = tile("w1s_raw", [P, 2, H], U8, tag="v_w1")
-        v_w = [tile("v_w0", [P, S], U32)]
-        v_g = tile("v_g", [P, 2, S], U8, tag="big0")
-        v_s = tile("v_s", [P, 2, S], U8)
-        w1_p = []
+        tab = [tile("tab%d" % a, [P, T], I32, tag=("wgA", "pageA2")[a]) for a in range(2)]
+        tab_s = tile("tab_s", [P, T], U8)
+        w1_raw = tile("w1_raw", [P, 2, 2 * H], U8, tag="big0")
+        w1s_raw = tile("w1s_raw", [P, H], U8)
+        v_w = [tile("v_w%d" % a, [P, S], U32) for a in range(2)]
+        v_g = tile("v_g", [P, S], U8)
+        scale = [tile("scale%d" % a, [P, S + H], U8) for a in range(2)]
+        v_s = [scale[a][:, 0:S] for a in range(2)]
+        w1s_p = [scale[a][:, S:S + H] for a in range(2)]
+        w1_p = [tile("w1_p%d" % h, [P, 2, 1024], U8, tag=("w1_p0", "big1")[h]) for h in range(2)]
 
         nc.sync.dma_start(idx[:], offs)
         nc.sync.dma_start(idx2[:], offs2)
         nc.sync.dma_start(idx3[:], offs3)
-        nc.sync.dma_start(tab_s[16:32].bitcast(I32), tab_scales.rearrange("a q c -> q a c").bitcast(I32))
+        nc.sync.dma_start(tab_s[0:32].bitcast(I32), tab_scales.rearrange("a q c -> (a q) c").bitcast(I32))
+        nc.sync.dma_start(w1s_raw[0:32].bitcast(I32), w1_scales.rearrange("a q c -> (a q) c").bitcast(I32))
         nc.sync.dma_start(tab[0][:], tab_words[0].rearrange("p t i -> p (t i)").bitcast(I32))
         nc.sync.dma_start(w1_raw[:].bitcast(I32), w1_words.rearrange("a p b -> p a b").bitcast(I32))
         nc.sync.dma_start(tab[1][:], tab_words[1].rearrange("p t i -> p (t i)").bitcast(I32))
 
         pageA = [tile("pageA%d" % i, [P, T2], F32) for i in range(2)]
-        nc.gpsimd.memset(pageA[0][:], 0.0)
-        nc.vector.memset(w1s_raw[:].bitcast(I32), 0)
-        for q in range(4):
-            (nc.gpsimd if q >= 1 else nc.scalar).dma_start(
-                w1s_raw[32 * q:32 * q + 4].bitcast(I32),
-                w1_scales[:, 4 * q:4 * q + 4, :].rearrange("a q c -> q a c").bitcast(I32))
-        for rows in (slice(0, 16), slice(32, 64), slice(64, 128)):
-            nc.vector.memset(tab_s[rows].bitcast(I32), 0)
-        nc.vector.memset(v_s[:].bitcast(I32), 0)
-        nc.gpsimd.memset(pageA[1][:], 0.0)
+        for raw in (tab_s, w1s_raw):
+            for rows in (slice(32, 64), slice(64, 128)):
+                nc.vector.memset(raw[rows].bitcast(I32), 0)
+        nc.vector.memset(scale[1][:].bitcast(I32), 0)
+        for page in pageA:
+            nc.gpsimd.memset(page[:], 0.0)
+        nc.vector.tensor_copy(v_g[:], tab_s[:].indirect(idx[:]))
+        nc.vector.tensor_copy(w1s_p[0].rearrange("p (h t m) -> p h t m", h=2, t=4),
+                              w1s_raw[:].rearrange("p (h m t) -> p h t m", h=2, t=4))
+        nc.vector.tensor_copy(v_s[0].bitcast(I32), v_g[:].bitcast(I32))
         for a in range(2):
-            nc.vector.tensor_copy(v_g[:, a, :], tab_s[:, a, :].indirect(idx[:]))
-        for q in range(4):
-            nc.scalar.dma_start(v_s[32 * q:32 * q + 4].bitcast(I32), v_g[16 + 4 * q:20 + 4 * q].bitcast(I32))
+            for q in range(1 - a, 4):
+                row = 16 * a + 4 * q
+                nc.scalar.dma_start(scale[a][32 * q:32 * q + 4].bitcast(I32), scale[0][row:row + 4].bitcast(I32))
 
-        def permute_w1(h):
-            w1_p.append(tile("w1_p%d" % h, [P, 2, 1024], U8, tag=("w1_p0", "big1")[h]))
+        nc.vector.tensor_copy(v_w[0][:], tab[0][:].bitcast(U32).indirect(idx[:]))
+        for h in range(2):
             nc.vector.tensor_copy(
                 w1_p[h][:].bitcast(U16).rearrange("p a (t m) -> p a t m", t=4),
                 w1_raw[:].bitcast(U16)[:, :, 512 * h:512 * h + 512].rearrange("p a (m t) -> p a t m", t=4))
-
-        nc.vector.tensor_copy(v_w[0][:], tab[0][:].bitcast(U32).indirect(idx[:]))
-        permute_w1(0)
-        w1s_p = tile("w1s_p", [P, 2, H], U8)
-        nc.vector.tensor_copy(w1s_p[:].rearrange("p a (h t m) -> p (a h) t m", h=2, t=4),
-                              w1s_raw[:].rearrange("p a (h m t) -> p (a h) t m", h=2, t=4))
-        v_w.append(tile("v_w1", [P, S], U32))
         nc.vector.tensor_copy(v_w[1][:], tab[1][:].bitcast(U32).indirect(idx[:]))
-        permute_w1(1)
         pageA.append(tile("pageA2", [P, T2], F32))
         nc.gpsimd.memset(pageA[2][:], 0.0)
 
@@ -94,7 +89,7 @@ def tile_list_antenna_hour_urgency_kernel(tc, tab_words, tab_scales, offs, offs2
         w2_raw = tile("w2_raw", [P, 3, 4, R], F32, tag="big0")
         wg1_v = wg1.rearrange("(p t) j -> p t j", t=4)
         for q in (0, 2, 1, 3):
-            nc.sync.dma_start(wgA[32 * q:32 * q + 32, 0, :], wg1_v[:, 0, :])
+            (nc.sync if q < 2 else nc.scalar).dma_start(wgA[32 * q:32 * q + 32, 0, :], wg1_v[:, 0, :])
         for q in (0, 2, 1, 3):
             nc.sync.dma_start(wgA[32 * q:32 * q + 32, 1:4, :], wg1_v[:, 1:4, :])
         w4_v = w4.rearrange("(a p j) n -> a p j n", a=2, j=4)
@@ -112,8 +107,8 @@ def tile_list_antenna_hour_urgency_kernel(tc, tab_words, tab_scales, offs, offs2
             first, last = (0, 1) if s == 0 else (1, 0)
             for a in (first, last):
                 nc.tensor.matmul_mx(out=h1_acc[s][:], lhsT=w1_p[h][:, a, 256 * t:256 * t + 256].bitcast(FP4X4),
-                                    lhsT_scale=w1s_p[:, a, 128 * s:128 * s + 128],
-                                    rhs=v_w[a][:].bitcast(FP8X4), rhs_scale=v_s[:, a, :],
+                                    lhsT_scale=w1s_p[a][:, 128 * s:128 * s + 128],
+                                    rhs=v_w[a][:].bitcast(FP8X4), rhs_scale=v_s[a],
                                     start=(a == first), stop=(a == last))
             if s < 7:
                 nc.scalar.copy(h1[s][:], h1_acc[s][:])
@@ -211,7 +206,7 @@ def tile_list_antenna_hour_urgency_kernel(tc, tab_words, tab_scales, offs, offs2
             for a in range(2):
                 nc.tensor.matmul_mx(out=acc[:], lhsT=w2_q[:, a, 128 * t:128 * t + 128].bitcast(FP8X4),
                                     lhsT_scale=w2_s[:, a, 128 * t:128 * t + 128],
-                                    rhs=v_w[a][:].bitcast(FP8X4), rhs_scale=v_s[:, a, :], start=(a == 0), stop=(a == 1))
+                                    rhs=v_w[a][:].bitcast(FP8X4), rhs_scale=v_s[a], start=(a == 0), stop=(a == 1))
             nc.scalar.activation(d_pl[:, t, :], acc[:], RELU, bias=bias[:, t:t + 1])
         nc.scalar.copy(d_b[:].rearrange("p (c i) t -> p c t i", i=4), d_pl[:].rearrange("p t (c i) -> p c t i", i=4))
         nc.vector.quantize_mx(out=d_q[:].bitcast(FP8X4), scales=d_s[:], in_=d_b[:].rearrange("p j t -> p (j t)"))

@@ -18,8 +18,14 @@ MAX = mybir.AluOpType.max
 RELU = mybir.ActivationFunctionType.Relu
 
 P = 128
-CH = 256
-A_PAGES, B_PAGES = 4, 2
+PACK = 4
+SLICES = H // P
+LAST = SLICES - 1
+CHUNK = 256
+CHUNKS = T2 // CHUNK
+A_PAGES = 4
+B_PAGES = 2
+QUADRANTS = (0, 2, 1, 3)
 
 
 def tile_list_antenna_hour_urgency_kernel(tc, tab_words, tab_scales, offs, offs2, offs3, w1_words,
@@ -40,14 +46,14 @@ def tile_list_antenna_hour_urgency_kernel(tc, tab_words, tab_scales, offs, offs2
         idx3 = tile("idx3", [P, S // 16], U16)
         tab = [tile("tab%d" % a, [P, T], I32, tag=("wgA", "pageA2")[a]) for a in range(2)]
         tab_s = tile("tab_s", [P, T], U8)
-        w1_raw = tile("w1_raw", [P, 2, 2 * H], U8, tag="big0")
+        w1_raw = tile("w1_raw", [P, 2, 2 * H], U8, tag="w2_raw")
         w1s_raw = tile("w1s_raw", [P, H], U8)
         v_w = [tile("v_w%d" % a, [P, S], U32) for a in range(2)]
         v_g = tile("v_g", [P, S], U8)
         scale = [tile("scale%d" % a, [P, S + H], U8) for a in range(2)]
         v_s = [scale[a][:, 0:S] for a in range(2)]
         w1s_p = [scale[a][:, S:S + H] for a in range(2)]
-        w1_p = [tile("w1_p%d" % h, [P, 2, 1024], U8, tag=("w1_p0", "big1")[h]) for h in range(2)]
+        w1_p = [tile("w1_p%d" % h, [P, 2, 1024], U8, tag=("w4_raw0", "l_raw")[h]) for h in range(2)]
 
         nc.sync.dma_start(idx[:], offs)
         nc.sync.dma_start(idx2[:], offs2)
@@ -65,9 +71,10 @@ def tile_list_antenna_hour_urgency_kernel(tc, tab_words, tab_scales, offs, offs2
         nc.vector.memset(scale[1][:].bitcast(I32), 0)
         for page in pageA:
             nc.gpsimd.memset(page[:], 0.0)
+
         nc.vector.tensor_copy(v_g[:], tab_s[:].indirect(idx[:]))
-        nc.vector.tensor_copy(w1s_p[0].rearrange("p (h t m) -> p h t m", h=2, t=4),
-                              w1s_raw[:].rearrange("p (h m t) -> p h t m", h=2, t=4))
+        nc.vector.tensor_copy(w1s_p[0].rearrange("p (h t m) -> p h t m", h=2, t=PACK),
+                              w1s_raw[:].rearrange("p (h m t) -> p h t m", h=2, t=PACK))
         nc.vector.tensor_copy(v_s[0].bitcast(I32), v_g[:].bitcast(I32))
         for a in range(2):
             for q in range(1 - a, 4):
@@ -77,53 +84,56 @@ def tile_list_antenna_hour_urgency_kernel(tc, tab_words, tab_scales, offs, offs2
         nc.vector.tensor_copy(v_w[0][:], tab[0][:].bitcast(U32).indirect(idx[:]))
         for h in range(2):
             nc.vector.tensor_copy(
-                w1_p[h][:].bitcast(U16).rearrange("p a (t m) -> p a t m", t=4),
-                w1_raw[:].bitcast(U16)[:, :, 512 * h:512 * h + 512].rearrange("p a (m t) -> p a t m", t=4))
+                w1_p[h][:].bitcast(U16).rearrange("p a (t m) -> p a t m", t=PACK),
+                w1_raw[:].bitcast(U16)[:, :, 512 * h:512 * h + 512].rearrange("p a (m t) -> p a t m", t=PACK))
         nc.vector.tensor_copy(v_w[1][:], tab[1][:].bitcast(U32).indirect(idx[:]))
         pageA.append(tile("pageA2", [P, T2], F32))
         nc.gpsimd.memset(pageA[2][:], 0.0)
 
-        wgA_t = tile("wgA", [P, 4 * S + 16], F32, tag="wgA")
-        wgA = wgA_t[:, 0:4 * S].rearrange("p (t j) -> p t j", t=4)
-        bias = wgA_t[:, 4 * S:4 * S + 4]
-        w2_raw = tile("w2_raw", [P, 3, 4, R], F32, tag="big0")
-        wg1_v = wg1.rearrange("(p t) j -> p t j", t=4)
-        for q in (0, 2, 1, 3):
+        wgA_bias = tile("wgA", [P, PACK * S + 16], F32)
+        wgA = wgA_bias[:, 0:PACK * S].rearrange("p (t j) -> p t j", t=PACK)
+        bias = wgA_bias[:, PACK * S:PACK * S + PACK]
+        w2_raw = tile("w2_raw", [P, 2, PACK, R], F32)
+        wg1_v = wg1.rearrange("(p t) j -> p t j", t=PACK)
+        for q in QUADRANTS:
             (nc.sync if q < 2 else nc.scalar).dma_start(wgA[32 * q:32 * q + 32, 0, :], wg1_v[:, 0, :])
-        for q in (0, 2, 1, 3):
-            nc.sync.dma_start(wgA[32 * q:32 * q + 32, 1:4, :], wg1_v[:, 1:4, :])
-        w4_v = w4.rearrange("(a p j) n -> a p j n", a=2, j=4)
-        w2_v = w2.rearrange("(a p j) m -> a p j m", a=2, j=4)
-        nc.sync.dma_start(w2_raw[:, 0], w2_v[0])
-        nc.sync.dma_start(w2_raw[:, 2], w4_v[0])
-        nc.sync.dma_start(w2_raw[:, 1], w2_v[1])
-        nc.sync.dma_start(bias, b2.rearrange("(p t) -> p t", t=4))
+        for q in QUADRANTS:
+            nc.sync.dma_start(wgA[32 * q:32 * q + 32, 1:PACK, :], wg1_v[:, 1:PACK, :])
+        w2_v = w2.rearrange("(a p j) m -> a p j m", a=2, j=PACK)
+        w4_v = w4.rearrange("(a p j) n -> a p j n", a=2, j=PACK)
+        for a in range(2):
+            nc.sync.dma_start(w2_raw[:, a], w2_v[a])
+        nc.sync.dma_start(bias, b2.rearrange("(p t) -> p t", t=PACK))
 
-        h1_acc = [bank(s, "acc_h1_%d" % s) for s in range(8)]
-        h1 = [tile("h1_%d" % s, [P, S], F32) for s in range(7)]
-        h2 = [tile("h2_%d" % s, [P, S], F32) for s in range(8)]
-        for s in range(8):
-            h, t = divmod(s, 4)
-            first, last = (0, 1) if s == 0 else (1, 0)
-            for a in (first, last):
+        h1_acc = [bank(s, "acc_h1_%d" % s) for s in range(SLICES)]
+        h1 = [tile("h1_%d" % s, [P, S], F32) for s in range(LAST)]
+        h2 = [tile("h2_%d" % s, [P, S], F32) for s in range(SLICES)]
+        for s in range(SLICES):
+            h, t = divmod(s, PACK)
+            first, second = (0, 1) if s == 0 else (1, 0)
+            for a in (first, second):
                 nc.tensor.matmul_mx(out=h1_acc[s][:], lhsT=w1_p[h][:, a, 256 * t:256 * t + 256].bitcast(FP4X4),
-                                    lhsT_scale=w1s_p[a][:, 128 * s:128 * s + 128],
+                                    lhsT_scale=w1s_p[a][:, P * s:P * s + P],
                                     rhs=v_w[a][:].bitcast(FP8X4), rhs_scale=v_s[a],
-                                    start=(a == first), stop=(a == last))
-            if s < 7:
+                                    start=(a == first), stop=(a == second))
+            if s < LAST:
                 nc.scalar.copy(h1[s][:], h1_acc[s][:])
 
+        w4_raw0 = tile("w4_raw0", [P, PACK, N], F32)
+        nc.sync.dma_start(w4_raw0[:], w4_v[0])
+
         def scatter_a(s):
-            nc.vector.tensor_tensor(pageA[s % A_PAGES][:].indirect(idx2[:]), h1[s][:], wgA[:, s % 4, :], MULT)
+            nc.vector.tensor_tensor(pageA[s % A_PAGES][:].indirect(idx2[:]), h1[s][:], wgA[:, s % PACK, :], MULT)
 
         def page_b(s):
-            return pageB[min(s, 6) % B_PAGES]
+            return pageB[min(s, LAST - 1) % B_PAGES]
 
         def scatter_b(s):
-            nc.vector.tensor_tensor(page_b(s)[:].indirect(idx3[:]), h2[s][:], wgB[:, s % 4, :], MULT)
+            nc.vector.tensor_tensor(page_b(s)[:].indirect(idx3[:]), h2[s][:], wgB[:, s % PACK, :], MULT)
 
-        for s in range(3):
+        for s in range(A_PAGES - 1):
             scatter_a(s)
+
         w3_in = tile("w3_in", [P, H + H // 4], I32, tag="h1_0")
         w3_raw = w3_in[:, 0:H]
         w3s_raw = w3_in[:, H:H + H // 4]
@@ -134,179 +144,166 @@ def tile_list_antenna_hour_urgency_kernel(tc, tab_words, tab_scales, offs, offs2
 
         pageA.append(tile("pageA3", [P, T2], F32, tag="h1_1"))
         nc.gpsimd.memset(pageA[3][:], 0.0)
-        scatter_a(3)
-        l_raw = tile("l_raw", [P, 8, T2], F32, tag="big1")
-        late = tile("late", [P, 8, S], F32, tag="h1_2")
-        wgB = late[:, 0:4, :]
-        w4_raw = [w2_raw[:, 2], late[:, 4:8, :]]
-        least_v = least.rearrange("(a p t) c -> a t p c", a=2, t=4)
-        for s in range(3):
+        scatter_a(A_PAGES - 1)
+
+        l_raw = tile("l_raw", [P, SLICES, T2], F32)
+        wgB_w4 = tile("wgB_w4", [P, 2 * PACK, S], F32, tag="h1_2")
+        wgB = wgB_w4[:, 0:PACK, :]
+        w4_raw = [w4_raw0[:], wgB_w4[:, PACK:2 * PACK, :]]
+        least_v = least.rearrange("(a p t) c -> a t p c", a=2, t=PACK)
+        early = 3
+        for s in range(early):
             nc.sync.dma_start(l_raw[:, s, :], least_v[0, s])
-        for q in (0, 2, 1, 3):
-            nc.sync.dma_start(wgB[32 * q:32 * q + 32], wg2.rearrange("(p t) j -> p t j", t=4))
-        nc.sync.dma_start(l_raw[:, 3, :], least_v[0, 3])
+        for q in QUADRANTS:
+            nc.sync.dma_start(wgB[32 * q:32 * q + 32], wg2.rearrange("(p t) j -> p t j", t=PACK))
+        for s in range(early, SLICES):
+            nc.sync.dma_start(l_raw[:, s, :], least_v[s // PACK, s % PACK])
         nc.sync.dma_start(w4_raw[1], w4_v[1])
-        nc.sync.dma_start(l_raw[:, 4, :], least_v[1, 0])
-        nc.sync.dma_start(l_raw[:, 5, :], least_v[1, 1])
-        nc.sync.dma_start(l_raw[:, 6, :], least_v[1, 2])
-        nc.sync.dma_start(l_raw[:, 7, :], least_v[1, 3])
 
         w2_q = tile("w2_q", [P, 2, R], U32)
         w2_s = tile("w2_s", [P, 2, R], U8)
         for a in range(2):
-            w2_b = tile("w2_b%d" % a, [P, 4 * R], BF16, tag="wb%d" % a)
-            nc.scalar.copy(w2_b[:].rearrange("p (t m j) -> p m t j", t=4, j=4),
-                           w2_raw[:, a].rearrange("p j (m t) -> p m t j", t=4))
+            w2_b = tile("w2_b%d" % a, [P, PACK * R], BF16)
+            nc.scalar.copy(w2_b[:].rearrange("p (t m j) -> p m t j", t=PACK, j=PACK),
+                           w2_raw[:, a].rearrange("p j (m t) -> p m t j", t=PACK))
             nc.vector.quantize_mx(out=w2_q[:, a, :].bitcast(FP8X4), scales=w2_s[:, a, :], in_=w2_b[:])
-        pageB = [tile("pageB%d" % i, [P, T2], F32, tag="wb%d" % i) for i in range(B_PAGES)]
-        for page in pageB:
-            nc.gpsimd.memset(page[:], 0.0)
+
         w3_p = tile("w3_p", [P, H], I32)
-        nc.vector.tensor_copy(w3_p[:].rearrange("p (h t u i) -> p h u t i", h=2, t=4, i=4),
-                              w3_raw.rearrange("p (h u i t) -> p h u t i", h=2, t=4, i=4))
+        nc.vector.tensor_copy(w3_p[:].rearrange("p (h t u i) -> p h u t i", h=2, t=PACK, i=4),
+                              w3_raw.rearrange("p (h u i t) -> p h u t i", h=2, t=PACK, i=4))
         w3s_p = tile("w3s_p", [P, H], U8)
-        nc.vector.tensor_copy(w3s_p[:].rearrange("p (h t m) -> p h t m", h=2, t=4),
-                              w3s_raw.bitcast(U8).rearrange("p (h m t) -> p h t m", h=2, t=4))
+        nc.vector.tensor_copy(w3s_p[:].rearrange("p (h t m) -> p h t m", h=2, t=PACK),
+                              w3s_raw.bitcast(U8).rearrange("p (h m t) -> p h t m", h=2, t=PACK))
 
         w4_q = tile("w4_q", [P, 2, N], U32)
         w4_s = tile("w4_s", [P, 2, N], U8)
 
+        def weave(dst, src):
+            nc.scalar.copy(dst.rearrange("p (c n) i -> p c i n", n=4), src.rearrange("p i (c n) -> p c i n", n=4))
+
         def quantise_w4(a):
-            w4_b = tile("w4_b%d" % a, [P, N, 4], BF16)
-            nc.scalar.copy(w4_b[:].rearrange("p (c i) j -> p c j i", i=4),
-                           w4_raw[a].rearrange("p j (c i) -> p c j i", i=4))
+            w4_b = tile("w4_b%d" % a, [P, N, PACK], BF16)
+            weave(w4_b[:], w4_raw[a])
             nc.vector.quantize_mx(out=w4_q[:, a, :].bitcast(FP8X4), scales=w4_s[:, a, :],
                                   in_=w4_b[:].rearrange("p n j -> p (n j)"))
 
-        quantise_w4(0)
-        z_pl = [tile("z_pl0", [P, 4, T2], BF16, tag="big0")]
+        z_rows = [tile("z_rows0", [P, PACK, T2], BF16, tag="w2_raw")]
 
-        def plane(s):
-            return z_pl[s // 4][:, s % 4, :]
+        def z_slice(s):
+            return z_rows[s // PACK][:, s % PACK, :]
 
         def round_a(s):
-            nc.scalar.copy(plane(s), pageA[s % A_PAGES][:])
+            nc.scalar.copy(z_slice(s), pageA[s % A_PAGES][:])
 
         def max_least(s):
             l_b = tile("l_b%d" % s, [P, T2], BF16)
             nc.scalar.copy(l_b[:], l_raw[:, s, :])
-            nc.vector.tensor_tensor(plane(s), plane(s), l_b[:], MAX)
+            nc.vector.tensor_tensor(z_slice(s), z_slice(s), l_b[:], MAX)
 
-        for s in range(3):
+        for s in range(LAST - A_PAGES):
             round_a(s)
             scatter_a(s + A_PAGES)
-        max_least(0)
+        pageB = [tile("pageB%d" % i, [P, T2], F32, tag="h1_%d" % (A_PAGES + i)) for i in range(B_PAGES)]
+        for page in pageB:
+            nc.gpsimd.memset(page[:], 0.0)
+        quantise_w4(0)
 
-        d_pl = tile("d_pl", [P, 4, S], BF16)
-        d_b = tile("d_b", [P, S, 4], BF16)
+        d_rows = tile("d_rows", [P, PACK, S], BF16)
+        d_b = tile("d_b", [P, S, PACK], BF16)
         d_q = tile("d_q", [P, S], U32)
         d_s = tile("d_s", [P, S], U8)
-        for t in range(4):
+        for t in range(PACK):
             acc = bank(t, "acc_d_%d" % t)
             for a in range(2):
-                nc.tensor.matmul_mx(out=acc[:], lhsT=w2_q[:, a, 128 * t:128 * t + 128].bitcast(FP8X4),
-                                    lhsT_scale=w2_s[:, a, 128 * t:128 * t + 128],
+                nc.tensor.matmul_mx(out=acc[:], lhsT=w2_q[:, a, P * t:P * t + P].bitcast(FP8X4),
+                                    lhsT_scale=w2_s[:, a, P * t:P * t + P],
                                     rhs=v_w[a][:].bitcast(FP8X4), rhs_scale=v_s[a], start=(a == 0), stop=(a == 1))
-            nc.scalar.activation(d_pl[:, t, :], acc[:], RELU, bias=bias[:, t:t + 1])
-        nc.scalar.copy(d_b[:].rearrange("p (c i) t -> p c t i", i=4), d_pl[:].rearrange("p t (c i) -> p c t i", i=4))
+            nc.scalar.activation(d_rows[:, t, :], acc[:], RELU, bias=bias[:, t:t + 1])
+        weave(d_b[:], d_rows[:])
         nc.vector.quantize_mx(out=d_q[:].bitcast(FP8X4), scales=d_s[:], in_=d_b[:].rearrange("p j t -> p (j t)"))
 
-        h1.append(tile("h1_7", [P, S], F32, tag="d_pl"))
-        nc.scalar.copy(h1[7][:], h1_acc[7][:])
-        round_a(3)
-        scatter_a(7)
-        max_least(1)
-        max_least(2)
-        for s in range(8):
-            acc = bank((s + 4) % 7 if s < 7 else 7, "acc_h2_%d" % s)
-            nc.tensor.matmul_mx(out=acc[:], lhsT=w3_p[:, 128 * s:128 * s + 128].bitcast(FP8X4),
-                                lhsT_scale=w3s_p[:, 128 * s:128 * s + 128],
+        h1.append(tile("h1_last", [P, S], F32, tag="d_rows"))
+        nc.scalar.copy(h1[LAST][:], h1_acc[LAST][:])
+        round_a(LAST - A_PAGES)
+        scatter_a(LAST)
+        for s in range(early):
+            max_least(s)
+
+        for s in range(SLICES):
+            acc = bank((s + PACK) % LAST if s < LAST else LAST, "acc_h2_%d" % s)
+            nc.tensor.matmul_mx(out=acc[:], lhsT=w3_p[:, P * s:P * s + P].bitcast(FP8X4),
+                                lhsT_scale=w3s_p[:, P * s:P * s + P],
                                 rhs=d_q[:].bitcast(FP8X4), rhs_scale=d_s[:], start=True, stop=True)
             nc.scalar.copy(h2[s][:], acc[:])
-        z_pl.append(tile("z_pl1", [P, 4, T2], BF16, tag="w3_p"))
+        z_rows.append(tile("z_rows1", [P, PACK, T2], BF16, tag="w3_p"))
         for s in range(B_PAGES):
             scatter_b(s)
 
+        z_b = [[tile("z_b%d_%d" % (a, c), [P, CHUNK, PACK], BF16) for c in range(CHUNKS)] for a in range(2)]
         z_q = tile("z_q", [P, 2, T2], U32)
-        z_s = [tile("z_s%d" % i, [P, CH], U8) for i in range(8)]
-        o_acc = [bank(b, "acc_o_%d" % b) for b in range(8)]
-        o_sb = [tile("o_sb%d" % i, [P, 4, CH], F32, tag=("pageA0", "pageA1", "pageA2", "h1_1")[i]) for i in range(4)]
+        z_s = [[tile("z_s%d_%d" % (a, c), [P, CHUNK], U8) for c in range(CHUNKS)] for a in range(2)]
+        o_acc = [bank(b, "acc_o_%d" % b) for b in range(2 * CHUNKS)]
+        o_tags = ("pageA0", "pageA1", "pageA2", "h1_1")
+        o_sb = [tile("o_sb%d" % c, [P, N // P, CHUNK], F32, tag=o_tags[c]) for c in range(CHUNKS)]
         out_v = out.rearrange("(n p) c -> p n c", p=P)
+
+        def chunk(c):
+            return slice(CHUNK * c, CHUNK * c + CHUNK)
 
         def max_b(s):
             b_b = tile("b_b%d" % s, [P, T2], BF16, tag="b_b%d" % (s % 2))
             nc.scalar.copy(b_b[:], page_b(s)[:])
-            nc.vector.tensor_tensor(plane(s), plane(s), b_b[:], MAX)
-            if s + B_PAGES < 7:
+            nc.vector.tensor_tensor(z_slice(s), z_slice(s), b_b[:], MAX)
+            if s + B_PAGES < LAST:
                 scatter_b(s + B_PAGES)
 
-        z_b = [tile("z_b%d" % i, [P, CH, 4], BF16) for i in range(8)]
+        def weave_z(a, c):
+            weave(z_b[a][c][:], z_rows[a][:, :, chunk(c)])
 
-        def weave(a, c):
-            cols = slice(CH * c, CH * c + CH)
-            nc.scalar.copy(z_b[4 * a + c][:].rearrange("p (c i) t -> p c t i", i=4),
-                           z_pl[a][:, :, cols].rearrange("p t (c i) -> p c t i", i=4))
+        def multiply_z(a, c):
+            nc.vector.quantize_mx(out=z_q[:, a, chunk(c)].bitcast(FP8X4), scales=z_s[a][c][:],
+                                  in_=z_b[a][c][:].rearrange("p c t -> p (c t)"))
+            for n in range(N // P):
+                k, half = divmod(n, 2)
+                nc.tensor.matmul_mx(out=o_acc[2 * c + k][:, CHUNK * half:CHUNK * half + CHUNK],
+                                    lhsT=w4_q[:, a, P * n:P * n + P].bitcast(FP8X4),
+                                    lhsT_scale=w4_s[:, a, P * n:P * n + P],
+                                    rhs=z_q[:, a, chunk(c)].bitcast(FP8X4), rhs_scale=z_s[a][c][:],
+                                    start=(a == 0 and half == 0), stop=(a == 1 and half == 1))
 
-        def finish(a, c):
-            cols = slice(CH * c, CH * c + CH)
-            nc.vector.quantize_mx(out=z_q[:, a, cols].bitcast(FP8X4), scales=z_s[4 * a + c][:],
-                                  in_=z_b[4 * a + c][:].rearrange("p c t -> p (c t)"))
-            for n in range(4):
-                acc = o_acc[2 * c + n // 2]
-                nc.tensor.matmul_mx(out=acc[:, CH * (n % 2):CH * (n % 2) + CH],
-                                    lhsT=w4_q[:, a, 128 * n:128 * n + 128].bitcast(FP8X4),
-                                    lhsT_scale=w4_s[:, a, 128 * n:128 * n + 128],
-                                    rhs=z_q[:, a, cols].bitcast(FP8X4), rhs_scale=z_s[4 * a + c][:],
-                                    start=(a == 0 and n % 2 == 0), stop=(a == 1 and n % 2 == 1))
-
-        def max_last(c):
-            cols = slice(CH * c, CH * c + CH)
-            nc.vector.tensor_tensor(z_b[4 + c][:, :, 3], page_b(7)[:, cols], z_b[4 + c][:, :, 3], MAX)
-
-        max_least(3)
-        max_b(0)
-        round_a(4)
-        max_b(1)
-        round_a(5)
+        max_least(early)
+        for s in range(PACK):
+            max_b(s)
+            round_a(PACK + s)
+            max_least(PACK + s)
+        max_b(LAST - 3)
+        for c in range(CHUNKS):
+            weave_z(0, c)
+            multiply_z(0, c)
+        max_b(LAST - 2)
         quantise_w4(1)
-        max_b(2)
-        round_a(6)
-        max_least(4)
-        max_b(3)
-        round_a(7)
-        max_least(5)
-        max_b(4)
-        max_least(6)
-        weave(0, 0)
-        finish(0, 0)
-        weave(0, 1)
-        finish(0, 1)
-        max_b(5)
-        max_least(7)
-        weave(0, 2)
-        finish(0, 2)
-        weave(0, 3)
-        finish(0, 3)
-        max_b(6)
-        scatter_b(7)
-        for c in range(3):
-            weave(1, c)
-        late_cols = slice(3 * CH, 4 * CH)
-        nc.vector.tensor_tensor(z_pl[1][:, 3, late_cols], page_b(7)[:, late_cols], z_pl[1][:, 3, late_cols], MAX)
-        weave(1, 3)
-        for c in range(4):
-            cols = slice(CH * c, CH * c + CH)
-            if c < 3:
-                max_last(c)
-            finish(1, c)
+        max_b(LAST - 1)
+        scatter_b(LAST)
+
+        end = CHUNKS - 1
+        for c in range(end):
+            weave_z(1, c)
+        nc.vector.tensor_tensor(z_slice(LAST)[:, chunk(end)], page_b(LAST)[:, chunk(end)],
+                                z_slice(LAST)[:, chunk(end)], MAX)
+        weave_z(1, end)
+        for c in range(CHUNKS):
+            if c < end:
+                woven = z_b[1][c][:, :, PACK - 1]
+                nc.vector.tensor_tensor(woven, page_b(LAST)[:, chunk(c)], woven, MAX)
+            multiply_z(1, c)
+            shared = c >= CHUNKS // 2
             for k in range(2):
-                b = 2 * c + k
                 dst = o_sb[c][:, 2 * k:2 * k + 2, :]
-                if b in (5, 7):
-                    nc.vector.tensor_copy(dst.rearrange("p n c -> p (n c)"), o_acc[b][:])
+                if shared and k == 1:
+                    nc.vector.tensor_copy(dst.rearrange("p n c -> p (n c)"), o_acc[2 * c + k][:])
                 else:
-                    nc.scalar.copy(dst.rearrange("p n c -> p (n c)"), o_acc[b][:])
-                if c < 2:
-                    nc.sync.dma_start(out_v[:, 2 * k:2 * k + 2, cols], dst)
-            if c >= 2:
-                nc.sync.dma_start(out_v[:, :, cols], o_sb[c][:])
+                    nc.scalar.copy(dst.rearrange("p n c -> p (n c)"), o_acc[2 * c + k][:])
+                if not shared:
+                    nc.sync.dma_start(out_v[:, 2 * k:2 * k + 2, chunk(c)], dst)
+            if shared:
+                nc.sync.dma_start(out_v[:, :, chunk(c)], o_sb[c][:])

@@ -22,7 +22,10 @@ PACK = 4
 SLICES = H // P
 LAST = SLICES - 1
 CHUNK = 256
-CHUNKS = T2 // CHUNK
+WIDTHS = (128, 256, 128, 256, 256)
+CUT = 384
+FIRST = (0, 1)
+STARTS = (0, 128, 384, 512, 768)
 A_PAGES = 4
 B_PAGES = 2
 QUADRANTS = (0, 2, 1, 3)
@@ -44,7 +47,7 @@ def tile_list_antenna_hour_urgency_kernel(tc, tab_words, tab_scales, offs, offs2
         idx = tile("idx", [P, S // 16], U16)
         idx2 = tile("idx2", [P, S // 16], U16)
         idx3 = tile("idx3", [P, S // 16], U16)
-        tab = [tile("tab%d" % a, [P, T], I32, tag=("wgA", "pageA2")[a]) for a in range(2)]
+        tab = [tile("tab%d" % a, [P, T], I32, tag=("w3_p", "pageA2")[a]) for a in range(2)]
         tab_s = tile("tab_s", [P, T], U8)
         w1_raw = tile("w1_raw", [P, 2, 2 * H], U8, tag="w2_raw")
         w1s_raw = tile("w1s_raw", [P, H], U8)
@@ -56,21 +59,23 @@ def tile_list_antenna_hour_urgency_kernel(tc, tab_words, tab_scales, offs, offs2
         w1_p = [tile("w1_p%d" % h, [P, 2, 1024], U8, tag=("w4_raw0", "l_raw")[h]) for h in range(2)]
 
         nc.sync.dma_start(idx[:], offs)
-        nc.sync.dma_start(idx2[:], offs2)
-        nc.sync.dma_start(idx3[:], offs3)
         nc.sync.dma_start(tab_s[0:32].bitcast(I32), tab_scales.rearrange("a q c -> (a q) c").bitcast(I32))
         nc.sync.dma_start(w1s_raw[0:32].bitcast(I32), w1_scales.rearrange("a q c -> (a q) c").bitcast(I32))
+        nc.gpsimd.memset(w1s_raw[32:64].bitcast(I32), 0)
+        nc.sync.dma_start(w1s_raw[48:64].bitcast(I32), w3_scales[0].bitcast(I32))
         nc.sync.dma_start(tab[0][:], tab_words[0].rearrange("p t i -> p (t i)").bitcast(I32))
         nc.sync.dma_start(w1_raw[:].bitcast(I32), w1_words.rearrange("a p b -> p a b").bitcast(I32))
+        nc.sync.dma_start(idx2[:], offs2)
         nc.sync.dma_start(tab[1][:], tab_words[1].rearrange("p t i -> p (t i)").bitcast(I32))
 
-        pageA = [tile("pageA%d" % i, [P, T2], F32) for i in range(2)]
-        for raw in (tab_s, w1s_raw):
-            for rows in (slice(32, 64), slice(64, 128)):
-                nc.vector.memset(raw[rows].bitcast(I32), 0)
+        pageA = [tile("pageA0", [P, T2], F32)]
+        for raw, rows in ((tab_s, slice(32, 64)), (tab_s, slice(64, 128)), (w1s_raw, slice(64, 128))):
+            nc.vector.memset(raw[rows].bitcast(I32), 0)
         nc.vector.memset(scale[1][:].bitcast(I32), 0)
         for page in pageA:
             nc.gpsimd.memset(page[:], 0.0)
+        warm = tile("warm", [P, 16], F32)
+        nc.scalar.copy(warm[:, 0:1], pageA[0][:, 0:1])
 
         nc.vector.tensor_copy(v_g[:], tab_s[:].indirect(idx[:]))
         nc.vector.tensor_copy(w1s_p[0].rearrange("p (h t m) -> p h t m", h=2, t=PACK),
@@ -81,12 +86,17 @@ def tile_list_antenna_hour_urgency_kernel(tc, tab_words, tab_scales, offs, offs2
                 row = 16 * a + 4 * q
                 nc.scalar.dma_start(scale[a][32 * q:32 * q + 4].bitcast(I32), scale[0][row:row + 4].bitcast(I32))
 
+        pageA.append(tile("pageA1", [P, T2], F32, tag="v_g"))
+        nc.gpsimd.memset(pageA[1][:], 0.0)
+
         nc.vector.tensor_copy(v_w[0][:], tab[0][:].bitcast(U32).indirect(idx[:]))
         for h in range(2):
             nc.vector.tensor_copy(
                 w1_p[h][:].bitcast(U16).rearrange("p a (t m) -> p a t m", t=PACK),
                 w1_raw[:].bitcast(U16)[:, :, 512 * h:512 * h + 512].rearrange("p a (m t) -> p a t m", t=PACK))
-        nc.vector.tensor_copy(v_w[1][:], tab[1][:].bitcast(U32).indirect(idx[:]))
+        for j in range(2):
+            nc.vector.tensor_copy(v_w[1][:, 256 * j:256 * j + 256],
+                                  tab[1][:].bitcast(U32).indirect(idx[:, 16 * j:16 * j + 16]))
         pageA.append(tile("pageA2", [P, T2], F32))
         nc.gpsimd.memset(pageA[2][:], 0.0)
 
@@ -96,28 +106,45 @@ def tile_list_antenna_hour_urgency_kernel(tc, tab_words, tab_scales, offs, offs2
         w2_raw = tile("w2_raw", [P, 2, PACK, R], F32)
         wg1_v = wg1.rearrange("(p t) j -> p t j", t=PACK)
         for q in QUADRANTS:
-            (nc.sync if q < 2 else nc.scalar).dma_start(wgA[32 * q:32 * q + 32, 0, :], wg1_v[:, 0, :])
+            nc.sync.dma_start(wgA[32 * q:32 * q + 32, 0, :], wg1_v[:, 0, :])
         for q in QUADRANTS:
             nc.sync.dma_start(wgA[32 * q:32 * q + 32, 1:PACK, :], wg1_v[:, 1:PACK, :])
+        nc.sync.dma_start(idx3[:], offs3)
         w2_v = w2.rearrange("(a p j) m -> a p j m", a=2, j=PACK)
         w4_v = w4.rearrange("(a p j) n -> a p j n", a=2, j=PACK)
         for a in range(2):
             nc.sync.dma_start(w2_raw[:, a], w2_v[a])
         nc.sync.dma_start(bias, b2.rearrange("(p t) -> p t", t=PACK))
 
-        h1_acc = [bank(s, "acc_h1_%d" % s) for s in range(SLICES)]
+        h1_acc = [bank(s, "acc_h1_%d" % s) for s in range(LAST)]
         h1 = [tile("h1_%d" % s, [P, S], F32) for s in range(LAST)]
-        h2 = [tile("h2_%d" % s, [P, S], F32) for s in range(SLICES)]
-        for s in range(SLICES):
+        h2 = [tile("h2_%d" % s, [P, S], F32) for s in range(LAST)]
+        h2_last = [tile("h2_last0", [P, CUT], F32)]
+        def h1_pass(acc, s, a, cols, start, stop):
             h, t = divmod(s, PACK)
-            first, second = (0, 1) if s == 0 else (1, 0)
+            nc.tensor.matmul_mx(out=acc, lhsT=w1_p[h][:, a, 256 * t:256 * t + 256].bitcast(FP4X4),
+                                lhsT_scale=w1s_p[a][:, P * s:P * s + P],
+                                rhs=v_w[a][:, cols].bitcast(FP8X4), rhs_scale=v_s[a][:, cols],
+                                start=start, stop=stop)
+
+        def h1_half(acc, j, passes):
+            for a in passes:
+                for u in range(2):
+                    h1_pass(acc[:, P * u:P * u + P], 0, a, slice(256 * j + P * u, 256 * j + P * u + P),
+                            a == passes[0] and u == 0, a == passes[1] and u == 1)
+            nc.scalar.copy(h1[0][:, 256 * j:256 * j + 256], acc[:, 0:256])
+
+        h1_half(h1_acc[0], 0, (0, 1))
+        for s in range(1, SLICES):
+            if s == LAST:
+                h1_acc.append(bank(LAST, "acc_h1_last"))
+            first, second = FIRST if s == 1 else (1, 0)
             for a in (first, second):
-                nc.tensor.matmul_mx(out=h1_acc[s][:], lhsT=w1_p[h][:, a, 256 * t:256 * t + 256].bitcast(FP4X4),
-                                    lhsT_scale=w1s_p[a][:, P * s:P * s + P],
-                                    rhs=v_w[a][:].bitcast(FP8X4), rhs_scale=v_s[a],
-                                    start=(a == first), stop=(a == second))
+                h1_pass(h1_acc[s][:], s, a, slice(0, S), a == first, a == second)
             if s < LAST:
                 nc.scalar.copy(h1[s][:], h1_acc[s][:])
+            if s == 1:
+                h1_half(bank(LAST, "acc_h1_0b"), 1, (1, 0))
 
         w4_raw0 = tile("w4_raw0", [P, PACK, N], F32)
         nc.sync.dma_start(w4_raw0[:], w4_v[0])
@@ -131,16 +158,22 @@ def tile_list_antenna_hour_urgency_kernel(tc, tab_words, tab_scales, offs, offs2
         def scatter_b(s):
             nc.vector.tensor_tensor(page_b(s)[:].indirect(idx3[:]), h2[s][:], wgB[:, s % PACK, :], MULT)
 
-        for s in range(A_PAGES - 1):
-            scatter_a(s)
+        def scatter_first(j):
+            cols = slice(256 * j, 256 * j + 256)
+            nc.vector.tensor_tensor(pageA[0][:].indirect(idx2[:, 16 * j:16 * j + 16]), h1[0][:, cols],
+                                    wgA[:, 0, cols], MULT)
 
-        w3_in = tile("w3_in", [P, H + H // 4], I32, tag="h1_0")
+        scatter_first(0)
+        scatter_a(1)
+        scatter_first(1)
+        scatter_a(2)
+
+        w3_in = tile("w3_in", [P, H], I32, tag="h1_0")
         w3_raw = w3_in[:, 0:H]
-        w3s_raw = w3_in[:, H:H + H // 4]
-        nc.gpsimd.memset(w3s_raw, 0)
         nc.sync.dma_start(w3_raw, w3_words[0].rearrange("p c i -> p (c i)").bitcast(I32))
         for q in range(4):
-            nc.sync.dma_start(w3s_raw[32 * q:32 * q + 4], w3_scales[0, 4 * q:4 * q + 4, :].bitcast(I32))
+            nc.sync.dma_start(w1s_p[0][32 * q + 4:32 * q + 8].bitcast(I32),
+                              w1s_p[0][48 + 4 * q:52 + 4 * q].bitcast(I32))
 
         pageA.append(tile("pageA3", [P, T2], F32, tag="h1_1"))
         nc.gpsimd.memset(pageA[3][:], 0.0)
@@ -157,8 +190,9 @@ def tile_list_antenna_hour_urgency_kernel(tc, tab_words, tab_scales, offs, offs2
         for q in QUADRANTS:
             nc.sync.dma_start(wgB[32 * q:32 * q + 32], wg2.rearrange("(p t) j -> p t j", t=PACK))
         for s in range(early, SLICES):
+            if s == LAST - 1:
+                nc.sync.dma_start(w4_raw[1], w4_v[1])
             nc.sync.dma_start(l_raw[:, s, :], least_v[s // PACK, s % PACK])
-        nc.sync.dma_start(w4_raw[1], w4_v[1])
 
         w2_q = tile("w2_q", [P, 2, R], U32)
         w2_s = tile("w2_s", [P, 2, R], U8)
@@ -171,20 +205,19 @@ def tile_list_antenna_hour_urgency_kernel(tc, tab_words, tab_scales, offs, offs2
         w3_p = tile("w3_p", [P, H], I32)
         nc.vector.tensor_copy(w3_p[:].rearrange("p (h t u i) -> p h u t i", h=2, t=PACK, i=4),
                               w3_raw.rearrange("p (h u i t) -> p h u t i", h=2, t=PACK, i=4))
-        w3s_p = tile("w3s_p", [P, H], U8)
-        nc.vector.tensor_copy(w3s_p[:].rearrange("p (h t m) -> p h t m", h=2, t=PACK),
-                              w3s_raw.bitcast(U8).rearrange("p (h m t) -> p h t m", h=2, t=PACK))
 
-        w4_q = tile("w4_q", [P, 2, N], U32)
-        w4_s = tile("w4_s", [P, 2, N], U8)
+        w4_q = []
+        w4_s = [tile("w4_s%d" % a, [P, N], U8) for a in range(2)]
 
         def weave(dst, src):
             nc.scalar.copy(dst.rearrange("p (c n) i -> p c i n", n=4), src.rearrange("p i (c n) -> p c i n", n=4))
 
+        w4_bs = [tile("w4_b%d" % a, [P, N, PACK], BF16) for a in range(2)]
+
         def quantise_w4(a):
-            w4_b = tile("w4_b%d" % a, [P, N, PACK], BF16)
-            weave(w4_b[:], w4_raw[a])
-            nc.vector.quantize_mx(out=w4_q[:, a, :].bitcast(FP8X4), scales=w4_s[:, a, :],
+            w4_b = w4_bs[a]
+            w4_q.append(tile("w4_q%d" % a, [P, N], U32, tag=("w4_q0", "w4_q1")[a]))
+            nc.vector.quantize_mx(out=w4_q[a][:].bitcast(FP8X4), scales=w4_s[a][:],
                                   in_=w4_b[:].rearrange("p n j -> p (n j)"))
 
         z_rows = [tile("z_rows0", [P, PACK, T2], BF16, tag="w2_raw")]
@@ -206,6 +239,7 @@ def tile_list_antenna_hour_urgency_kernel(tc, tab_words, tab_scales, offs, offs2
         pageB = [tile("pageB%d" % i, [P, T2], F32, tag="h1_%d" % (A_PAGES + i)) for i in range(B_PAGES)]
         for page in pageB:
             nc.gpsimd.memset(page[:], 0.0)
+        weave(w4_bs[0][:], w4_raw[0])
         quantise_w4(0)
 
         d_rows = tile("d_rows", [P, PACK, S], BF16)
@@ -232,23 +266,33 @@ def tile_list_antenna_hour_urgency_kernel(tc, tab_words, tab_scales, offs, offs2
         for s in range(SLICES):
             acc = bank((s + PACK) % LAST if s < LAST else LAST, "acc_h2_%d" % s)
             nc.tensor.matmul_mx(out=acc[:], lhsT=w3_p[:, P * s:P * s + P].bitcast(FP8X4),
-                                lhsT_scale=w3s_p[:, P * s:P * s + P],
+                                lhsT_scale=w1s_p[0][4:P, P * s:P * s + P],
                                 rhs=d_q[:].bitcast(FP8X4), rhs_scale=d_s[:], start=True, stop=True)
-            nc.scalar.copy(h2[s][:], acc[:])
+            if s < LAST:
+                nc.scalar.copy(h2[s][:], acc[:])
+            else:
+                nc.scalar.copy(h2_last[0][:], acc[:, 0:CUT])
+                h2_acc = acc
         z_rows.append(tile("z_rows1", [P, PACK, T2], BF16, tag="w3_p"))
         for s in range(B_PAGES):
             scatter_b(s)
 
-        z_b = [[tile("z_b%d_%d" % (a, c), [P, CHUNK, PACK], BF16) for c in range(CHUNKS)] for a in range(2)]
-        z_q = tile("z_q", [P, 2, T2], U32)
-        z_s = [[tile("z_s%d_%d" % (a, c), [P, CHUNK], U8) for c in range(CHUNKS)] for a in range(2)]
-        o_acc = [bank(b, "acc_o_%d" % b) for b in range(2 * CHUNKS)]
-        o_tags = ("pageA0", "pageA1", "pageA2", "h1_1")
-        o_sb = [tile("o_sb%d" % c, [P, N // P, CHUNK], F32, tag=o_tags[c]) for c in range(CHUNKS)]
+        HALF = T2 // 2
+        z_b0 = [tile("z_b0_%d" % j, [P, HALF, PACK], BF16) for j in range(2)]
+        z_b1 = [tile("z_b1_%d" % c, [P, w, PACK], BF16) for c, w in enumerate(WIDTHS)]
+        z_q1 = tile("z_q1", [P, T2], U32)
+        z_s1 = [tile("z_s1_%d" % c, [P, w], U8) for c, w in enumerate(WIDTHS)]
+        o_acc = [bank(b, "acc_o_%d" % b) for b in range(7)]
+        o_sb = tile("o_sb", [P, N // P, T2], F32, tag="l_raw")
         out_v = out.rearrange("(n p) c -> p n c", p=P)
 
         def chunk(c):
-            return slice(CHUNK * c, CHUNK * c + CHUNK)
+            return slice(STARTS[c], STARTS[c] + WIDTHS[c])
+
+        def banks(c):
+            per = 512 // WIDTHS[c]
+            first = STARTS[c] * PACK // 512
+            return [(first + k, range(per * k, per * k + per)) for k in range(PACK // per)]
 
         def max_b(s):
             b_b = tile("b_b%d" % s, [P, T2], BF16, tag="b_b%d" % (s % 2))
@@ -257,53 +301,85 @@ def tile_list_antenna_hour_urgency_kernel(tc, tab_words, tab_scales, offs, offs2
             if s + B_PAGES < LAST:
                 scatter_b(s + B_PAGES)
 
-        def weave_z(a, c):
-            weave(z_b[a][c][:], z_rows[a][:, :, chunk(c)])
+        def multiply(a, c, codes, scales):
+            w = WIDTHS[c]
+            for b, blocks in banks(c):
+                for k, n in enumerate(blocks):
+                    nc.tensor.matmul_mx(out=o_acc[b][:, w * k:w * k + w],
+                                        lhsT=w4_q[a][:, P * n:P * n + P].bitcast(FP8X4),
+                                        lhsT_scale=w4_s[a][:, P * n:P * n + P],
+                                        rhs=codes.bitcast(FP8X4), rhs_scale=scales,
+                                        start=(a == 0 and k == 0), stop=(a == 1 and k == len(blocks) - 1))
 
-        def multiply_z(a, c):
-            nc.vector.quantize_mx(out=z_q[:, a, chunk(c)].bitcast(FP8X4), scales=z_s[a][c][:],
-                                  in_=z_b[a][c][:].rearrange("p c t -> p (c t)"))
-            for n in range(N // P):
-                k, half = divmod(n, 2)
-                nc.tensor.matmul_mx(out=o_acc[2 * c + k][:, CHUNK * half:CHUNK * half + CHUNK],
-                                    lhsT=w4_q[:, a, P * n:P * n + P].bitcast(FP8X4),
-                                    lhsT_scale=w4_s[:, a, P * n:P * n + P],
-                                    rhs=z_q[:, a, chunk(c)].bitcast(FP8X4), rhs_scale=z_s[a][c][:],
-                                    start=(a == 0 and half == 0), stop=(a == 1 and half == 1))
+        first_q = {}
+
+        def multiply_first(j, tag, mult):
+            if j not in first_q:
+                z_q0 = tile("z_q0_%d" % j, [P, HALF], U32, tag=tag)
+                z_s0 = tile("z_s0_%d" % j, [P, HALF], U8)
+                nc.vector.quantize_mx(out=z_q0[:].bitcast(FP8X4), scales=z_s0[:],
+                                      in_=z_b0[j][:].rearrange("p c t -> p (c t)"))
+                first_q[j] = (z_q0, z_s0)
+            if not mult:
+                return
+            z_q0, z_s0 = first_q[j]
+            for c in range(len(WIDTHS)):
+                if STARTS[c] // HALF == j:
+                    cols = slice(STARTS[c] - HALF * j, STARTS[c] - HALF * j + WIDTHS[c])
+                    multiply(0, c, z_q0[:, cols], z_s0[:, cols])
+
+        def scatter_last(j):
+            cols = (slice(0, CUT), slice(CUT, S))[j]
+            nc.vector.tensor_tensor(page_b(LAST)[:].indirect(idx3[:, cols.start // 16:cols.stop // 16]), h2_last[j][:],
+                                    wgB[:, PACK - 1, cols], MULT)
 
         max_least(early)
         for s in range(PACK):
             max_b(s)
             round_a(PACK + s)
             max_least(PACK + s)
-        max_b(LAST - 3)
-        for c in range(CHUNKS):
-            weave_z(0, c)
-            multiply_z(0, c)
-        max_b(LAST - 2)
+        weave(w4_bs[1][:], w4_raw[1])
         quantise_w4(1)
-        max_b(LAST - 1)
-        scatter_b(LAST)
+        max_b(LAST - 3)
+        def weave_first(j, u):
+            weave(z_b0[j][:, 256 * u:256 * u + 256, :], z_rows[0][:, :, HALF * j + 256 * u:HALF * j + 256 * u + 256])
 
-        end = CHUNKS - 1
-        for c in range(end):
-            weave_z(1, c)
-        nc.vector.tensor_tensor(z_slice(LAST)[:, chunk(end)], page_b(LAST)[:, chunk(end)],
-                                z_slice(LAST)[:, chunk(end)], MAX)
-        weave_z(1, end)
-        for c in range(CHUNKS):
-            if c < end:
-                woven = z_b[1][c][:, :, PACK - 1]
-                nc.vector.tensor_tensor(woven, page_b(LAST)[:, chunk(c)], woven, MAX)
-            multiply_z(1, c)
-            shared = c >= CHUNKS // 2
-            for k in range(2):
-                dst = o_sb[c][:, 2 * k:2 * k + 2, :]
-                if shared and k == 1:
-                    nc.vector.tensor_copy(dst.rearrange("p n c -> p (n c)"), o_acc[2 * c + k][:])
+        for j, u in ((1, 0), (1, 1), (0, 0)):
+            weave_first(j, u)
+        max_b(LAST - 2)
+        weave_first(0, 1)
+        multiply_first(0, "z_q0_0", True)
+        for j, cols in enumerate((slice(0, 512), slice(512, 1024))):
+            b_b = tile("b_b6_%d" % j, [P, cols.stop - cols.start], BF16)
+            nc.scalar.copy(b_b[:], page_b(LAST - 1)[:, cols])
+            nc.vector.tensor_tensor(z_slice(LAST - 1)[:, cols], z_slice(LAST - 1)[:, cols], b_b[:], MAX)
+        scatter_last(0)
+        multiply_first(1, "h2_last0", False)
+        for c in range(3):
+            weave(z_b1[c][:], z_rows[1][:, :, chunk(c)])
+        h2_last.append(tile("h2_last1", [P, S - CUT], F32, tag="b_b6_1"))
+        nc.scalar.copy(h2_last[1][:], h2_acc[:, CUT:S])
+        o_acc.append(bank(7, "acc_o_7"))
+        for c in range(3, len(WIDTHS)):
+            weave(z_b1[c][:], z_rows[1][:, :, chunk(c)])
+        multiply_first(1, "h2_last0", True)
+        scatter_last(1)
+        def max_last(c):
+            woven = z_b1[c][:, :, PACK - 1]
+            nc.vector.tensor_tensor(woven, page_b(LAST)[:, chunk(c)], woven, MAX)
+
+        max_last(0)
+        for c in range(len(WIDTHS)):
+            if c + 1 < len(WIDTHS):
+                max_last(c + 1)
+            nc.vector.quantize_mx(out=z_q1[:, chunk(c)].bitcast(FP8X4), scales=z_s1[c][:],
+                                  in_=z_b1[c][:].rearrange("p c t -> p (c t)"))
+            multiply(1, c, z_q1[:, chunk(c)], z_s1[c][:])
+            for k, (b, blocks) in enumerate(banks(c)):
+                dst = o_sb[:, blocks.start:blocks.stop, chunk(c)]
+                src = o_acc[b][:].rearrange("p (n c) -> p n c", c=WIDTHS[c])
+                if c >= 3 and k == 1:
+                    nc.vector.tensor_copy(dst, src)
                 else:
-                    nc.scalar.copy(dst.rearrange("p n c -> p (n c)"), o_acc[2 * c + k][:])
-                if not shared:
-                    nc.sync.dma_start(out_v[:, 2 * k:2 * k + 2, chunk(c)], dst)
-            if shared:
-                nc.sync.dma_start(out_v[:, :, chunk(c)], o_sb[c][:])
+                    nc.scalar.copy(dst, src)
+                nc.sync.dma_start(out_v[:, blocks.start:blocks.stop, chunk(c)], dst)

@@ -24,7 +24,9 @@ LAST = SLICES - 1
 CHUNK = 256
 WIDTHS = (128, 256, 128, 256, 256)
 CUT = 384
-FIRST = (0, 1)
+FIRST_WIDTHS = (512, 256, 256)
+FIRST_STARTS = (0, 512, 768)
+FIRST = (1, 0)
 STARTS = (0, 128, 384, 512, 768)
 A_PAGES = 4
 B_PAGES = 2
@@ -63,15 +65,15 @@ def tile_list_antenna_hour_urgency_kernel(tc, tab_words, tab_scales, offs, offs2
         nc.sync.dma_start(w1s_raw[0:32].bitcast(I32), w1_scales.rearrange("a q c -> (a q) c").bitcast(I32))
         nc.gpsimd.memset(w1s_raw[32:64].bitcast(I32), 0)
         nc.sync.dma_start(w1s_raw[48:64].bitcast(I32), w3_scales[0].bitcast(I32))
-        nc.sync.dma_start(tab[0][:], tab_words[0].rearrange("p t i -> p (t i)").bitcast(I32))
-        nc.sync.dma_start(w1_raw[:].bitcast(I32), w1_words.rearrange("a p b -> p a b").bitcast(I32))
         nc.sync.dma_start(idx2[:], offs2)
-        nc.sync.dma_start(tab[1][:], tab_words[1].rearrange("p t i -> p (t i)").bitcast(I32))
+        nc.sync.dma_start(w1_raw[:].bitcast(I32), w1_words.rearrange("a p b -> p a b").bitcast(I32))
+        nc.sync.dma_start(tab[0][:], tab_words[0].rearrange("p t i -> p (t i)").bitcast(I32), max_dma_last_dim=2048)
+        nc.sync.dma_start(tab[1][:], tab_words[1].rearrange("p t i -> p (t i)").bitcast(I32), max_dma_last_dim=2048)
 
         pageA = [tile("pageA0", [P, T2], F32)]
         for raw, rows in ((tab_s, slice(32, 64)), (tab_s, slice(64, 128)), (w1s_raw, slice(64, 128))):
-            nc.vector.memset(raw[rows].bitcast(I32), 0)
-        nc.vector.memset(scale[1][:].bitcast(I32), 0)
+            nc.gpsimd.memset(raw[rows].bitcast(I32), 0)
+        nc.gpsimd.memset(scale[1][:].bitcast(I32), 0)
         for page in pageA:
             nc.gpsimd.memset(page[:], 0.0)
         warm = tile("warm", [P, 16], F32)
@@ -228,10 +230,13 @@ def tile_list_antenna_hour_urgency_kernel(tc, tab_words, tab_scales, offs, offs2
         def round_a(s):
             nc.scalar.copy(z_slice(s), pageA[s % A_PAGES][:])
 
-        def max_least(s):
-            l_b = tile("l_b%d" % s, [P, T2], BF16)
-            nc.scalar.copy(l_b[:], l_raw[:, s, :])
-            nc.vector.tensor_tensor(z_slice(s), z_slice(s), l_b[:], MAX)
+        l_b = [tile("l_b%d" % a, [P, PACK * T2], BF16) for a in range(2)]
+
+        def round_least(s):
+            nc.scalar.copy(l_b[s // PACK][:, T2 * (s % PACK):T2 * (s % PACK + 1)], l_raw[:, s, :])
+
+        def z_flat(a):
+            return z_rows[a][:].rearrange("p i c -> p (i c)")
 
         for s in range(LAST - A_PAGES):
             round_a(s)
@@ -261,7 +266,7 @@ def tile_list_antenna_hour_urgency_kernel(tc, tab_words, tab_scales, offs, offs2
         round_a(LAST - A_PAGES)
         scatter_a(LAST)
         for s in range(early):
-            max_least(s)
+            round_least(s)
 
         for s in range(SLICES):
             acc = bank((s + PACK) % LAST if s < LAST else LAST, "acc_h2_%d" % s)
@@ -278,7 +283,7 @@ def tile_list_antenna_hour_urgency_kernel(tc, tab_words, tab_scales, offs, offs2
             scatter_b(s)
 
         HALF = T2 // 2
-        z_b0 = [tile("z_b0_%d" % j, [P, HALF, PACK], BF16) for j in range(2)]
+        z_b0 = [tile("z_b0_%d" % j, [P, w, PACK], BF16) for j, w in enumerate(FIRST_WIDTHS)]
         z_b1 = [tile("z_b1_%d" % c, [P, w, PACK], BF16) for c, w in enumerate(WIDTHS)]
         z_q1 = tile("z_q1", [P, T2], U32)
         z_s1 = [tile("z_s1_%d" % c, [P, w], U8) for c, w in enumerate(WIDTHS)]
@@ -294,10 +299,12 @@ def tile_list_antenna_hour_urgency_kernel(tc, tab_words, tab_scales, offs, offs2
             first = STARTS[c] * PACK // 512
             return [(first + k, range(per * k, per * k + per)) for k in range(PACK // per)]
 
-        def max_b(s):
-            b_b = tile("b_b%d" % s, [P, T2], BF16, tag="b_b%d" % (s % 2))
-            nc.scalar.copy(b_b[:], page_b(s)[:])
-            nc.vector.tensor_tensor(z_slice(s), z_slice(s), b_b[:], MAX)
+        b_b = [tile("b_b0", [P, PACK * T2], BF16, tag="w2_b0"), tile("b_b1", [P, 2 * T2], BF16, tag="w2_b1")]
+
+        def round_b(s):
+            nc.scalar.copy(b_b[s // PACK][:, T2 * (s % PACK):T2 * (s % PACK + 1)], page_b(s)[:])
+            if s == PACK - 1:
+                nc.vector.tensor_tensor(z_flat(0), z_flat(0), b_b[0][:], MAX)
             if s + B_PAGES < LAST:
                 scatter_b(s + B_PAGES)
 
@@ -313,48 +320,56 @@ def tile_list_antenna_hour_urgency_kernel(tc, tab_words, tab_scales, offs, offs2
 
         first_q = {}
 
-        def multiply_first(j, tag, mult):
-            if j not in first_q:
-                z_q0 = tile("z_q0_%d" % j, [P, HALF], U32, tag=tag)
-                z_s0 = tile("z_s0_%d" % j, [P, HALF], U8)
-                nc.vector.quantize_mx(out=z_q0[:].bitcast(FP8X4), scales=z_s0[:],
-                                      in_=z_b0[j][:].rearrange("p c t -> p (c t)"))
-                first_q[j] = (z_q0, z_s0)
-            if not mult:
-                return
+        def quantise_first(j, tag):
+            w = FIRST_WIDTHS[j]
+            z_q0 = tile("z_q0_%d" % j, [P, w], U32, tag=tag)
+            z_s0 = tile("z_s0_%d" % j, [P, w], U8)
+            nc.vector.quantize_mx(out=z_q0[:].bitcast(FP8X4), scales=z_s0[:],
+                                  in_=z_b0[j][:].rearrange("p c t -> p (c t)"))
+            first_q[j] = (z_q0, z_s0)
+
+        def multiply_first(j):
             z_q0, z_s0 = first_q[j]
             for c in range(len(WIDTHS)):
-                if STARTS[c] // HALF == j:
-                    cols = slice(STARTS[c] - HALF * j, STARTS[c] - HALF * j + WIDTHS[c])
-                    multiply(0, c, z_q0[:, cols], z_s0[:, cols])
+                at = STARTS[c] - FIRST_STARTS[j]
+                if 0 <= at < FIRST_WIDTHS[j]:
+                    multiply(0, c, z_q0[:, at:at + WIDTHS[c]], z_s0[:, at:at + WIDTHS[c]])
 
         def scatter_last(j):
             cols = (slice(0, CUT), slice(CUT, S))[j]
             nc.vector.tensor_tensor(page_b(LAST)[:].indirect(idx3[:, cols.start // 16:cols.stop // 16]), h2_last[j][:],
                                     wgB[:, PACK - 1, cols], MULT)
 
-        max_least(early)
+        def weave_first(j, u):
+            weave(z_b0[j][:, 256 * u:256 * u + 256, :], z_rows[0][:, :, FIRST_STARTS[j] + 256 * u:FIRST_STARTS[j] + 256 * u + 256])
+
+        round_least(early)
+        nc.vector.tensor_tensor(z_flat(0), z_flat(0), l_b[0][:], MAX)
         for s in range(PACK):
-            max_b(s)
+            round_b(s)
             round_a(PACK + s)
-            max_least(PACK + s)
+            round_least(PACK + s)
+        kept = tile("kept", [P, HALF], BF16)
+        cut = slice(2 * T2 + HALF, 3 * T2)
+        for cols in (slice(0, cut.start), cut, slice(cut.stop, PACK * T2)):
+            nc.vector.tensor_tensor(kept[:] if cols == cut else z_flat(1)[:, cols], z_flat(1)[:, cols], l_b[1][:, cols], MAX)
         weave(w4_bs[1][:], w4_raw[1])
         quantise_w4(1)
-        max_b(LAST - 3)
-        def weave_first(j, u):
-            weave(z_b0[j][:, 256 * u:256 * u + 256, :], z_rows[0][:, :, HALF * j + 256 * u:HALF * j + 256 * u + 256])
-
-        for j, u in ((1, 0), (1, 1), (0, 0)):
+        round_b(LAST - 3)
+        for j, u in ((1, 0), (2, 0), (0, 0)):
             weave_first(j, u)
-        max_b(LAST - 2)
+        round_b(LAST - 2)
+        nc.vector.tensor_tensor(z_flat(1)[:, 0:2 * T2], z_flat(1)[:, 0:2 * T2], b_b[1][:], MAX)
         weave_first(0, 1)
-        multiply_first(0, "z_q0_0", True)
+        quantise_first(0, "z_q0_0")
+        multiply_first(0)
         for j, cols in enumerate((slice(0, 512), slice(512, 1024))):
-            b_b = tile("b_b6_%d" % j, [P, cols.stop - cols.start], BF16)
-            nc.scalar.copy(b_b[:], page_b(LAST - 1)[:, cols])
-            nc.vector.tensor_tensor(z_slice(LAST - 1)[:, cols], z_slice(LAST - 1)[:, cols], b_b[:], MAX)
+            b_6 = tile("b_b6_%d" % j, [P, cols.stop - cols.start], BF16)
+            nc.scalar.copy(b_6[:], page_b(LAST - 1)[:, cols])
+            nc.vector.tensor_tensor(z_slice(LAST - 1)[:, cols], (z_slice(LAST - 1)[:, cols], kept[:])[j], b_6[:], MAX)
         scatter_last(0)
-        multiply_first(1, "h2_last0", False)
+        quantise_first(1, "kept")
+        multiply_first(1)
         for c in range(3):
             weave(z_b1[c][:], z_rows[1][:, :, chunk(c)])
         h2_last.append(tile("h2_last1", [P, S - CUT], F32, tag="b_b6_1"))
@@ -362,7 +377,6 @@ def tile_list_antenna_hour_urgency_kernel(tc, tab_words, tab_scales, offs, offs2
         o_acc.append(bank(7, "acc_o_7"))
         for c in range(3, len(WIDTHS)):
             weave(z_b1[c][:], z_rows[1][:, :, chunk(c)])
-        multiply_first(1, "h2_last0", True)
         scatter_last(1)
         def max_last(c):
             woven = z_b1[c][:, :, PACK - 1]
@@ -372,6 +386,9 @@ def tile_list_antenna_hour_urgency_kernel(tc, tab_words, tab_scales, offs, offs2
         for c in range(len(WIDTHS)):
             if c + 1 < len(WIDTHS):
                 max_last(c + 1)
+            else:
+                quantise_first(2, "z_b1_3")
+                multiply_first(2)
             nc.vector.quantize_mx(out=z_q1[:, chunk(c)].bitcast(FP8X4), scales=z_s1[c][:],
                                   in_=z_b1[c][:].rearrange("p c t -> p (c t)"))
             multiply(1, c, z_q1[:, chunk(c)], z_s1[c][:])

@@ -24,8 +24,8 @@ LAST = SLICES - 1
 CHUNK = 256
 WIDTHS = (128, 256, 128, 256, 256)
 CUT = 384
-FIRST_WIDTHS = (512, 256, 256)
-FIRST_STARTS = (0, 512, 768)
+FIRST_WIDTHS = (512, 512)
+FIRST_STARTS = (0, 512)
 FIRST = (1, 0)
 STARTS = (0, 128, 384, 512, 768)
 A_PAGES = 4
@@ -109,8 +109,9 @@ def tile_list_antenna_hour_urgency_kernel(tc, tab_words, tab_scales, offs, offs2
         wg1_v = wg1.rearrange("(p t) j -> p t j", t=PACK)
         for q in QUADRANTS:
             nc.sync.dma_start(wgA[32 * q:32 * q + 32, 0, :], wg1_v[:, 0, :])
-        for q in QUADRANTS:
-            nc.sync.dma_start(wgA[32 * q:32 * q + 32, 1:PACK, :], wg1_v[:, 1:PACK, :])
+        for rows in (slice(1, 2), slice(2, PACK)):
+            for q in QUADRANTS:
+                nc.sync.dma_start(wgA[32 * q:32 * q + 32, rows, :], wg1_v[:, rows, :])
         nc.sync.dma_start(idx3[:], offs3)
         w2_v = w2.rearrange("(a p j) m -> a p j m", a=2, j=PACK)
         w4_v = w4.rearrange("(a p j) n -> a p j n", a=2, j=PACK)
@@ -149,7 +150,6 @@ def tile_list_antenna_hour_urgency_kernel(tc, tab_words, tab_scales, offs, offs2
                 h1_half(bank(LAST, "acc_h1_0b"), 1, (1, 0))
 
         w4_raw0 = tile("w4_raw0", [P, PACK, N], F32)
-        nc.sync.dma_start(w4_raw0[:], w4_v[0])
 
         def scatter_a(s):
             nc.vector.tensor_tensor(pageA[s % A_PAGES][:].indirect(idx2[:]), h1[s][:], wgA[:, s % PACK, :], MULT)
@@ -170,6 +170,9 @@ def tile_list_antenna_hour_urgency_kernel(tc, tab_words, tab_scales, offs, offs2
         scatter_first(1)
         scatter_a(2)
 
+        l_raw = tile("l_raw", [P, SLICES, T2], F32)
+        least_v = least.rearrange("(a p t) c -> a t p c", a=2, t=PACK)
+        nc.sync.dma_start(l_raw[:, 0, :], least_v[0, 0])
         w3_in = tile("w3_in", [P, H], I32, tag="h1_0")
         w3_raw = w3_in[:, 0:H]
         nc.sync.dma_start(w3_raw, w3_words[0].rearrange("p c i -> p (c i)").bitcast(I32))
@@ -181,16 +184,16 @@ def tile_list_antenna_hour_urgency_kernel(tc, tab_words, tab_scales, offs, offs2
         nc.gpsimd.memset(pageA[3][:], 0.0)
         scatter_a(A_PAGES - 1)
 
-        l_raw = tile("l_raw", [P, SLICES, T2], F32)
         wgB_w4 = tile("wgB_w4", [P, 2 * PACK, S], F32, tag="h1_2")
         wgB = wgB_w4[:, 0:PACK, :]
         w4_raw = [w4_raw0[:], wgB_w4[:, PACK:2 * PACK, :]]
-        least_v = least.rearrange("(a p t) c -> a t p c", a=2, t=PACK)
-        early = 3
-        for s in range(early):
+        early = 4
+        for s in range(1, early):
             nc.sync.dma_start(l_raw[:, s, :], least_v[0, s])
-        for q in QUADRANTS:
-            nc.sync.dma_start(wgB[32 * q:32 * q + 32], wg2.rearrange("(p t) j -> p t j", t=PACK))
+        nc.sync.dma_start(w4_raw0[:], w4_v[0])
+        for rows in (slice(0, 2), slice(2, PACK)):
+            for q in QUADRANTS:
+                nc.sync.dma_start(wgB[32 * q:32 * q + 32, rows], wg2.rearrange("(p t) j -> p t j", t=PACK)[:, rows])
         for s in range(early, SLICES):
             if s == LAST - 1:
                 nc.sync.dma_start(w4_raw[1], w4_v[1])
@@ -244,8 +247,8 @@ def tile_list_antenna_hour_urgency_kernel(tc, tab_words, tab_scales, offs, offs2
         pageB = [tile("pageB%d" % i, [P, T2], F32, tag="h1_%d" % (A_PAGES + i)) for i in range(B_PAGES)]
         for page in pageB:
             nc.gpsimd.memset(page[:], 0.0)
-        weave(w4_bs[0][:], w4_raw[0])
-        quantise_w4(0)
+
+        round_least(0)
 
         d_rows = tile("d_rows", [P, PACK, S], BF16)
         d_b = tile("d_b", [P, S, PACK], BF16)
@@ -265,7 +268,7 @@ def tile_list_antenna_hour_urgency_kernel(tc, tab_words, tab_scales, offs, offs2
         nc.scalar.copy(h1[LAST][:], h1_acc[LAST][:])
         round_a(LAST - A_PAGES)
         scatter_a(LAST)
-        for s in range(early):
+        for s in range(1, early):
             round_least(s)
 
         for s in range(SLICES):
@@ -343,8 +346,9 @@ def tile_list_antenna_hour_urgency_kernel(tc, tab_words, tab_scales, offs, offs2
         def weave_first(j, u):
             weave(z_b0[j][:, 256 * u:256 * u + 256, :], z_rows[0][:, :, FIRST_STARTS[j] + 256 * u:FIRST_STARTS[j] + 256 * u + 256])
 
-        round_least(early)
         nc.vector.tensor_tensor(z_flat(0), z_flat(0), l_b[0][:], MAX)
+        weave(w4_bs[0][:], w4_raw[0])
+        quantise_w4(0)
         for s in range(PACK):
             round_b(s)
             round_a(PACK + s)
@@ -356,7 +360,7 @@ def tile_list_antenna_hour_urgency_kernel(tc, tab_words, tab_scales, offs, offs2
         weave(w4_bs[1][:], w4_raw[1])
         quantise_w4(1)
         round_b(LAST - 3)
-        for j, u in ((1, 0), (2, 0), (0, 0)):
+        for j, u in ((1, 0), (1, 1), (0, 0)):
             weave_first(j, u)
         round_b(LAST - 2)
         nc.vector.tensor_tensor(z_flat(1)[:, 0:2 * T2], z_flat(1)[:, 0:2 * T2], b_b[1][:], MAX)
@@ -369,7 +373,6 @@ def tile_list_antenna_hour_urgency_kernel(tc, tab_words, tab_scales, offs, offs2
             nc.vector.tensor_tensor(z_slice(LAST - 1)[:, cols], (z_slice(LAST - 1)[:, cols], kept[:])[j], b_6[:], MAX)
         scatter_last(0)
         quantise_first(1, "kept")
-        multiply_first(1)
         for c in range(3):
             weave(z_b1[c][:], z_rows[1][:, :, chunk(c)])
         h2_last.append(tile("h2_last1", [P, S - CUT], F32, tag="b_b6_1"))
@@ -377,6 +380,7 @@ def tile_list_antenna_hour_urgency_kernel(tc, tab_words, tab_scales, offs, offs2
         o_acc.append(bank(7, "acc_o_7"))
         for c in range(3, len(WIDTHS)):
             weave(z_b1[c][:], z_rows[1][:, :, chunk(c)])
+        multiply_first(1)
         scatter_last(1)
         def max_last(c):
             woven = z_b1[c][:, :, PACK - 1]
@@ -386,9 +390,6 @@ def tile_list_antenna_hour_urgency_kernel(tc, tab_words, tab_scales, offs, offs2
         for c in range(len(WIDTHS)):
             if c + 1 < len(WIDTHS):
                 max_last(c + 1)
-            else:
-                quantise_first(2, "z_b1_3")
-                multiply_first(2)
             nc.vector.quantize_mx(out=z_q1[:, chunk(c)].bitcast(FP8X4), scales=z_s1[c][:],
                                   in_=z_b1[c][:].rearrange("p c t -> p (c t)"))
             multiply(1, c, z_q1[:, chunk(c)], z_s1[c][:])

@@ -18,23 +18,34 @@ MAX = mybir.AluOpType.max
 RELU = mybir.ActivationFunctionType.Relu
 
 P = 128
+BANK = 512
 PACK = 4
 SLICES = H // P
 LAST = SLICES - 1
-CHUNK = 256
-WIDTHS = (128, 256, 128, 256, 256)
-CUT = 384
-FIRST_WIDTHS = (512, 512)
-FIRST_STARTS = (0, 512)
-FIRST = (1, 0)
-STARTS = (0, 128, 384, 512, 768)
 A_PAGES = 4
 B_PAGES = 2
 QUADRANTS = (0, 2, 1, 3)
+TABLE_PIECE = 2048
+LIST_HALVES = (slice(0, S // 2), slice(S // 2, S))
+LAST_PARTS = (slice(0, 384), slice(384, S))
+HALF = T2 // 2
+WEAVE = 256
+CHUNKS = (slice(0, 128), slice(128, 384), slice(384, 512), slice(512, 768), slice(768, 1024))
+WOVEN_AHEAD = 2
+SHARED_FROM = 3
+
+
+def width(cols):
+    return cols.stop - cols.start
+
+
+def entries(idx, part):
+    return idx[:, part.start // 16:part.stop // 16]
 
 
 def tile_list_antenna_hour_urgency_kernel(tc, tab_words, tab_scales, offs, offs2, offs3, w1_words,
-                                                    w1_scales, w2, b2, w3_words, w3_scales, wg1, wg2, least, w4, out):
+                                                       w1_scales, w2, b2, w3_words, w3_scales, wg1, wg2, least, w4,
+                                                       out):
     nc = tc.nc
     with ExitStack() as ctx:
         sb = ctx.enter_context(tc.tile_pool(name="sb", bufs=1))
@@ -44,74 +55,78 @@ def tile_list_antenna_hour_urgency_kernel(tc, tab_words, tab_scales, offs, offs2
             return sb.tile(shape, dtype, name=name, tag=tag or name, align_bytes=64)
 
         def bank(b, name):
-            return ps.tile([P, 512], F32, name=name, tag="bank%d" % b)
+            return ps.tile([P, BANK], F32, name=name, tag="bank%d" % b)
 
         idx = tile("idx", [P, S // 16], U16)
         idx2 = tile("idx2", [P, S // 16], U16)
         idx3 = tile("idx3", [P, S // 16], U16)
         tab = [tile("tab%d" % a, [P, T], I32, tag=("w3_p", "pageA2")[a]) for a in range(2)]
         tab_s = tile("tab_s", [P, T], U8)
-        w1_raw = tile("w1_raw", [P, 2, 2 * H], U8, tag="w2_raw")
-        w1s_raw = tile("w1s_raw", [P, H], U8)
+        w1_raw = tile("w1_raw", [P, 2, 2 * H], U8, tag="pageA1")
+        ws_raw = tile("ws_raw", [P, H], U8)
         v_w = [tile("v_w%d" % a, [P, S], U32) for a in range(2)]
         v_g = tile("v_g", [P, S], U8)
         scale = [tile("scale%d" % a, [P, S + H], U8) for a in range(2)]
         v_s = [scale[a][:, 0:S] for a in range(2)]
-        w1s_p = [scale[a][:, S:S + H] for a in range(2)]
+        ws_p = [scale[a][:, S:S + H] for a in range(2)]
         w1_p = [tile("w1_p%d" % h, [P, 2, 1024], U8, tag=("w4_raw0", "l_raw")[h]) for h in range(2)]
 
         nc.sync.dma_start(idx[:], offs)
         nc.sync.dma_start(tab_s[0:32].bitcast(I32), tab_scales.rearrange("a q c -> (a q) c").bitcast(I32))
-        nc.sync.dma_start(w1s_raw[0:32].bitcast(I32), w1_scales.rearrange("a q c -> (a q) c").bitcast(I32))
-        nc.gpsimd.memset(w1s_raw[32:64].bitcast(I32), 0)
-        nc.sync.dma_start(w1s_raw[48:64].bitcast(I32), w3_scales[0].bitcast(I32))
+        nc.sync.dma_start(ws_raw[0:32].bitcast(I32), w1_scales.rearrange("a q c -> (a q) c").bitcast(I32))
+        nc.gpsimd.memset(ws_raw[32:64].bitcast(I32), 0)
+        nc.sync.dma_start(ws_raw[48:64].bitcast(I32), w3_scales[0].bitcast(I32))
         nc.sync.dma_start(idx2[:], offs2)
         nc.sync.dma_start(w1_raw[:].bitcast(I32), w1_words.rearrange("a p b -> p a b").bitcast(I32))
-        nc.sync.dma_start(tab[0][:], tab_words[0].rearrange("p t i -> p (t i)").bitcast(I32), max_dma_last_dim=2048)
-        nc.sync.dma_start(tab[1][:], tab_words[1].rearrange("p t i -> p (t i)").bitcast(I32), max_dma_last_dim=2048)
+        for a in range(2):
+            nc.sync.dma_start(tab[a][:], tab_words[a].rearrange("p t i -> p (t i)").bitcast(I32),
+                              max_dma_last_dim=TABLE_PIECE)
 
-        pageA = [tile("pageA0", [P, T2], F32)]
-        for raw, rows in ((tab_s, slice(32, 64)), (tab_s, slice(64, 128)), (w1s_raw, slice(64, 128))):
+        for raw, rows in ((tab_s, slice(32, 64)), (tab_s, slice(64, 128)), (ws_raw, slice(64, 128))):
             nc.gpsimd.memset(raw[rows].bitcast(I32), 0)
+
+        pageA = []
+
+        def new_page_a(tag):
+            pageA.append(tile("pageA%d" % len(pageA), [P, T2], F32, tag=tag))
+            nc.gpsimd.memset(pageA[-1][:], 0.0)
+
+        new_page_a("pageA0")
         nc.gpsimd.memset(scale[1][:].bitcast(I32), 0)
-        for page in pageA:
-            nc.gpsimd.memset(page[:], 0.0)
         warm = tile("warm", [P, 16], F32)
         nc.scalar.copy(warm[:, 0:1], pageA[0][:, 0:1])
 
         nc.vector.tensor_copy(v_g[:], tab_s[:].indirect(idx[:]))
-        nc.vector.tensor_copy(w1s_p[0].rearrange("p (h t m) -> p h t m", h=2, t=PACK),
-                              w1s_raw[:].rearrange("p (h m t) -> p h t m", h=2, t=PACK))
+        nc.vector.tensor_copy(ws_p[0].rearrange("p (h t m) -> p h t m", h=2, t=PACK),
+                              ws_raw[:].rearrange("p (h m t) -> p h t m", h=2, t=PACK))
         nc.vector.tensor_copy(v_s[0].bitcast(I32), v_g[:].bitcast(I32))
         for a in range(2):
             for q in range(1 - a, 4):
                 row = 16 * a + 4 * q
                 nc.scalar.dma_start(scale[a][32 * q:32 * q + 4].bitcast(I32), scale[0][row:row + 4].bitcast(I32))
 
-        pageA.append(tile("pageA1", [P, T2], F32, tag="v_g"))
-        nc.gpsimd.memset(pageA[1][:], 0.0)
-
         nc.vector.tensor_copy(v_w[0][:], tab[0][:].bitcast(U32).indirect(idx[:]))
         for h in range(2):
             nc.vector.tensor_copy(
                 w1_p[h][:].bitcast(U16).rearrange("p a (t m) -> p a t m", t=PACK),
                 w1_raw[:].bitcast(U16)[:, :, 512 * h:512 * h + 512].rearrange("p a (m t) -> p a t m", t=PACK))
-        for j in range(2):
-            nc.vector.tensor_copy(v_w[1][:, 256 * j:256 * j + 256],
-                                  tab[1][:].bitcast(U32).indirect(idx[:, 16 * j:16 * j + 16]))
-        pageA.append(tile("pageA2", [P, T2], F32))
-        nc.gpsimd.memset(pageA[2][:], 0.0)
+        new_page_a("pageA1")
+        for part in LIST_HALVES:
+            nc.vector.tensor_copy(v_w[1][:, part], tab[1][:].bitcast(U32).indirect(entries(idx, part)))
+        new_page_a("pageA2")
 
         wgA_bias = tile("wgA", [P, PACK * S + 16], F32)
         wgA = wgA_bias[:, 0:PACK * S].rearrange("p (t j) -> p t j", t=PACK)
         bias = wgA_bias[:, PACK * S:PACK * S + PACK]
         w2_raw = tile("w2_raw", [P, 2, PACK, R], F32)
-        wg1_v = wg1.rearrange("(p t) j -> p t j", t=PACK)
-        for q in QUADRANTS:
-            nc.sync.dma_start(wgA[32 * q:32 * q + 32, 0, :], wg1_v[:, 0, :])
-        for rows in (slice(1, 2), slice(2, PACK)):
-            for q in QUADRANTS:
-                nc.sync.dma_start(wgA[32 * q:32 * q + 32, rows, :], wg1_v[:, rows, :])
+
+        def load_wg(dst, wg, cuts):
+            for lo, hi in zip(cuts, cuts[1:]):
+                for q in QUADRANTS:
+                    nc.sync.dma_start(dst[32 * q:32 * q + 32, lo:hi],
+                                      wg.rearrange("(p t) j -> p (t j)", t=PACK)[:, lo:hi])
+
+        load_wg(wgA_bias, wg1, (0, S // 2, 2 * S, PACK * S))
         nc.sync.dma_start(idx3[:], offs3)
         w2_v = w2.rearrange("(a p j) m -> a p j m", a=2, j=PACK)
         w4_v = w4.rearrange("(a p j) n -> a p j n", a=2, j=PACK)
@@ -120,39 +135,39 @@ def tile_list_antenna_hour_urgency_kernel(tc, tab_words, tab_scales, offs, offs2
         nc.sync.dma_start(bias, b2.rearrange("(p t) -> p t", t=PACK))
 
         h1_acc = [bank(s, "acc_h1_%d" % s) for s in range(LAST)]
-        h1 = [tile("h1_%d" % s, [P, S], F32) for s in range(LAST)]
+        h1 = [tile("h1_%d" % s, [P, S], F32) for s in range(SLICES)]
         h2 = [tile("h2_%d" % s, [P, S], F32) for s in range(LAST)]
-        h2_last = [tile("h2_last0", [P, CUT], F32)]
+        h2_last = [tile("h2_last0", [P, width(LAST_PARTS[0])], F32)]
+
         def h1_pass(acc, s, a, cols, start, stop):
             h, t = divmod(s, PACK)
             nc.tensor.matmul_mx(out=acc, lhsT=w1_p[h][:, a, 256 * t:256 * t + 256].bitcast(FP4X4),
-                                lhsT_scale=w1s_p[a][:, P * s:P * s + P],
+                                lhsT_scale=ws_p[a][:, P * s:P * s + P],
                                 rhs=v_w[a][:, cols].bitcast(FP8X4), rhs_scale=v_s[a][:, cols],
                                 start=start, stop=stop)
 
-        def h1_half(acc, j, passes):
+        def h1_first_slice(acc, part, passes):
             for a in passes:
                 for u in range(2):
-                    h1_pass(acc[:, P * u:P * u + P], 0, a, slice(256 * j + P * u, 256 * j + P * u + P),
+                    h1_pass(acc[:, P * u:P * u + P], 0, a, slice(part.start + P * u, part.start + P * u + P),
                             a == passes[0] and u == 0, a == passes[1] and u == 1)
-            nc.scalar.copy(h1[0][:, 256 * j:256 * j + 256], acc[:, 0:256])
+            nc.scalar.copy(h1[0][:, part], acc[:, 0:width(part)])
 
-        h1_half(h1_acc[0], 0, (0, 1))
+        h1_first_slice(h1_acc[0], LIST_HALVES[0], (0, 1))
         for s in range(1, SLICES):
             if s == LAST:
                 h1_acc.append(bank(LAST, "acc_h1_last"))
-            first, second = FIRST if s == 1 else (1, 0)
-            for a in (first, second):
-                h1_pass(h1_acc[s][:], s, a, slice(0, S), a == first, a == second)
-            if s < LAST:
-                nc.scalar.copy(h1[s][:], h1_acc[s][:])
+            for a in (1, 0):
+                h1_pass(h1_acc[s][:], s, a, slice(0, S), a == 1, a == 0)
+            nc.scalar.copy(h1[s][:], h1_acc[s][:])
             if s == 1:
-                h1_half(bank(LAST, "acc_h1_0b"), 1, (1, 0))
+                h1_first_slice(bank(LAST, "acc_h1_0b"), LIST_HALVES[1], (1, 0))
 
         w4_raw0 = tile("w4_raw0", [P, PACK, N], F32)
 
-        def scatter_a(s):
-            nc.vector.tensor_tensor(pageA[s % A_PAGES][:].indirect(idx2[:]), h1[s][:], wgA[:, s % PACK, :], MULT)
+        def scatter_a(s, part=slice(0, S)):
+            nc.vector.tensor_tensor(pageA[s % A_PAGES][:].indirect(entries(idx2, part)), h1[s][:, part],
+                                    wgA[:, s % PACK, part], MULT)
 
         def page_b(s):
             return pageB[min(s, LAST - 1) % B_PAGES]
@@ -160,44 +175,38 @@ def tile_list_antenna_hour_urgency_kernel(tc, tab_words, tab_scales, offs, offs2
         def scatter_b(s):
             nc.vector.tensor_tensor(page_b(s)[:].indirect(idx3[:]), h2[s][:], wgB[:, s % PACK, :], MULT)
 
-        def scatter_first(j):
-            cols = slice(256 * j, 256 * j + 256)
-            nc.vector.tensor_tensor(pageA[0][:].indirect(idx2[:, 16 * j:16 * j + 16]), h1[0][:, cols],
-                                    wgA[:, 0, cols], MULT)
-
-        scatter_first(0)
+        scatter_a(0, LIST_HALVES[0])
         scatter_a(1)
-        scatter_first(1)
+        scatter_a(0, LIST_HALVES[1])
         scatter_a(2)
 
         l_raw = tile("l_raw", [P, SLICES, T2], F32)
         least_v = least.rearrange("(a p t) c -> a t p c", a=2, t=PACK)
-        nc.sync.dma_start(l_raw[:, 0, :], least_v[0, 0])
-        w3_in = tile("w3_in", [P, H], I32, tag="h1_0")
-        w3_raw = w3_in[:, 0:H]
-        nc.sync.dma_start(w3_raw, w3_words[0].rearrange("p c i -> p (c i)").bitcast(I32))
-        for q in range(4):
-            nc.sync.dma_start(w1s_p[0][32 * q + 4:32 * q + 8].bitcast(I32),
-                              w1s_p[0][48 + 4 * q:52 + 4 * q].bitcast(I32))
 
-        pageA.append(tile("pageA3", [P, T2], F32, tag="h1_1"))
-        nc.gpsimd.memset(pageA[3][:], 0.0)
+        def load_least(s):
+            nc.sync.dma_start(l_raw[:, s, :], least_v[s // PACK, s % PACK])
+
+        load_least(0)
+        w3_raw = tile("w3_raw", [P, H], I32, tag="h1_0")
+        nc.sync.dma_start(w3_raw[:], w3_words[0].rearrange("p c i -> p (c i)").bitcast(I32))
+        for q in range(4):
+            nc.sync.dma_start(ws_p[0][32 * q + 4:32 * q + 8].bitcast(I32), ws_p[0][48 + 4 * q:52 + 4 * q].bitcast(I32))
+
+        new_page_a("h1_1")
         scatter_a(A_PAGES - 1)
 
         wgB_w4 = tile("wgB_w4", [P, 2 * PACK, S], F32, tag="h1_2")
         wgB = wgB_w4[:, 0:PACK, :]
         w4_raw = [w4_raw0[:], wgB_w4[:, PACK:2 * PACK, :]]
-        early = 4
-        for s in range(1, early):
-            nc.sync.dma_start(l_raw[:, s, :], least_v[0, s])
-        nc.sync.dma_start(w4_raw0[:], w4_v[0])
-        for rows in (slice(0, 2), slice(2, PACK)):
-            for q in QUADRANTS:
-                nc.sync.dma_start(wgB[32 * q:32 * q + 32, rows], wg2.rearrange("(p t) j -> p t j", t=PACK)[:, rows])
-        for s in range(early, SLICES):
-            if s == LAST - 1:
-                nc.sync.dma_start(w4_raw[1], w4_v[1])
-            nc.sync.dma_start(l_raw[:, s, :], least_v[s // PACK, s % PACK])
+        for s in range(1, PACK):
+            load_least(s)
+        nc.sync.dma_start(w4_raw[0], w4_v[0])
+        load_wg(wgB.rearrange("p t j -> p (t j)"), wg2, (0, B_PAGES * S, PACK * S))
+        for s in range(PACK, LAST - 1):
+            load_least(s)
+        nc.sync.dma_start(w4_raw[1], w4_v[1])
+        for s in range(LAST - 1, SLICES):
+            load_least(s)
 
         w2_q = tile("w2_q", [P, 2, R], U32)
         w2_s = tile("w2_s", [P, 2, R], U8)
@@ -209,37 +218,39 @@ def tile_list_antenna_hour_urgency_kernel(tc, tab_words, tab_scales, offs, offs2
 
         w3_p = tile("w3_p", [P, H], I32)
         nc.vector.tensor_copy(w3_p[:].rearrange("p (h t u i) -> p h u t i", h=2, t=PACK, i=4),
-                              w3_raw.rearrange("p (h u i t) -> p h u t i", h=2, t=PACK, i=4))
+                              w3_raw[:].rearrange("p (h u i t) -> p h u t i", h=2, t=PACK, i=4))
 
-        w4_q = []
+        w4_q = [tile("w4_q%d" % a, [P, N], U32) for a in range(2)]
         w4_s = [tile("w4_s%d" % a, [P, N], U8) for a in range(2)]
 
         def weave(dst, src):
             nc.scalar.copy(dst.rearrange("p (c n) i -> p c i n", n=4), src.rearrange("p i (c n) -> p c i n", n=4))
 
-        w4_bs = [tile("w4_b%d" % a, [P, N, PACK], BF16) for a in range(2)]
+        def quantise(codes, scales, woven):
+            nc.vector.quantize_mx(out=codes.bitcast(FP8X4), scales=scales, in_=woven.rearrange("p c i -> p (c i)"))
 
         def quantise_w4(a):
-            w4_b = w4_bs[a]
-            w4_q.append(tile("w4_q%d" % a, [P, N], U32, tag=("w4_q0", "w4_q1")[a]))
-            nc.vector.quantize_mx(out=w4_q[a][:].bitcast(FP8X4), scales=w4_s[a][:],
-                                  in_=w4_b[:].rearrange("p n j -> p (n j)"))
+            w4_b = tile("w4_b%d" % a, [P, N, PACK], BF16)
+            weave(w4_b[:], w4_raw[a])
+            quantise(w4_q[a][:], w4_s[a][:], w4_b[:])
 
         z_rows = [tile("z_rows0", [P, PACK, T2], BF16, tag="w2_raw")]
+        l_b = [tile("l_b%d" % a, [P, PACK * T2], BF16, tag=("w2_b1", "l_b1")[a]) for a in range(2)]
 
         def z_slice(s):
             return z_rows[s // PACK][:, s % PACK, :]
 
+        def z_flat(a):
+            return z_rows[a][:].rearrange("p i c -> p (i c)")
+
+        def place(tiles, s):
+            return tiles[s // PACK][:, T2 * (s % PACK):T2 * (s % PACK + 1)]
+
         def round_a(s):
             nc.scalar.copy(z_slice(s), pageA[s % A_PAGES][:])
 
-        l_b = [tile("l_b%d" % a, [P, PACK * T2], BF16) for a in range(2)]
-
         def round_least(s):
-            nc.scalar.copy(l_b[s // PACK][:, T2 * (s % PACK):T2 * (s % PACK + 1)], l_raw[:, s, :])
-
-        def z_flat(a):
-            return z_rows[a][:].rearrange("p i c -> p (i c)")
+            nc.scalar.copy(place(l_b, s), l_raw[:, s, :])
 
         for s in range(LAST - A_PAGES):
             round_a(s)
@@ -247,7 +258,6 @@ def tile_list_antenna_hour_urgency_kernel(tc, tab_words, tab_scales, offs, offs2
         pageB = [tile("pageB%d" % i, [P, T2], F32, tag="h1_%d" % (A_PAGES + i)) for i in range(B_PAGES)]
         for page in pageB:
             nc.gpsimd.memset(page[:], 0.0)
-
         round_least(0)
 
         d_rows = tile("d_rows", [P, PACK, S], BF16)
@@ -261,59 +271,55 @@ def tile_list_antenna_hour_urgency_kernel(tc, tab_words, tab_scales, offs, offs2
                                     lhsT_scale=w2_s[:, a, P * t:P * t + P],
                                     rhs=v_w[a][:].bitcast(FP8X4), rhs_scale=v_s[a], start=(a == 0), stop=(a == 1))
             nc.scalar.activation(d_rows[:, t, :], acc[:], RELU, bias=bias[:, t:t + 1])
+        round_least(1)
         weave(d_b[:], d_rows[:])
-        nc.vector.quantize_mx(out=d_q[:].bitcast(FP8X4), scales=d_s[:], in_=d_b[:].rearrange("p j t -> p (j t)"))
+        quantise(d_q[:], d_s[:], d_b[:])
 
-        h1.append(tile("h1_last", [P, S], F32, tag="d_rows"))
-        nc.scalar.copy(h1[LAST][:], h1_acc[LAST][:])
         round_a(LAST - A_PAGES)
         scatter_a(LAST)
-        for s in range(1, early):
+        for s in range(2, PACK):
             round_least(s)
 
         for s in range(SLICES):
-            acc = bank((s + PACK) % LAST if s < LAST else LAST, "acc_h2_%d" % s)
-            nc.tensor.matmul_mx(out=acc[:], lhsT=w3_p[:, P * s:P * s + P].bitcast(FP8X4),
-                                lhsT_scale=w1s_p[0][4:P, P * s:P * s + P],
+            h2_acc = bank((s + PACK) % LAST if s < LAST else LAST, "acc_h2_%d" % s)
+            nc.tensor.matmul_mx(out=h2_acc[:], lhsT=w3_p[:, P * s:P * s + P].bitcast(FP8X4),
+                                lhsT_scale=ws_p[0][4:P, P * s:P * s + P],
                                 rhs=d_q[:].bitcast(FP8X4), rhs_scale=d_s[:], start=True, stop=True)
             if s < LAST:
-                nc.scalar.copy(h2[s][:], acc[:])
+                nc.scalar.copy(h2[s][:], h2_acc[:])
             else:
-                nc.scalar.copy(h2_last[0][:], acc[:, 0:CUT])
-                h2_acc = acc
+                nc.scalar.copy(h2_last[0][:], h2_acc[:, LAST_PARTS[0]])
         z_rows.append(tile("z_rows1", [P, PACK, T2], BF16, tag="w3_p"))
         for s in range(B_PAGES):
             scatter_b(s)
 
-        HALF = T2 // 2
-        z_b0 = [tile("z_b0_%d" % j, [P, w, PACK], BF16) for j, w in enumerate(FIRST_WIDTHS)]
-        z_b1 = [tile("z_b1_%d" % c, [P, w, PACK], BF16) for c, w in enumerate(WIDTHS)]
+        z_b0 = [tile("z_b0_%d" % j, [P, HALF, PACK], BF16) for j in range(2)]
+        z_b1 = [tile("z_b1_%d" % c, [P, width(cols), PACK], BF16) for c, cols in enumerate(CHUNKS)]
         z_q1 = tile("z_q1", [P, T2], U32)
-        z_s1 = [tile("z_s1_%d" % c, [P, w], U8) for c, w in enumerate(WIDTHS)]
-        o_acc = [bank(b, "acc_o_%d" % b) for b in range(7)]
+        z_s1 = [tile("z_s1_%d" % c, [P, width(cols)], U8) for c, cols in enumerate(CHUNKS)]
+        o_acc = [bank(b, "acc_o_%d" % b) for b in range(LAST)]
         o_sb = tile("o_sb", [P, N // P, T2], F32, tag="l_raw")
         out_v = out.rearrange("(n p) c -> p n c", p=P)
-
-        def chunk(c):
-            return slice(STARTS[c], STARTS[c] + WIDTHS[c])
-
-        def banks(c):
-            per = 512 // WIDTHS[c]
-            first = STARTS[c] * PACK // 512
-            return [(first + k, range(per * k, per * k + per)) for k in range(PACK // per)]
-
         b_b = [tile("b_b0", [P, PACK * T2], BF16, tag="w2_b0"), tile("b_b1", [P, 2 * T2], BF16, tag="w2_b1")]
 
+        def banks(cols):
+            per = BANK // width(cols)
+            first = cols.start * (N // P) // BANK
+            return [(first + k, range(per * k, per * k + per)) for k in range(N // P // per)]
+
+        def maximum(dst, a, b):
+            nc.vector.tensor_tensor(dst, a, b, MAX)
+
         def round_b(s):
-            nc.scalar.copy(b_b[s // PACK][:, T2 * (s % PACK):T2 * (s % PACK + 1)], page_b(s)[:])
+            nc.scalar.copy(place(b_b, s), page_b(s)[:])
             if s == PACK - 1:
-                nc.vector.tensor_tensor(z_flat(0), z_flat(0), b_b[0][:], MAX)
+                maximum(z_flat(0), z_flat(0), b_b[0][:])
             if s + B_PAGES < LAST:
                 scatter_b(s + B_PAGES)
 
-        def multiply(a, c, codes, scales):
-            w = WIDTHS[c]
-            for b, blocks in banks(c):
+        def multiply(a, cols, codes, scales):
+            w = width(cols)
+            for b, blocks in banks(cols):
                 for k, n in enumerate(blocks):
                     nc.tensor.matmul_mx(out=o_acc[b][:, w * k:w * k + w],
                                         lhsT=w4_q[a][:, P * n:P * n + P].bitcast(FP8X4),
@@ -321,83 +327,77 @@ def tile_list_antenna_hour_urgency_kernel(tc, tab_words, tab_scales, offs, offs2
                                         rhs=codes.bitcast(FP8X4), rhs_scale=scales,
                                         start=(a == 0 and k == 0), stop=(a == 1 and k == len(blocks) - 1))
 
-        first_q = {}
+        def weave_pass0(j, u):
+            at = WEAVE * u
+            weave(z_b0[j][:, at:at + WEAVE, :], z_rows[0][:, :, HALF * j + at:HALF * j + at + WEAVE])
 
-        def quantise_first(j, tag):
-            w = FIRST_WIDTHS[j]
-            z_q0 = tile("z_q0_%d" % j, [P, w], U32, tag=tag)
-            z_s0 = tile("z_s0_%d" % j, [P, w], U8)
-            nc.vector.quantize_mx(out=z_q0[:].bitcast(FP8X4), scales=z_s0[:],
-                                  in_=z_b0[j][:].rearrange("p c t -> p (c t)"))
-            first_q[j] = (z_q0, z_s0)
+        def quantise_pass0(j, tag):
+            z_q0 = tile("z_q0_%d" % j, [P, HALF], U32, tag=tag)
+            z_s0 = tile("z_s0_%d" % j, [P, HALF], U8)
+            quantise(z_q0[:], z_s0[:], z_b0[j][:])
+            return z_q0, z_s0
 
-        def multiply_first(j):
-            z_q0, z_s0 = first_q[j]
-            for c in range(len(WIDTHS)):
-                at = STARTS[c] - FIRST_STARTS[j]
-                if 0 <= at < FIRST_WIDTHS[j]:
-                    multiply(0, c, z_q0[:, at:at + WIDTHS[c]], z_s0[:, at:at + WIDTHS[c]])
+        def multiply_pass0(j, z_q0, z_s0):
+            for cols in CHUNKS:
+                if cols.start // HALF == j:
+                    own = slice(cols.start - HALF * j, cols.stop - HALF * j)
+                    multiply(0, cols, z_q0[:, own], z_s0[:, own])
 
         def scatter_last(j):
-            cols = (slice(0, CUT), slice(CUT, S))[j]
-            nc.vector.tensor_tensor(page_b(LAST)[:].indirect(idx3[:, cols.start // 16:cols.stop // 16]), h2_last[j][:],
-                                    wgB[:, PACK - 1, cols], MULT)
+            nc.vector.tensor_tensor(page_b(LAST)[:].indirect(entries(idx3, LAST_PARTS[j])), h2_last[j][:],
+                                    wgB[:, PACK - 1, LAST_PARTS[j]], MULT)
 
-        def weave_first(j, u):
-            weave(z_b0[j][:, 256 * u:256 * u + 256, :], z_rows[0][:, :, FIRST_STARTS[j] + 256 * u:FIRST_STARTS[j] + 256 * u + 256])
-
-        nc.vector.tensor_tensor(z_flat(0), z_flat(0), l_b[0][:], MAX)
-        weave(w4_bs[0][:], w4_raw[0])
+        maximum(z_flat(0), z_flat(0), l_b[0][:])
         quantise_w4(0)
         for s in range(PACK):
             round_b(s)
             round_a(PACK + s)
             round_least(PACK + s)
         kept = tile("kept", [P, HALF], BF16)
-        cut = slice(2 * T2 + HALF, 3 * T2)
-        for cols in (slice(0, cut.start), cut, slice(cut.stop, PACK * T2)):
-            nc.vector.tensor_tensor(kept[:] if cols == cut else z_flat(1)[:, cols], z_flat(1)[:, cols], l_b[1][:, cols], MAX)
-        weave(w4_bs[1][:], w4_raw[1])
+        apart = slice(2 * T2 + HALF, 3 * T2)
+        for cols in (slice(0, apart.start), apart, slice(apart.stop, PACK * T2)):
+            maximum(kept[:] if cols == apart else z_flat(1)[:, cols], z_flat(1)[:, cols], l_b[1][:, cols])
         quantise_w4(1)
         round_b(LAST - 3)
         for j, u in ((1, 0), (1, 1), (0, 0)):
-            weave_first(j, u)
+            weave_pass0(j, u)
         round_b(LAST - 2)
-        nc.vector.tensor_tensor(z_flat(1)[:, 0:2 * T2], z_flat(1)[:, 0:2 * T2], b_b[1][:], MAX)
-        weave_first(0, 1)
-        quantise_first(0, "z_q0_0")
-        multiply_first(0)
-        for j, cols in enumerate((slice(0, 512), slice(512, 1024))):
-            b_6 = tile("b_b6_%d" % j, [P, cols.stop - cols.start], BF16)
-            nc.scalar.copy(b_6[:], page_b(LAST - 1)[:, cols])
-            nc.vector.tensor_tensor(z_slice(LAST - 1)[:, cols], (z_slice(LAST - 1)[:, cols], kept[:])[j], b_6[:], MAX)
+        maximum(z_flat(1)[:, 0:2 * T2], z_flat(1)[:, 0:2 * T2], b_b[1][:])
+        weave_pass0(0, 1)
+        multiply_pass0(0, *quantise_pass0(0, "z_q0_0"))
+        for j in range(2):
+            cols = slice(HALF * j, HALF * j + HALF)
+            b_half = tile("b_half%d" % j, [P, HALF], BF16)
+            nc.scalar.copy(b_half[:], page_b(LAST - 1)[:, cols])
+            maximum(z_slice(LAST - 1)[:, cols], (z_slice(LAST - 1)[:, cols], kept[:])[j], b_half[:])
+
         scatter_last(0)
-        quantise_first(1, "kept")
-        for c in range(3):
-            weave(z_b1[c][:], z_rows[1][:, :, chunk(c)])
-        h2_last.append(tile("h2_last1", [P, S - CUT], F32, tag="b_b6_1"))
-        nc.scalar.copy(h2_last[1][:], h2_acc[:, CUT:S])
-        o_acc.append(bank(7, "acc_o_7"))
-        for c in range(3, len(WIDTHS)):
-            weave(z_b1[c][:], z_rows[1][:, :, chunk(c)])
-        multiply_first(1)
+        second_half = quantise_pass0(1, "kept")
+        for c in range(WOVEN_AHEAD):
+            weave(z_b1[c][:], z_rows[1][:, :, CHUNKS[c]])
+        h2_last.append(tile("h2_last1", [P, width(LAST_PARTS[1])], F32, tag="b_half1"))
+        nc.scalar.copy(h2_last[1][:], h2_acc[:, LAST_PARTS[1]])
+        o_acc.append(bank(LAST, "acc_o_last"))
+        for c in range(WOVEN_AHEAD, len(CHUNKS)):
+            weave(z_b1[c][:], z_rows[1][:, :, CHUNKS[c]])
+        multiply_pass0(1, *second_half)
         scatter_last(1)
+
         def max_last(c):
             woven = z_b1[c][:, :, PACK - 1]
-            nc.vector.tensor_tensor(woven, page_b(LAST)[:, chunk(c)], woven, MAX)
+            maximum(woven, page_b(LAST)[:, CHUNKS[c]], woven)
 
         max_last(0)
-        for c in range(len(WIDTHS)):
-            if c + 1 < len(WIDTHS):
+        for c, cols in enumerate(CHUNKS):
+            if c + 1 < len(CHUNKS):
                 max_last(c + 1)
-            nc.vector.quantize_mx(out=z_q1[:, chunk(c)].bitcast(FP8X4), scales=z_s1[c][:],
-                                  in_=z_b1[c][:].rearrange("p c t -> p (c t)"))
-            multiply(1, c, z_q1[:, chunk(c)], z_s1[c][:])
-            for k, (b, blocks) in enumerate(banks(c)):
-                dst = o_sb[:, blocks.start:blocks.stop, chunk(c)]
-                src = o_acc[b][:].rearrange("p (n c) -> p n c", c=WIDTHS[c])
-                if c >= 3 and k == 1:
+            quantise(z_q1[:, cols], z_s1[c][:], z_b1[c][:])
+            multiply(1, cols, z_q1[:, cols], z_s1[c][:])
+            for k, (b, blocks) in enumerate(banks(cols)):
+                dst = o_sb[:, blocks.start:blocks.stop, cols]
+                src = o_acc[b][:].rearrange("p (n c) -> p n c", c=width(cols))
+                if c >= SHARED_FROM and k == 1:
                     nc.vector.tensor_copy(dst, src)
                 else:
                     nc.scalar.copy(dst, src)
-                nc.sync.dma_start(out_v[:, blocks.start:blocks.stop, chunk(c)], dst)
+                nc.sync.dma_start(out_v[:, blocks.start:blocks.stop, cols], dst)

@@ -72,18 +72,17 @@ def tile_list_antenna_hour_urgency_kernel(tc, tab_words, tab_scales, offs, offs2
         w1_p = [tile("w1_p%d" % h, [P, 2, 1024], U8, tag=("w4_raw0", "l_raw")[h]) for h in range(2)]
 
         nc.sync.dma_start(idx[:], offs)
-        nc.sync.dma_start(tab_s[0:32].bitcast(I32), tab_scales.rearrange("a q c -> (a q) c").bitcast(I32))
-        nc.sync.dma_start(ws_raw[0:32].bitcast(I32), w1_scales.rearrange("a q c -> (a q) c").bitcast(I32))
-        nc.gpsimd.memset(ws_raw[32:64].bitcast(I32), 0)
+        nc.scalar.dma_start(tab_s[0:32].bitcast(I32), tab_scales.rearrange("a q c -> (a q) c").bitcast(I32))
+        nc.scalar.dma_start(ws_raw[0:32].bitcast(I32), w1_scales.rearrange("a q c -> (a q) c").bitcast(I32))
         nc.sync.dma_start(ws_raw[48:64].bitcast(I32), w3_scales[0].bitcast(I32))
-        nc.sync.dma_start(idx2[:], offs2)
         nc.sync.dma_start(w1_raw[:].bitcast(I32), w1_words.rearrange("a p b -> p a b").bitcast(I32))
+        nc.sync.dma_start(idx2[:], offs2)
         for a in range(2):
             nc.sync.dma_start(tab[a][:], tab_words[a].rearrange("p t i -> p (t i)").bitcast(I32),
                               max_dma_last_dim=TABLE_PIECE)
 
-        for raw, rows in ((tab_s, slice(32, 64)), (tab_s, slice(64, 128)), (ws_raw, slice(64, 128))):
-            nc.gpsimd.memset(raw[rows].bitcast(I32), 0)
+        for unloaded in (tab_s[32:64], tab_s[64:128], ws_raw[32:48], ws_raw[64:128]):
+            nc.gpsimd.memset(unloaded.bitcast(I32), 0)
 
         pageA = []
 

@@ -215,10 +215,6 @@ def tile_list_antenna_hour_urgency_kernel(tc, tab_words, tab_scales, offs, offs2
                            w2_raw[:, a].rearrange("p j (m t) -> p m t j", t=PACK))
             nc.vector.quantize_mx(out=w2_q[:, a, :].bitcast(FP8X4), scales=w2_s[:, a, :], in_=w2_b[:])
 
-        w3_p = tile("w3_p", [P, H], I32)
-        nc.vector.tensor_copy(w3_p[:].rearrange("p (h t u i) -> p h u t i", h=2, t=PACK, i=4),
-                              w3_raw[:].rearrange("p (h u i t) -> p h u t i", h=2, t=PACK, i=4))
-
         w4_q = [tile("w4_q%d" % a, [P, N], U32) for a in range(2)]
         w4_s = [tile("w4_s%d" % a, [P, N], U8) for a in range(2)]
 
@@ -258,6 +254,10 @@ def tile_list_antenna_hour_urgency_kernel(tc, tab_words, tab_scales, offs, offs2
         for page in pageB:
             nc.gpsimd.memset(page[:], 0.0)
         round_least(0)
+
+        w3_p = tile("w3_p", [P, H], U32)
+        nc.scalar.copy(w3_p[:].rearrange("p (h t u i) -> p h u t i", h=2, t=PACK, i=4),
+                       w3_raw[:].bitcast(U32).rearrange("p (h u i t) -> p h u t i", h=2, t=PACK, i=4))
 
         d_rows = tile("d_rows", [P, PACK, S], BF16)
         d_b = tile("d_b", [P, S, PACK], BF16)
@@ -370,26 +370,24 @@ def tile_list_antenna_hour_urgency_kernel(tc, tab_words, tab_scales, offs, offs2
             nc.scalar.copy(b_half[:], page_b(LAST - 1)[:, cols])
             maximum(z_slice(LAST - 1)[:, cols], (z_slice(LAST - 1)[:, cols], kept[:])[j], b_half[:])
 
+        def weave_pair(engine_copy, c, pair):
+            engine_copy(z_b1[c][:, :, pair], z_rows[1][:, pair, CHUNKS[c]].rearrange("p i c -> p c i"))
+
         scatter_last(0)
         second_half = quantise_pass0(1, "kept")
-        for c in range(WOVEN_AHEAD):
-            weave(z_b1[c][:], z_rows[1][:, :, CHUNKS[c]])
+        weave(z_b1[0][:], z_rows[1][:, :, CHUNKS[0]])
+        for c in range(1, WOVEN_AHEAD + 1):
+            weave_pair(nc.scalar.copy, c, slice(0, 2))
         h2_last.append(tile("h2_last1", [P, width(LAST_PARTS[1])], F32, tag="b_half1"))
         nc.scalar.copy(h2_last[1][:], h2_acc[:, LAST_PARTS[1]])
         o_acc.append(bank(LAST, "acc_o_last"))
-        for c in range(WOVEN_AHEAD, len(CHUNKS)):
-            weave(z_b1[c][:], z_rows[1][:, :, CHUNKS[c]])
+        for c in range(WOVEN_AHEAD + 1, len(CHUNKS)):
+            weave_pair(nc.scalar.copy, c, slice(0, 2))
         multiply_pass0(1, *second_half)
         scatter_last(1)
 
-        def max_last(c):
-            woven = z_b1[c][:, :, PACK - 1]
-            maximum(woven, page_b(LAST)[:, CHUNKS[c]], woven)
-
-        max_last(0)
-        for c, cols in enumerate(CHUNKS):
-            if c + 1 < len(CHUNKS):
-                max_last(c + 1)
+        def finish(c):
+            cols = CHUNKS[c]
             quantise(z_q1[:, cols], z_s1[c][:], z_b1[c][:])
             multiply(1, cols, z_q1[:, cols], z_s1[c][:])
             for k, (b, blocks) in enumerate(banks(cols)):
@@ -400,3 +398,19 @@ def tile_list_antenna_hour_urgency_kernel(tc, tab_words, tab_scales, offs, offs2
                 else:
                     nc.scalar.copy(dst, src)
                 nc.sync.dma_start(out_v[:, blocks.start:blocks.stop, cols], dst)
+
+        late = slice(CHUNKS[2].start, T2)
+        b_late = tile("b_late", [P, width(late)], BF16)
+        nc.scalar.copy(b_late[:], page_b(LAST)[:, late])
+        woven = z_b1[0][:, :, PACK - 1]
+        maximum(woven, page_b(LAST)[:, CHUNKS[0]], woven)
+        maximum(z_slice(LAST)[:, CHUNKS[1]], page_b(LAST)[:, CHUNKS[1]], z_slice(LAST)[:, CHUNKS[1]])
+        finish(0)
+        weave_pair(nc.vector.tensor_copy, 1, slice(2, 4))
+        maximum(z_slice(LAST)[:, late], z_slice(LAST)[:, late], b_late[:])
+        finish(1)
+        weave_pair(nc.vector.tensor_copy, 2, slice(2, 4))
+        for c in range(2, len(CHUNKS)):
+            if c + 1 < len(CHUNKS):
+                weave_pair(nc.vector.tensor_copy, c + 1, slice(2, 4))
+            finish(c)

@@ -92,8 +92,6 @@ def tile_list_antenna_hour_urgency_kernel(tc, tab_words, tab_scales, offs, offs2
 
         new_page_a("pageA0")
         nc.gpsimd.memset(scale[1][:].bitcast(I32), 0)
-        warm = tile("warm", [P, 16], F32)
-        nc.scalar.copy(warm[:, 0:1], pageA[0][:, 0:1])
 
         nc.vector.tensor_copy(v_g[:], tab_s[:].indirect(idx[:]))
         nc.vector.tensor_copy(ws_p[0].rearrange("p (h t m) -> p h t m", h=2, t=PACK),

@@ -25,7 +25,7 @@ LAST = SLICES - 1
 A_PAGES = 4
 B_PAGES = 2
 QUADRANTS = (0, 2, 1, 3)
-TABLE_PIECE = 2048
+TABLE_PIECE = 4096
 LIST_HALVES = (slice(0, S // 2), slice(S // 2, S))
 LAST_PARTS = (slice(0, 384), slice(384, S))
 HALF = T2 // 2

@@ -31,7 +31,8 @@ LAST_PARTS = (slice(0, 384), slice(384, S))
 HALF = T2 // 2
 WEAVE = 256
 CHUNKS = (slice(0, 128), slice(128, 384), slice(384, 512), slice(512, 768), slice(768, 1024))
-WOVEN_AHEAD = 2
+WOVEN_AHEAD = 3
+EARLY, LATE = slice(0, 2), slice(2, 4)
 SHARED_FROM = 3
 
 
@@ -350,10 +351,7 @@ def tile_list_antenna_hour_urgency_kernel(tc, tab_words, tab_scales, offs, offs2
             round_b(s)
             round_a(PACK + s)
             round_least(PACK + s)
-        kept = tile("kept", [P, HALF], BF16)
-        apart = slice(2 * T2 + HALF, 3 * T2)
-        for cols in (slice(0, apart.start), apart, slice(apart.stop, PACK * T2)):
-            maximum(kept[:] if cols == apart else z_flat(1)[:, cols], z_flat(1)[:, cols], l_b[1][:, cols])
+        maximum(z_flat(1), z_flat(1), l_b[1][:])
         quantise_w4(1)
         round_b(LAST - 3)
         for j, u in ((1, 0), (1, 1), (0, 0)):
@@ -366,23 +364,26 @@ def tile_list_antenna_hour_urgency_kernel(tc, tab_words, tab_scales, offs, offs2
             cols = slice(HALF * j, HALF * j + HALF)
             b_half = tile("b_half%d" % j, [P, HALF], BF16)
             nc.scalar.copy(b_half[:], page_b(LAST - 1)[:, cols])
-            maximum(z_slice(LAST - 1)[:, cols], (z_slice(LAST - 1)[:, cols], kept[:])[j], b_half[:])
+            maximum(z_slice(LAST - 1)[:, cols], z_slice(LAST - 1)[:, cols], b_half[:])
 
-        def weave_pair(engine_copy, c, pair):
-            engine_copy(z_b1[c][:, :, pair], z_rows[1][:, pair, CHUNKS[c]].rearrange("p i c -> p c i"))
+        def weave_pair(copy, c, pair):
+            copy(z_b1[c][:, :, pair], z_rows[1][:, pair, CHUNKS[c]].rearrange("p i c -> p c i"))
 
         scatter_last(0)
-        second_half = quantise_pass0(1, "kept")
+        second_half = quantise_pass0(1, "b_half1")
         weave(z_b1[0][:], z_rows[1][:, :, CHUNKS[0]])
-        for c in range(1, WOVEN_AHEAD + 1):
-            weave_pair(nc.scalar.copy, c, slice(0, 2))
-        h2_last.append(tile("h2_last1", [P, width(LAST_PARTS[1])], F32, tag="b_half1"))
+        for c in range(1, WOVEN_AHEAD):
+            weave_pair(nc.scalar.copy, c, EARLY)
+        h2_last.append(tile("h2_last1", [P, width(LAST_PARTS[1])], F32, tag="b_half0"))
         nc.scalar.copy(h2_last[1][:], h2_acc[:, LAST_PARTS[1]])
         o_acc.append(bank(LAST, "acc_o_last"))
-        for c in range(WOVEN_AHEAD + 1, len(CHUNKS)):
-            weave_pair(nc.scalar.copy, c, slice(0, 2))
+        for c in range(WOVEN_AHEAD, len(CHUNKS)):
+            weave_pair(nc.scalar.copy, c, EARLY)
         multiply_pass0(1, *second_half)
         scatter_last(1)
+
+        def max_in_row(cols, page_part):
+            maximum(z_slice(LAST)[:, cols], page_part, z_slice(LAST)[:, cols])
 
         def finish(c):
             cols = CHUNKS[c]
@@ -397,18 +398,17 @@ def tile_list_antenna_hour_urgency_kernel(tc, tab_words, tab_scales, offs, offs2
                     nc.scalar.copy(dst, src)
                 nc.sync.dma_start(out_v[:, blocks.start:blocks.stop, cols], dst)
 
-        late = slice(CHUNKS[2].start, T2)
-        b_late = tile("b_late", [P, width(late)], BF16)
-        nc.scalar.copy(b_late[:], page_b(LAST)[:, late])
+        b_late = tile("b_late", [P, HALF], BF16)
+        nc.scalar.copy(b_late[:], page_b(LAST)[:, HALF:T2])
         woven = z_b1[0][:, :, PACK - 1]
         maximum(woven, page_b(LAST)[:, CHUNKS[0]], woven)
-        maximum(z_slice(LAST)[:, CHUNKS[1]], page_b(LAST)[:, CHUNKS[1]], z_slice(LAST)[:, CHUNKS[1]])
-        finish(0)
-        weave_pair(nc.vector.tensor_copy, 1, slice(2, 4))
-        maximum(z_slice(LAST)[:, late], z_slice(LAST)[:, late], b_late[:])
-        finish(1)
-        weave_pair(nc.vector.tensor_copy, 2, slice(2, 4))
-        for c in range(2, len(CHUNKS)):
-            if c + 1 < len(CHUNKS):
-                weave_pair(nc.vector.tensor_copy, c + 1, slice(2, 4))
+        for c in (1, 2):
+            max_in_row(CHUNKS[c], page_b(LAST)[:, CHUNKS[c]])
+            finish(c - 1)
+            weave_pair(nc.vector.tensor_copy, c, LATE)
+        max_in_row(slice(HALF, T2), b_late[:])
+        finish(2)
+        for c in (3, 4):
+            weave_pair(nc.vector.tensor_copy, c, LATE)
+        for c in (3, 4):
             finish(c)

@@ -25,7 +25,6 @@ LAST = SLICES - 1
 A_PAGES = 4
 B_PAGES = 2
 QUADRANTS = (0, 2, 1, 3)
-TABLE_PIECE = 4096
 LIST_HALVES = (slice(0, S // 2), slice(S // 2, S))
 LAST_PARTS = (slice(0, 384), slice(384, S))
 HALF = T2 // 2
@@ -79,8 +78,7 @@ def tile_list_antenna_hour_urgency_kernel(tc, tab_words, tab_scales, offs, offs2
         nc.sync.dma_start(w1_raw[:].bitcast(I32), w1_words.rearrange("a p b -> p a b").bitcast(I32))
         nc.sync.dma_start(idx2[:], offs2)
         for a in range(2):
-            nc.sync.dma_start(tab[a][:], tab_words[a].rearrange("p t i -> p (t i)").bitcast(I32),
-                              max_dma_last_dim=TABLE_PIECE)
+            nc.sync.dma_start(tab[a][:], tab_words[a].rearrange("p t i -> p (t i)").bitcast(I32))
 
         for unloaded in (tab_s[32:64], tab_s[64:128], ws_raw[32:48], ws_raw[64:128]):
             nc.gpsimd.memset(unloaded.bitcast(I32), 0)

@@ -114,7 +114,7 @@ def tile_list_antenna_hour_urgency_kernel(tc, tab_words, tab_scales, offs, offs2
         wgA_bias = tile("wgA", [P, PACK * S + 16], F32)
         wgA = wgA_bias[:, 0:PACK * S].rearrange("p (t j) -> p t j", t=PACK)
         bias = wgA_bias[:, PACK * S:PACK * S + PACK]
-        w2_raw = tile("w2_raw", [P, 2, PACK, R], F32)
+        w2_raw = [tile("w2_raw%d" % a, [P, PACK, R], F32) for a in range(2)]
 
         def load_wg(dst, wg, cuts):
             for lo, hi in zip(cuts, cuts[1:]):
@@ -127,11 +127,11 @@ def tile_list_antenna_hour_urgency_kernel(tc, tab_words, tab_scales, offs, offs2
         w2_v = w2.rearrange("(a p j) m -> a p j m", a=2, j=PACK)
         w4_v = w4.rearrange("(a p j) n -> a p j n", a=2, j=PACK)
         for a in range(2):
-            nc.sync.dma_start(w2_raw[:, a], w2_v[a])
+            nc.sync.dma_start(w2_raw[a][:], w2_v[a])
         nc.sync.dma_start(bias, b2.rearrange("(p t) -> p t", t=PACK))
 
         h1_acc = [bank(s, "acc_h1_%d" % s) for s in range(LAST)]
-        h1 = [tile("h1_%d" % s, [P, S], F32) for s in range(SLICES)]
+        h1 = [tile("h1_%d" % s, [P, S], F32, tag="w2_raw0" if s == A_PAGES - 1 else None) for s in range(SLICES)]
         h2 = [tile("h2_%d" % s, [P, S], F32) for s in range(LAST)]
         h2_last = [tile("h2_last0", [P, width(LAST_PARTS[0])], F32)]
 
@@ -155,7 +155,8 @@ def tile_list_antenna_hour_urgency_kernel(tc, tab_words, tab_scales, offs, offs2
                 h1_acc.append(bank(LAST, "acc_h1_last"))
             for a in (1, 0):
                 h1_pass(h1_acc[s][:], s, a, slice(0, S), a == 1, a == 0)
-            nc.scalar.copy(h1[s][:], h1_acc[s][:])
+            if s != A_PAGES - 1:
+                nc.scalar.copy(h1[s][:], h1_acc[s][:])
             if s == 1:
                 h1_first_slice(bank(LAST, "acc_h1_0b"), LIST_HALVES[1], (1, 0))
 
@@ -189,7 +190,6 @@ def tile_list_antenna_hour_urgency_kernel(tc, tab_words, tab_scales, offs, offs2
             nc.sync.dma_start(ws_p[0][32 * q + 4:32 * q + 8].bitcast(I32), ws_p[0][48 + 4 * q:52 + 4 * q].bitcast(I32))
 
         new_page_a("h1_1")
-        scatter_a(A_PAGES - 1)
 
         wgB_w4 = tile("wgB_w4", [P, 2 * PACK, S], F32, tag="h1_2")
         wgB = wgB_w4[:, 0:PACK, :]
@@ -204,13 +204,25 @@ def tile_list_antenna_hour_urgency_kernel(tc, tab_words, tab_scales, offs, offs2
         for s in range(LAST - 1, SLICES):
             load_least(s)
 
-        w2_q = tile("w2_q", [P, 2, R], U32)
-        w2_s = tile("w2_s", [P, 2, R], U8)
+        w2_q = [tile("w2_q%d" % a, [P, R], U32) for a in range(2)]
+        w2_s = [tile("w2_s%d" % a, [P, R], U8) for a in range(2)]
+
+        def d_pass(t, a):
+            nc.tensor.matmul_mx(out=d_acc[t][:], lhsT=w2_q[a][:, P * t:P * t + P].bitcast(FP8X4),
+                                lhsT_scale=w2_s[a][:, P * t:P * t + P],
+                                rhs=v_w[a][:].bitcast(FP8X4), rhs_scale=v_s[a], start=(a == 0), stop=(a == 1))
+
         for a in range(2):
             w2_b = tile("w2_b%d" % a, [P, PACK * R], BF16)
             nc.scalar.copy(w2_b[:].rearrange("p (t m j) -> p m t j", t=PACK, j=PACK),
-                           w2_raw[:, a].rearrange("p j (m t) -> p m t j", t=PACK))
-            nc.vector.quantize_mx(out=w2_q[:, a, :].bitcast(FP8X4), scales=w2_s[:, a, :], in_=w2_b[:])
+                           w2_raw[a][:].rearrange("p j (m t) -> p m t j", t=PACK))
+            nc.vector.quantize_mx(out=w2_q[a][:].bitcast(FP8X4), scales=w2_s[a][:], in_=w2_b[:])
+            if a == 0:
+                nc.scalar.copy(h1[A_PAGES - 1][:], h1_acc[A_PAGES - 1][:])
+                scatter_a(A_PAGES - 1)
+                d_acc = [bank(t, "acc_d_%d" % t) for t in range(PACK)]
+                for t in range(PACK):
+                    d_pass(t, 0)
 
         w4_q = [tile("w4_q%d" % a, [P, N], U32) for a in range(2)]
         w4_s = [tile("w4_s%d" % a, [P, N], U8) for a in range(2)]
@@ -226,7 +238,7 @@ def tile_list_antenna_hour_urgency_kernel(tc, tab_words, tab_scales, offs, offs2
             weave(w4_b[:], w4_raw[a])
             quantise(w4_q[a][:], w4_s[a][:], w4_b[:])
 
-        z_rows = [tile("z_rows0", [P, PACK, T2], BF16, tag="w2_raw")]
+        z_rows = [tile("z_rows0", [P, PACK, T2], BF16, tag="w2_raw1")]
         l_b = [tile("l_b%d" % a, [P, PACK * T2], BF16, tag=("w2_b1", "l_b1")[a]) for a in range(2)]
 
         def z_slice(s):
@@ -261,12 +273,8 @@ def tile_list_antenna_hour_urgency_kernel(tc, tab_words, tab_scales, offs, offs2
         d_q = tile("d_q", [P, S], U32)
         d_s = tile("d_s", [P, S], U8)
         for t in range(PACK):
-            acc = bank(t, "acc_d_%d" % t)
-            for a in range(2):
-                nc.tensor.matmul_mx(out=acc[:], lhsT=w2_q[:, a, P * t:P * t + P].bitcast(FP8X4),
-                                    lhsT_scale=w2_s[:, a, P * t:P * t + P],
-                                    rhs=v_w[a][:].bitcast(FP8X4), rhs_scale=v_s[a], start=(a == 0), stop=(a == 1))
-            nc.scalar.activation(d_rows[:, t, :], acc[:], RELU, bias=bias[:, t:t + 1])
+            d_pass(t, 1)
+            nc.scalar.activation(d_rows[:, t, :], d_acc[t][:], RELU, bias=bias[:, t:t + 1])
         round_least(1)
         weave(d_b[:], d_rows[:])
         quantise(d_q[:], d_s[:], d_b[:])
@@ -345,9 +353,11 @@ def tile_list_antenna_hour_urgency_kernel(tc, tab_words, tab_scales, offs, offs2
 
         maximum(z_flat(0), z_flat(0), l_b[0][:])
         quantise_w4(0)
+        round_a(PACK)
         for s in range(PACK):
             round_b(s)
-            round_a(PACK + s)
+            if s + 1 < PACK:
+                round_a(PACK + s + 1)
             round_least(PACK + s)
         maximum(z_flat(1), z_flat(1), l_b[1][:])
         quantise_w4(1)

@@ -60,9 +60,9 @@ def tile_list_antenna_hour_urgency_kernel(tc, tab_words, tab_scales, offs, offs2
         idx = tile("idx", [P, S // 16], U16)
         idx2 = tile("idx2", [P, S // 16], U16)
         idx3 = tile("idx3", [P, S // 16], U16)
-        tab = [tile("tab%d" % a, [P, T], I32, tag=("w3_p", "pageA2")[a]) for a in range(2)]
+        tab = [tile("tab%d" % a, [P, T], I32, tag=("w3_p", "pageA1")[a]) for a in range(2)]
         tab_s = tile("tab_s", [P, T], U8)
-        w1_raw = tile("w1_raw", [P, 2, 2 * H], U8, tag="pageA1")
+        w1_raw = tile("w1_raw", [P, 2, 2 * H], U8)
         ws_raw = tile("ws_raw", [P, H], U8)
         v_w = [tile("v_w%d" % a, [P, S], U32) for a in range(2)]
         v_g = tile("v_g", [P, S], U8)
@@ -106,10 +106,9 @@ def tile_list_antenna_hour_urgency_kernel(tc, tab_words, tab_scales, offs, offs2
             nc.vector.tensor_copy(
                 w1_p[h][:].bitcast(U16).rearrange("p a (t m) -> p a t m", t=PACK),
                 w1_raw[:].bitcast(U16)[:, :, 512 * h:512 * h + 512].rearrange("p a (m t) -> p a t m", t=PACK))
-        new_page_a("pageA1")
         for part in LIST_HALVES:
             nc.vector.tensor_copy(v_w[1][:, part], tab[1][:].bitcast(U32).indirect(entries(idx, part)))
-        new_page_a("pageA2")
+        new_page_a("pageA1")
 
         wgA_bias = tile("wgA", [P, PACK * S + 16], F32)
         wgA = wgA_bias[:, 0:PACK * S].rearrange("p (t j) -> p t j", t=PACK)
@@ -174,7 +173,9 @@ def tile_list_antenna_hour_urgency_kernel(tc, tab_words, tab_scales, offs, offs2
 
         scatter_a(0, LIST_HALVES[0])
         scatter_a(1)
+        new_page_a("h1_1")
         scatter_a(0, LIST_HALVES[1])
+        new_page_a("h1_0")
         scatter_a(2)
 
         l_raw = tile("l_raw", [P, SLICES, T2], F32)
@@ -184,12 +185,10 @@ def tile_list_antenna_hour_urgency_kernel(tc, tab_words, tab_scales, offs, offs2
             nc.sync.dma_start(l_raw[:, s, :], least_v[s // PACK, s % PACK])
 
         load_least(0)
-        w3_raw = tile("w3_raw", [P, H], I32, tag="h1_0")
+        w3_raw = tile("w3_raw", [P, H], I32, tag="w1_raw")
         nc.sync.dma_start(w3_raw[:], w3_words[0].rearrange("p c i -> p (c i)").bitcast(I32))
         for q in range(4):
             nc.sync.dma_start(ws_p[0][32 * q + 4:32 * q + 8].bitcast(I32), ws_p[0][48 + 4 * q:52 + 4 * q].bitcast(I32))
-
-        new_page_a("h1_1")
 
         wgB_w4 = tile("wgB_w4", [P, 2 * PACK, S], F32, tag="h1_2")
         wgB = wgB_w4[:, 0:PACK, :]

from contextlib import ExitStack

import concourse.mybir as mybir

K, R, H, N, T, S, T2 = 1024, 512, 1024, 512, 2048, 512, 1024
FLOPS = 2 * (K * H * S + K * R * S + R * H * S + H * N * T2)

F32 = mybir.dt.float32
BF16 = mybir.dt.bfloat16
I32 = mybir.dt.int32
U32 = mybir.dt.uint32
U16 = mybir.dt.uint16
U8 = mybir.dt.uint8
FP8X4 = mybir.dt.float8_e4m3fn_x4
FP4X4 = mybir.dt.float4_e2m1fn_x4
MULT = mybir.AluOpType.mult
MAX = mybir.AluOpType.max
RELU = mybir.ActivationFunctionType.Relu

P = 128
BANK = 512
PACK = 4
SLICES = H // P
LAST = SLICES - 1
A_PAGES = 4
B_PAGES = 2
QUADRANTS = (0, 2, 1, 3)
LIST_HALVES = (slice(0, S // 2), slice(S // 2, S))
LAST_PARTS = (slice(0, 384), slice(384, S))
HALF = T2 // 2
WEAVE = 256
CHUNKS = (slice(0, 128), slice(128, 384), slice(384, 512), slice(512, 768), slice(768, 1024))
WOVEN_AHEAD = 3
EARLY, LATE = slice(0, 2), slice(2, 4)
SHARED_FROM = 3


def width(cols):
    return cols.stop - cols.start


def entries(idx, part):
    return idx[:, part.start // 16:part.stop // 16]


def tile_list_antenna_hour_urgency_kernel(tc, tab_words, tab_scales, offs, offs2, offs3, w1_words,
                                                       w1_scales, w2, b2, w3_words, w3_scales, wg1, wg2, least, w4,
                                                       out):
    nc = tc.nc
    with ExitStack() as ctx:
        sb = ctx.enter_context(tc.tile_pool(name="sb", bufs=1))
        ps = ctx.enter_context(tc.psum_pool(name="ps", bufs=1))

        def tile(name, shape, dtype, tag=None):
            return sb.tile(shape, dtype, name=name, tag=tag or name, align_bytes=64)

        def bank(b, name):
            return ps.tile([P, BANK], F32, name=name, tag="bank%d" % b)

        idx = tile("idx", [P, S // 16], U16)
        idx2 = tile("idx2", [P, S // 16], U16)
        idx3 = tile("idx3", [P, S // 16], U16)
        tab = [tile("tab%d" % a, [P, T], I32, tag=("w3_p", "pageA1")[a]) for a in range(2)]
        tab_s = tile("tab_s", [P, T], U8)
        w1_raw = tile("w1_raw", [P, 2, 2 * H], U8)
        ws_raw = tile("ws_raw", [P, H], U8)
        v_w = [tile("v_w%d" % a, [P, S], U32) for a in range(2)]
        v_g = tile("v_g", [P, S], U8)
        scale = [tile("scale%d" % a, [P, S + H], U8) for a in range(2)]
        v_s = [scale[a][:, 0:S] for a in range(2)]
        ws_p = [scale[a][:, S:S + H] for a in range(2)]
        w1_p = [tile("w1_p%d" % h, [P, 2, 1024], U8, tag=("w4_raw0", "l_raw")[h]) for h in range(2)]

        nc.sync.dma_start(idx[:], offs)
        nc.scalar.dma_start(tab_s[0:32].bitcast(I32), tab_scales.rearrange("a q c -> (a q) c").bitcast(I32))
        nc.scalar.dma_start(ws_raw[0:32].bitcast(I32), w1_scales.rearrange("a q c -> (a q) c").bitcast(I32))
        nc.sync.dma_start(ws_raw[48:64].bitcast(I32), w3_scales[0].bitcast(I32))
        nc.sync.dma_start(w1_raw[:].bitcast(I32), w1_words.rearrange("a p b -> p a b").bitcast(I32))
        nc.sync.dma_start(idx2[:], offs2)
        for a in range(2):
            nc.sync.dma_start(tab[a][:], tab_words[a].rearrange("p t i -> p (t i)").bitcast(I32))

        for unloaded in (tab_s[32:64], tab_s[64:128], ws_raw[32:48], ws_raw[64:128]):
            nc.gpsimd.memset(unloaded.bitcast(I32), 0)

        pageA = []

        def new_page_a(tag):
            pageA.append(tile("pageA%d" % len(pageA), [P, T2], F32, tag=tag))
            nc.gpsimd.memset(pageA[-1][:], 0.0)

        new_page_a("pageA0")
        nc.gpsimd.memset(scale[1][:].bitcast(I32), 0)

        nc.vector.tensor_copy(v_g[:], tab_s[:].indirect(idx[:]))
        nc.vector.tensor_copy(ws_p[0].rearrange("p (h t m) -> p h t m", h=2, t=PACK),
                              ws_raw[:].rearrange("p (h m t) -> p h t m", h=2, t=PACK))
        nc.vector.tensor_copy(v_s[0].bitcast(I32), v_g[:].bitcast(I32))
        for a in range(2):
            for q in range(1 - a, 4):
                row = 16 * a + 4 * q
                nc.scalar.dma_start(scale[a][32 * q:32 * q + 4].bitcast(I32), scale[0][row:row + 4].bitcast(I32))

        nc.vector.tensor_copy(v_w[0][:], tab[0][:].bitcast(U32).indirect(idx[:]))
        for h in range(2):
            nc.vector.tensor_copy(
                w1_p[h][:].bitcast(U16).rearrange("p a (t m) -> p a t m", t=PACK),
                w1_raw[:].bitcast(U16)[:, :, 512 * h:512 * h + 512].rearrange("p a (m t) -> p a t m", t=PACK))
        for part in LIST_HALVES:
            nc.vector.tensor_copy(v_w[1][:, part], tab[1][:].bitcast(U32).indirect(entries(idx, part)))
        new_page_a("pageA1")

        wgA_bias = tile("wgA", [P, PACK * S + 16], F32)
        wgA = wgA_bias[:, 0:PACK * S].rearrange("p (t j) -> p t j", t=PACK)
        bias = wgA_bias[:, PACK * S:PACK * S + PACK]
        w2_raw = [tile("w2_raw%d" % a, [P, PACK, R], F32) for a in range(2)]

        def load_wg(dst, wg, cuts):
            for lo, hi in zip(cuts, cuts[1:]):
                for q in QUADRANTS:
                    nc.sync.dma_start(dst[32 * q:32 * q + 32, lo:hi],
                                      wg.rearrange("(p t) j -> p (t j)", t=PACK)[:, lo:hi])

        load_wg(wgA_bias, wg1, (0, S // 2, 2 * S, PACK * S))
        nc.sync.dma_start(idx3[:], offs3)
        w2_v = w2.rearrange("(a p j) m -> a p j m", a=2, j=PACK)
        w4_v = w4.rearrange("(a p j) n -> a p j n", a=2, j=PACK)
        for a in range(2):
            nc.sync.dma_start(w2_raw[a][:], w2_v[a])
        nc.sync.dma_start(bias, b2.rearrange("(p t) -> p t", t=PACK))

        h1_acc = [bank(s, "acc_h1_%d" % s) for s in range(LAST)]
        h1 = [tile("h1_%d" % s, [P, S], F32, tag="w2_raw0" if s == A_PAGES - 1 else None) for s in range(SLICES)]
        h2 = [tile("h2_%d" % s, [P, S], F32) for s in range(LAST)]
        h2_last = [tile("h2_last0", [P, width(LAST_PARTS[0])], F32)]

        def h1_pass(acc, s, a, cols, start, stop):
            h, t = divmod(s, PACK)
            nc.tensor.matmul_mx(out=acc, lhsT=w1_p[h][:, a, 256 * t:256 * t + 256].bitcast(FP4X4),
                                lhsT_scale=ws_p[a][:, P * s:P * s + P],
                                rhs=v_w[a][:, cols].bitcast(FP8X4), rhs_scale=v_s[a][:, cols],
                                start=start, stop=stop)

        def h1_first_slice(acc, part, passes):
            for a in passes:
                for u in range(2):
                    h1_pass(acc[:, P * u:P * u + P], 0, a, slice(part.start + P * u, part.start + P * u + P),
                            a == passes[0] and u == 0, a == passes[1] and u == 1)
            nc.scalar.copy(h1[0][:, part], acc[:, 0:width(part)])

        h1_first_slice(h1_acc[0], LIST_HALVES[0], (0, 1))
        for s in range(1, SLICES):
            if s == LAST:
                h1_acc.append(bank(LAST, "acc_h1_last"))
            for a in (1, 0):
                h1_pass(h1_acc[s][:], s, a, slice(0, S), a == 1, a == 0)
            if s != A_PAGES - 1:
                nc.scalar.copy(h1[s][:], h1_acc[s][:])
            if s == 1:
                h1_first_slice(bank(LAST, "acc_h1_0b"), LIST_HALVES[1], (1, 0))

        w4_raw0 = tile("w4_raw0", [P, PACK, N], F32)

        def scatter_a(s, part=slice(0, S)):
            nc.vector.tensor_tensor(pageA[s % A_PAGES][:].indirect(entries(idx2, part)), h1[s][:, part],
                                    wgA[:, s % PACK, part], MULT)

        def page_b(s):
            return pageB[min(s, LAST - 1) % B_PAGES]

        def scatter_b(s):
            nc.vector.tensor_tensor(page_b(s)[:].indirect(idx3[:]), h2[s][:], wgB[:, s % PACK, :], MULT)

        scatter_a(0, LIST_HALVES[0])
        scatter_a(1)
        new_page_a("h1_1")
        scatter_a(0, LIST_HALVES[1])
        new_page_a("h1_0")
        scatter_a(2)

        l_raw = tile("l_raw", [P, SLICES, T2], F32)
        least_v = least.rearrange("(a p t) c -> a t p c", a=2, t=PACK)

        def load_least(s):
            nc.sync.dma_start(l_raw[:, s, :], least_v[s // PACK, s % PACK])

        load_least(0)
        w3_raw = tile("w3_raw", [P, H], I32, tag="w1_raw")
        nc.sync.dma_start(w3_raw[:], w3_words[0].rearrange("p c i -> p (c i)").bitcast(I32))
        for q in range(4):
            nc.sync.dma_start(ws_p[0][32 * q + 4:32 * q + 8].bitcast(I32), ws_p[0][48 + 4 * q:52 + 4 * q].bitcast(I32))

        wgB_w4 = tile("wgB_w4", [P, 2 * PACK, S], F32, tag="h1_2")
        wgB = wgB_w4[:, 0:PACK, :]
        w4_raw = [w4_raw0[:], wgB_w4[:, PACK:2 * PACK, :]]
        for s in range(1, PACK):
            load_least(s)
        nc.sync.dma_start(w4_raw[0], w4_v[0])
        load_wg(wgB.rearrange("p t j -> p (t j)"), wg2, (0, B_PAGES * S, PACK * S))
        for s in range(PACK, LAST - 1):
            load_least(s)
        nc.sync.dma_start(w4_raw[1], w4_v[1])
        for s in range(LAST - 1, SLICES):
            load_least(s)

        w2_q = [tile("w2_q%d" % a, [P, R], U32) for a in range(2)]
        w2_s = [tile("w2_s%d" % a, [P, R], U8) for a in range(2)]

        def d_pass(t, a):
            nc.tensor.matmul_mx(out=d_acc[t][:], lhsT=w2_q[a][:, P * t:P * t + P].bitcast(FP8X4),
                                lhsT_scale=w2_s[a][:, P * t:P * t + P],
                                rhs=v_w[a][:].bitcast(FP8X4), rhs_scale=v_s[a], start=(a == 0), stop=(a == 1))

        for a in range(2):
            w2_b = tile("w2_b%d" % a, [P, PACK * R], BF16)
            nc.scalar.copy(w2_b[:].rearrange("p (t m j) -> p m t j", t=PACK, j=PACK),
                           w2_raw[a][:].rearrange("p j (m t) -> p m t j", t=PACK))
            nc.vector.quantize_mx(out=w2_q[a][:].bitcast(FP8X4), scales=w2_s[a][:], in_=w2_b[:])
            if a == 0:
                nc.scalar.copy(h1[A_PAGES - 1][:], h1_acc[A_PAGES - 1][:])
                scatter_a(A_PAGES - 1)
                d_acc = [bank(t, "acc_d_%d" % t) for t in range(PACK)]
                for t in range(PACK):
                    d_pass(t, 0)

        w4_q = [tile("w4_q%d" % a, [P, N], U32) for a in range(2)]
        w4_s = [tile("w4_s%d" % a, [P, N], U8) for a in range(2)]

        def weave(dst, src):
            nc.scalar.copy(dst.rearrange("p (c n) i -> p c i n", n=4), src.rearrange("p i (c n) -> p c i n", n=4))

        def quantise(codes, scales, woven):
            nc.vector.quantize_mx(out=codes.bitcast(FP8X4), scales=scales, in_=woven.rearrange("p c i -> p (c i)"))

        def quantise_w4(a):
            w4_b = tile("w4_b%d" % a, [P, N, PACK], BF16)
            weave(w4_b[:], w4_raw[a])
            quantise(w4_q[a][:], w4_s[a][:], w4_b[:])

        z_rows = [tile("z_rows0", [P, PACK, T2], BF16, tag="w2_raw1")]
        l_b = [tile("l_b%d" % a, [P, PACK * T2], BF16, tag=("w2_b1", "l_b1")[a]) for a in range(2)]

        def z_slice(s):
            return z_rows[s // PACK][:, s % PACK, :]

        def z_flat(a):
            return z_rows[a][:].rearrange("p i c -> p (i c)")

        def place(tiles, s):
            return tiles[s // PACK][:, T2 * (s % PACK):T2 * (s % PACK + 1)]

        def round_a(s):
            nc.scalar.copy(z_slice(s), pageA[s % A_PAGES][:])

        def round_least(s):
            nc.scalar.copy(place(l_b, s), l_raw[:, s, :])

        for s in range(LAST - A_PAGES):
            round_a(s)
            scatter_a(s + A_PAGES)
        pageB = [tile("pageB%d" % i, [P, T2], F32, tag="h1_%d" % (A_PAGES + i)) for i in range(B_PAGES)]
        for page in pageB:
            nc.gpsimd.memset(page[:], 0.0)
        round_least(0)

        w3_p = tile("w3_p", [P, H], U32)
        nc.scalar.copy(w3_p[:].rearrange("p (h t u i) -> p h u t i", h=2, t=PACK, i=4),
                       w3_raw[:].bitcast(U32).rearrange("p (h u i t) -> p h u t i", h=2, t=PACK, i=4))

        d_rows = tile("d_rows", [P, PACK, S], BF16)
        d_b = tile("d_b", [P, S, PACK], BF16)
        d_q = tile("d_q", [P, S], U32)
        d_s = tile("d_s", [P, S], U8)
        for t in range(PACK):
            d_pass(t, 1)
            nc.scalar.activation(d_rows[:, t, :], d_acc[t][:], RELU, bias=bias[:, t:t + 1])
        round_least(1)
        weave(d_b[:], d_rows[:])
        quantise(d_q[:], d_s[:], d_b[:])

        round_a(LAST - A_PAGES)
        scatter_a(LAST)
        for s in range(2, PACK):
            round_least(s)

        for s in range(SLICES):
            h2_acc = bank((s + PACK) % LAST if s < LAST else LAST, "acc_h2_%d" % s)
            nc.tensor.matmul_mx(out=h2_acc[:], lhsT=w3_p[:, P * s:P * s + P].bitcast(FP8X4),
                                lhsT_scale=ws_p[0][4:P, P * s:P * s + P],
                                rhs=d_q[:].bitcast(FP8X4), rhs_scale=d_s[:], start=True, stop=True)
            if s < LAST:
                nc.scalar.copy(h2[s][:], h2_acc[:])
            else:
                nc.scalar.copy(h2_last[0][:], h2_acc[:, LAST_PARTS[0]])
        z_rows.append(tile("z_rows1", [P, PACK, T2], BF16, tag="w3_p"))
        for s in range(B_PAGES):
            scatter_b(s)

        z_b0 = [tile("z_b0_%d" % j, [P, HALF, PACK], BF16) for j in range(2)]
        z_b1 = [tile("z_b1_%d" % c, [P, width(cols), PACK], BF16) for c, cols in enumerate(CHUNKS)]
        z_q1 = tile("z_q1", [P, T2], U32)
        z_s1 = [tile("z_s1_%d" % c, [P, width(cols)], U8) for c, cols in enumerate(CHUNKS)]
        o_acc = [bank(b, "acc_o_%d" % b) for b in range(LAST)]
        o_sb = tile("o_sb", [P, N // P, T2], F32, tag="l_raw")
        out_v = out.rearrange("(n p) c -> p n c", p=P)
        b_b = [tile("b_b0", [P, PACK * T2], BF16, tag="w2_b0"), tile("b_b1", [P, 2 * T2], BF16, tag="w2_b1")]

        def banks(cols):
            per = BANK // width(cols)
            first = cols.start * (N // P) // BANK
            return [(first + k, range(per * k, per * k + per)) for k in range(N // P // per)]

        def maximum(dst, a, b):
            nc.vector.tensor_tensor(dst, a, b, MAX)

        def round_b(s):
            nc.scalar.copy(place(b_b, s), page_b(s)[:])
            if s == PACK - 1:
                maximum(z_flat(0), z_flat(0), b_b[0][:])
            if s + B_PAGES < LAST:
                scatter_b(s + B_PAGES)

        def multiply(a, cols, codes, scales):
            w = width(cols)
            for b, blocks in banks(cols):
                for k, n in enumerate(blocks):
                    nc.tensor.matmul_mx(out=o_acc[b][:, w * k:w * k + w],
                                        lhsT=w4_q[a][:, P * n:P * n + P].bitcast(FP8X4),
                                        lhsT_scale=w4_s[a][:, P * n:P * n + P],
                                        rhs=codes.bitcast(FP8X4), rhs_scale=scales,
                                        start=(a == 0 and k == 0), stop=(a == 1 and k == len(blocks) - 1))

        def weave_pass0(j, u):
            at = WEAVE * u
            weave(z_b0[j][:, at:at + WEAVE, :], z_rows[0][:, :, HALF * j + at:HALF * j + at + WEAVE])

        def quantise_pass0(j, tag):
            z_q0 = tile("z_q0_%d" % j, [P, HALF], U32, tag=tag)
            z_s0 = tile("z_s0_%d" % j, [P, HALF], U8)
            quantise(z_q0[:], z_s0[:], z_b0[j][:])
            return z_q0, z_s0

        def multiply_pass0(j, z_q0, z_s0):
            for cols in CHUNKS:
                if cols.start // HALF == j:
                    own = slice(cols.start - HALF * j, cols.stop - HALF * j)
                    multiply(0, cols, z_q0[:, own], z_s0[:, own])

        def scatter_last(j):
            nc.vector.tensor_tensor(page_b(LAST)[:].indirect(entries(idx3, LAST_PARTS[j])), h2_last[j][:],
                                    wgB[:, PACK - 1, LAST_PARTS[j]], MULT)

        maximum(z_flat(0), z_flat(0), l_b[0][:])
        quantise_w4(0)
        round_a(PACK)
        for s in range(PACK):
            round_b(s)
            if s + 1 < PACK:
                round_a(PACK + s + 1)
            round_least(PACK + s)
        maximum(z_flat(1), z_flat(1), l_b[1][:])
        quantise_w4(1)
        round_b(LAST - 3)
        for j, u in ((1, 0), (1, 1), (0, 0)):
            weave_pass0(j, u)
        round_b(LAST - 2)
        maximum(z_flat(1)[:, 0:2 * T2], z_flat(1)[:, 0:2 * T2], b_b[1][:])
        weave_pass0(0, 1)
        multiply_pass0(0, *quantise_pass0(0, "z_q0_0"))
        for j in range(2):
            cols = slice(HALF * j, HALF * j + HALF)
            b_half = tile("b_half%d" % j, [P, HALF], BF16)
            nc.scalar.copy(b_half[:], page_b(LAST - 1)[:, cols])
            maximum(z_slice(LAST - 1)[:, cols], z_slice(LAST - 1)[:, cols], b_half[:])

        def weave_pair(copy, c, pair):
            copy(z_b1[c][:, :, pair], z_rows[1][:, pair, CHUNKS[c]].rearrange("p i c -> p c i"))

        scatter_last(0)
        second_half = quantise_pass0(1, "b_half1")
        weave(z_b1[0][:], z_rows[1][:, :, CHUNKS[0]])
        for c in range(1, WOVEN_AHEAD):
            weave_pair(nc.scalar.copy, c, EARLY)
        h2_last.append(tile("h2_last1", [P, width(LAST_PARTS[1])], F32, tag="b_half0"))
        nc.scalar.copy(h2_last[1][:], h2_acc[:, LAST_PARTS[1]])
        o_acc.append(bank(LAST, "acc_o_last"))
        for c in range(WOVEN_AHEAD, len(CHUNKS)):
            weave_pair(nc.scalar.copy, c, EARLY)
        multiply_pass0(1, *second_half)
        scatter_last(1)

        def max_in_row(cols, page_part):
            maximum(z_slice(LAST)[:, cols], page_part, z_slice(LAST)[:, cols])

        def finish(c):
            cols = CHUNKS[c]
            quantise(z_q1[:, cols], z_s1[c][:], z_b1[c][:])
            multiply(1, cols, z_q1[:, cols], z_s1[c][:])
            for k, (b, blocks) in enumerate(banks(cols)):
                dst = o_sb[:, blocks.start:blocks.stop, cols]
                src = o_acc[b][:].rearrange("p (n c) -> p n c", c=width(cols))
                if c >= SHARED_FROM and k == 1:
                    nc.vector.tensor_copy(dst, src)
                else:
                    nc.scalar.copy(dst, src)
                nc.sync.dma_start(out_v[:, blocks.start:blocks.stop, cols], dst)

        b_late = tile("b_late", [P, HALF], BF16)
        nc.scalar.copy(b_late[:], page_b(LAST)[:, HALF:T2])
        woven = z_b1[0][:, :, PACK - 1]
        maximum(woven, page_b(LAST)[:, CHUNKS[0]], woven)
        for c in (1, 2):
            max_in_row(CHUNKS[c], page_b(LAST)[:, CHUNKS[c]])
            finish(c - 1)
            weave_pair(nc.vector.tensor_copy, c, LATE)
        max_in_row(slice(HALF, T2), b_late[:])
        finish(2)
        for c in (3, 4):
            weave_pair(nc.vector.tensor_copy, c, LATE)
        for c in (3, 4):
            finish(c)
